import numpy as np, ml_dtypes
CORES = [1,5,17,21,33,37,49,53]
N = 8
BF = ml_dtypes.bfloat16
S, L, CAP, RO, KM = 4096, 512, 96, 3, 3967
W = S + RO * CAP
def joined(c, T):
    e = np.add.accumulate(4 + (c & 3), axis=1)
    j = np.minimum(np.sum(e[:, :, None] <= (5 * np.arange(L) + 2)[None, None, :], axis=1), L - 2)
    p = np.take_along_axis(c, j, 1); q = np.take_along_axis(c, j + 1, 1)
    left = np.take_along_axis(T, p[:, None, :], 2)[:, 8:]; right = np.take_along_axis(T, q[:, None, :], 2)[:, :8]
    return p, np.concatenate([left, right], axis=1).astype(np.int64)
def places(z, w, k):
    u = np.sum(z * w[:, :, 0:1], axis=1) & (S - 1); v = np.sum(z * w[:, :, 1:2], axis=1) & (S - 1)
    return (((u * v) >> 5)[:, None, :] + k[:, :, None] * u[:, None, :]) & (S - 1)
def probe(z, w, k, b, U):
    h = places(z, w, k)
    d = np.stack([np.sum(np.abs(np.take_along_axis(U, h[:, m:m + 1], 2) - z), axis=1) for m in range(16)], axis=1)
    m = np.argmin(d, axis=1)[:, None, :]
    return np.take_along_axis(h, m, 1)[:, 0], np.take_along_axis(d, m, 1)[:, 0] < b[:, None]
def lowest(h, fit):
    win = np.zeros(fit.shape, bool)
    for g in range(8):
        i = np.flatnonzero(fit[g]); win[g, i[np.unique(h[g, i], return_index=True)[1]]] = True
    return win
def parts(rng):
    return (rng.integers(0, 256, (N, 8, 16, S), dtype=np.int16), rng.integers(0, 256, (N, 8, 16, S), dtype=np.int16), rng.integers(0, S, (N, 8, L)),
            rng.integers(0, 4096, (N, 8, 16, 2)), rng.integers(0, KM + 1, (N, 8, 16)), rng.integers(840, 1040, (N, 8)))
def pack(us, tp, c, w, k, th):
    return {"us": us.reshape(N, 128, S).astype(np.float32).astype(BF), "tp": tp.reshape(N, 128, S).astype(np.float32).astype(BF), "c0": np.ascontiguousarray(c).astype(np.int32),
            "hw": np.ascontiguousarray(w.reshape(N, 128, 2)).astype(np.int32), "km": np.ascontiguousarray(k.reshape(N, 128, 1)).astype(np.int32), "th": np.ascontiguousarray(th.reshape(N, 8, 1)).astype(np.int32)}
def setup_inputs(rng):
    return pack(*parts(rng))
def near(z, d):
    a = d[None, :] // 16 + (np.arange(16)[:, None] < d[None, :] % 16)
    return np.where(z < 128, z + a, z - a)
def setup_inputs_corners(rng):
    us, tp, c, w, k, th = parts(rng); w[:, :, 0, 0] |= 1; cnt = (0, 1, CAP - 1, CAP, CAP + 1, L); used = {}; sent = {}; zs = []
    def plant(q, g, h, z, todo):
        st, sl, ds = [], [], []
        for i, d in todo:
            r = int(rng.integers(0, 16)); cand = h[:, i].tolist()
            for m in range(16):
                s = cand[(m + r) % 16]
                if s not in used[q, g]:
                    used[q, g].add(s); st.append(s); sl.append(i); ds.append(d); break
        if st: us[q, g][:, np.array(st)] = near(z[:, np.array(sl)], np.array(ds))
    for q in range(N):
        for g in range(8):
            v = (g + q) % 8; used[q, g] = set()
            if v == 6: c[q, g] = 4 * rng.integers(0, S // 4, L) + 3; c[q, g, :3] = S - 1
            elif v == 7: c[q, g] = 4 * rng.integers(0, S // 4, L); c[q, g, L - 3:] = 0
            else: c[q, g] = 4 * rng.permutation(S // 4)[:L] + 1; k[q, g] = rng.permutation(min(S, KM + 1))[:16]; th[q, g] = rng.choice(np.array([1, 2, 64, 100]))
            if v in (1, 2, 3): us[q, g, :, 0] = 0; used[q, g].add(0)
        p, z = joined(c[q], tp[q]); even = (np.sum(z * w[q, :, :, 0:1], axis=1) & 1) == 0
        for g in range(8):
            if (g + q) % 8 < 6: tp[q, g, 8, np.unique(p[g, even[g]])] ^= 1
        p, z = joined(c[q], tp[q]); zs.append(z); h = places(z, w[q], k[q])
        for g in range(8):
            v = (g + q) % 8
            if v > 5: continue
            n = cnt[v]; pair = 2 if n >= 2 else 0; front = rng.permutation(L - 2).tolist(); t = int(th[q, g])
            poor = front[:n - pair] + ([L - 2, L - 1] if pair else []); fits = front[n - pair:] + ([] if pair else [L - 2])
            plant(q, g, h[g], z[g], [(i, (t - 1) * int(rng.integers(0, 2))) for i in fits] + [(i, t) for i in poor if i < L - 1 and rng.random() < 0.5])
            sent[q, g] = sorted(poor)[:CAP]
    for q in range(N):
        a = (q + 1) % N; h = places(zs[q], w[a], k[a])
        for g in range(8):
            if (q, g) in sent:
                t = int(th[a, g]); full = (g + q) % 8 == 4
                plant(a, g, h[g], zs[q][g], [(i, (0, t - 1, t)[int(rng.integers(0, 2 if full else 3))]) for i in sent[q, g] if i < L - 1 and (full or rng.random() < 0.6)])
    return pack(us, tp, c, w, k, th)
def setup_inputs_ends(rng):
    us = 255 * rng.integers(0, 2, (N, 8, 16, S), dtype=np.int16); tp = 255 * rng.integers(0, 2, (N, 8, 16, S), dtype=np.int16)
    inner = np.argsort(rng.random((N, 8, L)), axis=-1) < 5 * L // 16; anyc = rng.integers(0, S, (N, 8, L)); roll = rng.random((N, 8, L))
    w = 4095 * rng.integers(0, 2, (N, 8, 16, 2)); w[:, :, 0, 0] = 0; w[:, :, 1, 0] = 4095
    k = np.where(np.argsort(rng.random((N, 8, 16)), axis=-1) < 4, rng.integers(0, KM + 1, (N, 8, 16)), KM * rng.integers(0, 2, (N, 8, 16)))
    th = np.stack([4080 * (rng.permutation(8) % 2) for q in range(N)]); big = np.stack([rng.permutation(8) < 4 for q in range(N)]); big[:, 7] = True; big[0, 0] = True
    if th[N - 1, 7] == 0: th[N - 1, int(np.argmax(th[N - 1]))] = 0; th[N - 1, 7] = 4080
    c = np.where(inner, anyc, (S - 1) * (roll < 0.5)); base = ((S - 1) ** 2 >> 5) & (S - 1); one = np.zeros(16, np.int16); one[0] = 1
    for q in range(N):
        for g in range(8):
            if not big[q, g]: continue
            w[q, g] = 4095; us[q, g, :, 0] = 255; tp[q, g, :, 0] = 255; tp[q, g, :, S - 1] = 0; tp[q, g, :, S - 2] = 0; tp[q, g, 8, S - 2] = 1
            far = (S - 1, 1, 2) if g == 7 or rng.random() < 0.5 else (2, S - 1, 1)
            for lane, s in zip((1, 14, 15), far): k[q, g, lane] = (base - s) & (S - 1); us[q, g, :, s] = one
            k[q, g, 0] = 0; k[q, g, 2] = KM
            c[q, g] = np.where(inner[q, g], anyc[q, g] // 4 * 4, (S - 1) * (roll[q, g] < 0.2))
            if rng.random() < 0.5: c[q, g, 0] = S - 2; c[q, g, 1] = S - 1
            c[q, g, 4:6] = S - 1; c[q, g, 6:9] = 0; c[q, g, L - 2] = S - 2; c[q, g, L - 1] = S - 1
    return pack(us, tp, c, w, k, th)
def setup_inputs_refuse(rng):
    d = setup_inputs_ends(rng); d["th"][1] = 0
    return d
def setup_inputs_spread(rng):
    us, tp, c, w, k, th = parts(rng)
    def stones():
        v = np.floor(np.exp2(8 * rng.random((N, 8, 1, S), dtype=np.float32)) * rng.random((N, 8, 16, S), dtype=np.float32)).astype(np.int16)
        v = np.minimum(v, 255); return np.where(rng.random((N, 8, 1, S)) < 0.25, 255 - v, v)
    c = np.minimum((S * rng.random((N, 8, L)) ** 3).astype(np.int64), S - 1); c[:, ::2] = S - 1 - c[:, ::2]
    w = np.minimum(np.exp2(12.01 * rng.random((N, 8, 16, 2))).astype(np.int64) - (rng.random((N, 8, 16, 2)) < 0.05), 4095)
    k = np.maximum(np.minimum(np.exp2(12 * rng.random((N, 8, 16))).astype(np.int64) - 1, KM), 0)
    th = np.where(rng.random((N, 8)) < 0.25, rng.integers(0, 4081, (N, 8)), np.exp2(6 + 4 * rng.random((N, 8))).astype(np.int64))
    us = stones(); tp = stones()
    for q in range(N):
        g = int(rng.integers(0, 8))
        us[q, g] = rng.integers(0, 8, (16, S)); us[q, g, 0] += 248
        tp[q, g] = rng.integers(248, 256, (16, S)); tp[q, g, 8] = rng.integers(0, 2, S)
        w[q, g, :, 0] = 3072; w[q, g, 0, 0] = 4095; w[q, g, :, 1] = rng.integers(0, 4096, 16)
        k[q, g] = rng.permutation(KM + 1)[:16]; th[q, g] = 4080
    return pack(us, tp, c, w, k, th)
def setup_inputs_ties(rng):
    us, tp, c, w, k, th = parts(rng); flat = int(rng.integers(0, 8)); z = np.full((1, 16, 1), 255); z[0, 0] = 0
    for q in range(N):
        for g in range(8):
            pr = rng.integers(0, 256, (16, 12)); tp[q, g] = pr[:, rng.integers(0, 12, S)]
            us[q, g, :8] = pr[8:, rng.integers(0, 12, S)]; us[q, g, 8:] = pr[:8, rng.integers(0, 12, S)]
            th[q, g] = int(rng.choice(np.array([1, 400, 600, 700, 900])))
        us[q, flat] = 0; us[q, flat, 0] = 255; tp[q, flat] = 255; tp[q, flat, 8] = 0; th[q, flat] = 4080
        w[q, flat, 1, 0] ^= 1 - int(np.sum(w[q, flat, 1:, 0])) % 2
        if places(z, w[q, flat][None], k[q, flat][None])[0, 0, 0] == 0: k[q, flat, 0] ^= 1
    return pack(us, tp, c, w, k, th)
def check_inputs(d):
    bad = []
    for a, lo, hi in (("us", 0, 255), ("tp", 0, 255), ("c0", 0, S - 1), ("hw", 0, 4095), ("km", 0, KM), ("th", 0, 4080)):
        v = np.asarray(d[a]).astype(np.float64)
        if not (np.min(v) >= lo and np.max(v) <= hi): bad.append("range of " + a)
        elif np.any(v != np.floor(v)): bad.append("whole numbers in " + a)
    return bad
def reference(us, tp, c0, hw, km, th):
    U = np.zeros((N, 8, 16, W), np.int64); U[..., :S] = us.astype(np.float32).astype(np.int64).reshape(N, 8, 16, S)
    T = np.zeros((N, 8, 16, W), np.int64); T[..., :S] = tp.astype(np.float32).astype(np.int64).reshape(N, 8, 16, S)
    C = c0.astype(np.int64); w = hw.astype(np.int64).reshape(N, 8, 16, 2); k = km.astype(np.int64).reshape(N, 8, 16); t0 = th.astype(np.int64).reshape(N, 8)
    P = np.zeros(N, np.int64); out = []
    for t in range(RO):
        b = t0 + (P & 63)[:, None]; new, poor, zs = [], [], []
        for a in range(N):
            p, z = joined(C[a], T[a]); h, fit = probe(z, w[a], k[a], b[a], U[a]); win = lowest(h, fit)
            for g in range(8): U[a, g][:, h[g, win[g]]] = 255
            new.append(np.where(win, h, p)); poor.append(~fit); zs.append(z)
        for q in range(N):
            a = (q + 1 + t % (N - 1)) % N; sl = [np.flatnonzero(poor[q][g])[:CAP] for g in range(8)]
            z = np.zeros((8, 16, CAP), np.int64); use = np.zeros((8, CAP), bool)
            for g in range(8): z[g][:, :len(sl[g])] = zs[q][g][:, sl[g]]; use[g, :len(sl[g])] = True
            h, fit = probe(z, w[a], k[a], b[a], U[a]); win = lowest(h, fit & use)
            for g in range(8):
                s = np.flatnonzero(win[g]); n = h[g, s]; own = S + CAP * t + s
                U[q, g][:, own] = U[a, g][:, n]; T[q, g][:, own] = T[a, g][:, n]; U[a, g][:, n] = 255; new[q][g, sl[g][s]] = own
        P = np.array([int(np.sum(m)) for m in poor]); C = np.stack(new); out.append(C)
    return {"yc": np.concatenate(out, axis=2).astype(np.float32), "yu": U.reshape(N, 128, W).astype(np.float32).astype(BF)}

@@ -1,0 +1,736 @@
+from concourse.mybir import AluOpType, ActivationFunctionType
+
+NB, NA, S, W, R, NS = 32, 6, 4096, 4384, 3, 22
+ZC, UW = 4608, 4624
+SG = (1, 9)
+F, B, I, H, U16 = "float32", "bfloat16", "int32", "float16", "uint16"
+SCRATCH, PACK, PACKED = {}, {}, {}
+SEMAPHORES = ["sv", "ss", "sp", "sg", "d0", "d1", "d2", "d3", "d4", "d5", "dt", "lz", "ly", "lx"] + ["du%d" % t for t in range(4)]
+for _t in range(R):
+    SEMAPHORES += ["az%d" % _t, "ar%d" % _t, "au%d" % _t]
+    SCRATCH["ZR%d" % _t] = ("sbuf", [128, 96], B)
+    SCRATCH["RB%d" % _t] = ("sbuf", [128, 192], B)
+for _n in range(8):
+    SCRATCH["p%d" % _n] = ("psum", [128, 512], F)
+for _w, _d, _s in (
+        (UW, B, "U Tw FL"), (288, B, "UP"), (32, I, "CR"), (2048, B, "E2 E3 FX FD EH EL E1 LQ"), (2048, H, "WU WV KD"), (16384, B, "EQ"),
+        (512, F, "ior YC"), (544, F, "KD2 DA DB"), (1088, F, "KAB"), (102, F, "KE"), (512, B, "LJ"), (48, F, "la"), (2, I, "pi pq hwi"), (1, I, "kmi thi Pi Pj"), (1, F, "pf qf gf kmf thf"), (2, F, "hwf hwg hws hwm"),
+        (16, F, "io16 qm ql kq KM KS0 KS dA dB dC"), (16, I, "ki ka kb"), (128, F, "io8 io128 iox BF x1 x2 x3 x4 x5 x6 rep"), (128, B, "BD ID NI GE BH BL ZM"), (128, F, "O16"),
+        (96, F, "msk Hd Hj"), (32, F, "col tc tcq tc512 tc1024 tc4096 W40 W4 on idx T1 nf pen0 pen cum s1 OF lf hx hx0 hc wn wm wl ld hm lo l2 Cf cw ee ec mu rc pj pj2 fo jt jj a1 a2 a3 a4 a5 a6 a7 n1 n2 n3 n4 n5"),
+        (32, I, "PR qi k3 k4 Hh Ci f3 fi nx Ai"), (64, I, "uva kI kJ k2 dg"), (96, I, "uv"), (32, H, "uh qh hh"), (6, H, "ha"), (64, B, "dh dn"), (32, B, "pw wv"),
+        (32, U16, "OFu lou fou JJ JB ngu"), (8, U16, "glu sou"), (64, U16, "CL"), (512, U16, "HL HR"), (512, I, "X X2"),
+        (512, B, "JV L255 NB2 NG ZA Z TC GS LS JS DF0 DF1 DF2"), (1024, B, "JP NW JW AB0 AB1 AB2"), (528, B, "NR"), (1536, B, "ZS TS"), (384, B, "z4"), (576, F, "EA"),
+        (8, F, "k6 k7 gt gl gm gm0 gn go gp gh"), (192, B, "SB"), (96, B, "SU xt")):
+    for _n in _s.split():
+        if _w <= 64 and _n not in ("CR", "hwi", "kmi", "thi"):
+            _k = "pk" + _d
+            PACK[_n] = (_k, PACKED.get(_k, 0), _w)
+            PACKED[_k] = PACKED.get(_k, 0) + (_w + 7) // 8 * 8
+        else:
+            SCRATCH[_n] = ("sbuf", [128, _w], _d)
+for _k, _w in PACKED.items():
+    SCRATCH[_k] = ("sbuf", [128, _w], _k[2:])
+
+
+def rank_program(g, core, T, topo):
+    rank = T.rank_of(core)
+    if rank is None:
+        return
+    A, AF = AluOpType, ActivationFunctionType
+    Q = {"V": g.vector, "S": g.scalar, "P": g.tensor, "G": g, "Y": g.sync}
+    SEM = {"V": "sv", "S": "ss", "P": "sp", "G": "sg"}
+    count, known, snaps, rec = {}, {q: {} for q in Q}, {}, {}
+
+    def v(name, lo=None, hi=None, step=1, p=None):
+        buf, at, w = PACK[name] if name in PACK else (name, 0, SCRATCH[name][1][1])
+        lo = 0 if lo is None else lo
+        hi = w if hi is None else hi
+        rows = slice(None) if p is None else p
+        ap = T[buf][rows, at + lo:at + hi] if step == 1 else T[buf][rows, at + lo:at + hi:step]
+        return (ap, name, lo, hi, step)
+
+    def ind(win, off):
+        return (win[0].indirect(off[0]), (win, off))
+
+    def parts(x):
+        return list(x[1]) if len(x) == 2 else [x]
+
+    def hit(a, b):
+        if a[1] >= b[2] or b[1] >= a[2]:
+            return False
+        return not (a[3] == b[3] and a[3] > 1 and (a[1] - b[1]) % a[3])
+
+    def is_bank(n):
+        return n[0] == "p" and n[1:].isdigit()
+
+    def reg(x):
+        return (x[1], 0, 512, 1) if is_bank(x[1]) else (x[1], x[2], x[3], x[4])
+
+    def learn(q, e, n):
+        known[q][e] = max(known[q].get(e, 0), n)
+        for e2, n2 in snaps.get((e, n), {}).items():
+            known[q][e2] = max(known[q].get(e2, 0), n2)
+
+    def settle(q, reads, writes):
+        need = {}
+        for xs, isw in ((reads, False), (writes, True)):
+            for x in xs:
+                r = reg(x)
+                ps = is_bank(r[0])
+                for (o, e, n, w) in rec.get(r[0], []):
+                    if not hit(r, o):
+                        continue
+                    if e == q:
+                        if q == "P" or not (w or isw):
+                            continue
+                    elif not (w or isw or ps):
+                        continue
+                    need[e] = max(need.get(e, 0), count[e] if e[0] in "DL" else n)
+        for e, n in sorted(need.items(), key=lambda kv: -kv[1]):
+            if known[q].get(e, 0) < n:
+                Q[q].wait_ge(T.sem[SEM.get(e, e[1:])], n)
+                learn(q, e, n)
+
+    def note(e, n, reads, writes, snap):
+        snaps[(e, n)] = dict(snap)
+        for xs, isw in ((reads, False), (writes, True)):
+            for x in xs:
+                r = reg(x)
+                old = rec.setdefault(r[0], [])
+                if isw:
+                    old[:] = [o for o in old if not (o[0][1] >= r[1] and o[0][2] <= r[2] and r[3] == 1)]
+                old[:] = [o for o in old if not (o[0] == r and o[1] == e and o[3] == isw)]
+                old.append((r, e, n, isw))
+
+    def op(q, f, reads, writes):
+        rs = [p for x in reads if isinstance(x, tuple) for p in parts(x)]
+        ws = []
+        for x in writes:
+            ps = parts(x)
+            ws.append(ps[0])
+            rs += ps[1:]
+        settle(q, rs, ws)
+        count[q] = count.get(q, 0) + 1
+        f().then_inc(T.sem[SEM[q]], 1)
+        note(q, count[q], rs, ws, known[q])
+
+    def dma(q, sem, out, in_, reads, writes):
+        settle(q, reads, writes)
+        e = "D" + sem
+        count[e] = count.get(e, 0) + 16
+        Q[q].dma_start(out, in_).then_inc(T.sem[sem], 16)
+        note(e, count[e], reads, writes, known[q])
+
+    def _(x):
+        return x[0] if isinstance(x, tuple) else x
+
+    def ts(o, i, s1, op0, s2=None, op1=None):
+        rd = [i, s1, s2]
+        if op1 is None:
+            op("V", lambda: g.vector.tensor_scalar(out=_(o), in0=_(i), scalar1=_(s1), scalar2=None, op0=op0), rd, [o])
+        else:
+            op("V", lambda: g.vector.tensor_scalar(out=_(o), in0=_(i), scalar1=_(s1), scalar2=_(s2), op0=op0, op1=op1), rd, [o])
+
+    def tt(o, a, b, op0):
+        op("V", lambda: g.vector.tensor_tensor(out=_(o), in0=_(a), in1=_(b), op=op0), [a, b], [o])
+
+    def cp(o, i):
+        op("V", lambda: g.vector.tensor_copy(out=_(o), in_=_(i)), [i], [o])
+
+    def ms(o, c):
+        op("V", lambda: g.vector.memset(_(o), c), [], [o])
+
+    def scan(o, a, b, init, op0, op1):
+        op("V", lambda: g.vector.tensor_tensor_scan(_(o), _(a), _(b), init, op0, op1), [a, b], [o])
+
+    def act(o, i, func=AF.Copy, scale=None, bias=None):
+        kw = {}
+        if scale is not None:
+            kw["scale"] = _(scale)
+        if bias is not None:
+            kw["bias"] = _(bias)
+        op("S", lambda: g.scalar.activation(_(o), _(i), func, **kw), [i, scale, bias], [o])
+
+    def add_up(o, i, total):
+        op("S", lambda: g.scalar.activation(_(o), _(i), AF.Copy, accum_out=_(total)), [i], [o, total])
+
+    def weave(a, b, lead=0):
+        for k in range(lead):
+            next(a, None)
+        more = [a, b]
+        while more:
+            more = [x for x in more if next(x, more) is not more]
+
+    def mm(o, l, r, start=True, stop=True):
+        op("P", lambda: g.tensor.matmul(_(o), _(l), _(r), start, stop), [l, r], [o])
+
+    def iota(o, pattern, base, cm, flag=True):
+        op("G", lambda: g.iota(_(o), pattern, base, cm, allow_small_or_imprecise_dtypes=True) if flag else g.iota(_(o), pattern, base, cm), [], [o])
+
+    def col(j):
+        return v("col", j, j + 1)
+
+    def mat(name, q):
+        return v(name, 128 * q, 128 * q + 128)
+
+    def send(sem, lsem, dst, out, in_, reads):
+        settle("G", reads, [])
+        es = topo.engines(core, dst)[:8]
+        rid, pid, se = topo.addr(dst)
+        e = "L" + lsem
+        count[e] = count.get(e, 0) + len(es)
+        g.remote_dma(out, in_, T.sem[sem], T.sem[lsem], pid, rid, sum(1 << k for k in es))
+        note(e, count[e], reads, [], known["G"])
+
+    for t in range(R):
+        asker, lender = T.cores[(rank - 1 - t) % 8], T.cores[(rank + 1 + t) % 8]
+        for sem, src, ws in (("az%d" % t, asker, [v("ZR%d" % t)]), ("ar%d" % t, lender, [v("RB%d" % t)]), ("au%d" % t, lender, [v("UP", 96 * t, 96 * t + 96)])):
+            n = len(topo.engines(src, core)[:8])
+            count["A" + sem] = n
+            note("A" + sem, n, [], ws, {})
+
+    dma("Y", "d0", T.CR[:, :], T.c0[:, :], [], [v("CR")])
+    dma("S", "d1", T.hwi[:, :], T.hw[:, :], [], [v("hwi")])
+    dma("S", "d1", T.kmi[:, :], T.km[:, :], [], [v("kmi")])
+    for k in range(16):
+        lo = 8 * k
+        dma("S" if k % 2 else "Y", "d2", T.Tw[lo:lo + 8, 0:S], T.tp[(lo ^ 8):(lo ^ 8) + 8, :], [], [v("Tw", 0, S)] if k == 15 else [])
+    dma("Y", "dt", T.thi[0:8, :], T.th[:, :], [], [v("thi")])
+    for k in range(4):
+        dma("Y", "du%d" % k, T.U[:, 1024 * k:1024 * k + 1024], T.us[:, 1024 * k:1024 * k + 1024], [], [v("U", 1024 * k, 1024 * k + 1024)])
+
+    iota(v("pi"), [[0, 2]], 0, 1, False)
+    iota(v("io16"), [[1, 16]], 0, 0)
+    iota(v("io8"), [[1, 8], [0, 16]], 0, 0)
+    iota(v("iox"), [[0, 8], [1, 16]], 0, 0)
+    iota(v("E2"), [[-1, 16], [32, 8], [1, 16]], 0, 0)
+    iota(v("io128"), [[1, 128]], 0, 0)
+    iota(v("E3"), [[1, 16], [32, 8], [0, 16]], 0, 0)
+    iota(v("tc"), [[16, 32]], 0, 0)
+    iota(v("ior"), [[1, 512]], -256, 0)
+    iota(v("FL", 0, ZC), [[0, ZC]], 0, 0)
+    iota(v("FL", ZC, UW), [[0, UW - ZC]], 1, 0)
+    cp(v("pf"), v("pi", 0, 1))
+    ts(v("pq", 0, 1), v("pi", 0, 1), 4, A.arith_shift_right)
+    ts(v("pq", 1, 2), v("pi", 0, 1), 15, A.bitwise_and)
+    cp(v("gf"), v("pq", 0, 1))
+    cp(v("qf"), v("pq", 1, 2))
+    ts(v("qm"), v("io16"), v("qf"), A.is_equal)
+    ts(v("BD"), v("io8"), v("gf"), A.is_equal)
+    ts(v("x1"), v("iox"), 2.0, A.is_equal, 128.0, A.mult)
+    ts(v("x2"), v("iox"), 0.0, A.is_equal)
+    tt(v("x3"), v("x1"), v("x2"), A.add)
+    tt(v("BH"), v("x3"), v("BD"), A.mult)
+    for q in range(16):
+        act(mat("EH", q), v("BH"), scale=v("qm", q, q + 1))
+    ts(v("x4"), v("iox"), 2.0, A.is_equal)
+    ts(v("x5"), v("iox"), 1.0, A.is_equal)
+    tt(v("x6"), v("x4"), v("x5"), A.add)
+    tt(v("BL"), v("x6"), v("BD"), A.mult)
+    for q in range(16):
+        ts(mat("EL", q), v("BL"), v("qm", q, q + 1), A.mult)
+    ts(v("dg", 0, 32), v("CR"), 7, A.arith_shift_right)
+    ts(v("dg", 32, 64), v("CR"), 127, A.bitwise_and)
+    cp(v("dh"), v("dg"))
+    for q in range(16):
+        mm(v("p6", 32 * q, 32 * q + 32), mat("EH", q), v("dh", 0, 32), True, False)
+        mm(v("p6", 32 * q, 32 * q + 32), mat("EL", q), v("dh", 32, 64), False, True)
+    ms(v("NR", 512, 528), 0.0)
+    act(v("NR", 0, 512), v("p6"))
+    ts(col(0), v("qf"), 7.5, A.is_lt)
+    ts(col(4), v("qm", 0, 1), 128.0, A.mult)
+    tt(col(15), col(4), v("qm", 1, 2), A.add)
+    ts(col(13), v("gf"), 32.0, A.mult)
+    tt(col(14), col(13), v("qf"), A.add)
+    ts(v("FX"), v("E2"), col(13), A.is_equal, col(15), A.mult)
+    for j in (0, 1):
+        for q in range(16):
+            mm(v("p0", 32 * j, 32 * j + 32), mat("FX", q), v("NR", j + q, j + 512, 16), q == 0, q == 15)
+    ts(v("BF"), v("io8"), v("gf"), A.is_equal)
+    ts(col(1), col(0), -512.0, A.mult, 256.0, A.add)
+    ts(col(2), col(0), -256.0, A.mult)
+    ts(col(3), col(0), 256.0, A.mult)
+    ts(col(5), col(0), -256.0, A.mult, 255.0, A.add)
+    ts(col(6), v("qm", 1, 2), -512.0, A.mult)
+    ms(v("Tw", S, UW), 0.0)
+    cp(v("hwf"), v("hwi"))
+    ts(v("hwg"), v("hwf"), 2048.0, A.is_ge, -4096.0, A.mult)
+    tt(v("hws"), v("hwg"), v("hwf"), A.add)
+    ts(v("hwm"), v("hws"), col(3), A.mult)
+    cp(v("kmf"), v("kmi"))
+    ts(v("kq"), v("qm"), v("kmf"), A.mult)
+    mm(v("p5", 0, 2), v("BF"), v("hwm"))
+    mm(v("p5", 2, 18), v("BF"), v("kq"))
+    ts(v("WU"), v("E2"), col(13), A.is_equal, v("hws", 0, 1), A.mult)
+    cp(v("col", 7, 9), v("p5", 0, 2))
+    cp(v("KM"), v("p5", 2, 18))
+
+    def setup_hash():
+        ts(v("WV"), v("E2"), col(13), A.is_equal, v("hws", 1, 2), A.mult)
+        ts(v("KS0"), v("KM"), 2048.0, A.is_ge, -4096.0, A.mult)
+        ts(v("ID"), v("io128"), v("pf"), A.is_equal)
+        tt(v("KS"), v("KS0"), v("KM"), A.add)
+        for m in range(16):
+            ts(mat("KD", m), v("ID"), v("KS", m, m + 1), A.mult)
+        ts(v("NI"), v("ID"), -1.0, A.mult)
+
+    def setup_fill():
+        act(v("NW", 512, 1024), v("p6"))
+        act(v("JV"), v("ior"), scale=v("qm", 1, 2))
+        act(v("JP"), v("E2", 0, 1024), AF.Identity, scale=0.0, bias=col(6))
+        act(v("JW"), v("JP"))
+        act(v("L255"), v("E2", 0, 512), AF.Identity, scale=0.0, bias=col(5))
+
+    def setup_late():
+        ms(v("U", S, ZC), 0.0)
+        ts(v("U", ZC, UW), v("Tw", ZC, UW), col(2), A.add)
+        cp(v("Cf"), v("idx"))
+        cp(v("Ci"), v("idx"))
+        ts(v("FD"), v("E2"), col(13), A.is_equal, 4096.0, A.mult)
+        cp(v("ki"), v("KM"))
+        ts(v("ka"), v("ki"), 4, A.arith_shift_right)
+        ts(v("kb"), v("ki"), 15, A.bitwise_and)
+        ts(v("dC"), v("io16"), 256.0, A.mult)
+        tt(v("dB"), v("dC"), v("kb"), A.add)
+        tt(v("dA"), v("dC"), v("ka"), A.add)
+
+    def setup_last():
+        yield
+        for d, D in (("dA", "DA"), ("dB", "DB")):
+            tt(v(D, 1, 16), v(d, 0, 15), v(d, 1, 16), A.subtract)
+            ms(v(D, 0, 1), 33554432.0)
+            cp(v(D, 16, 17), v(d, 15, 16))
+            w = 17
+            while w < 544:
+                act(v(D, w, 2 * w), v(D, 0, w))
+                w *= 2
+        ms(v("KD2", 16, 544, 17), 67108864.0)
+        ms(v("KE", 16, 102, 17), 67108864.0)
+        yield
+        ts(v("rep", p=slice(0, 8)), v("io8", p=slice(0, 8)), v("pf", p=slice(0, 8)), A.is_equal)
+        cp(v("thf", p=slice(0, 8)), v("thi", p=slice(0, 8)))
+        mm(v("p5", 0, 1), v("rep", p=slice(0, 8)), v("thf", p=slice(0, 8)))
+        ts(v("x1"), v("io128"), v("pf"), A.is_le)
+        tt(v("GE"), v("x1"), v("BD"), A.mult)
+        ms(v("on"), 1.0)
+        ts(v("tcq"), v("tc"), v("qf"), A.add)
+        yield
+        for n in (512, 1024, 4096):
+            ts(v("tc%d" % n), v("tcq"), float(n), A.add)
+        ts(v("W40"), v("tcq"), 510.0, A.is_equal, 5112.0, A.mult)
+        ts(v("W4"), v("W40"), 4.0, A.add)
+        cp(col(9), v("p5", 0, 1))
+        ts(col(10), col(9), 4081.0, A.min, 4096.0, A.mult)
+        yield
+        ms(v("O16"), 0.0625)
+        ms(v("ZM"), 0.0)
+        ts(v("ql"), v("io16"), v("qf"), A.is_gt)
+        for q in range(1, 16):
+            act(mat("LQ", q), v("BD"), scale=v("ql", q, q + 1))
+        ms(v("ZS", 0, 96), 1024.0)
+        ms(v("TS", 0, 96), 0.0)
+        yield
+        ts(v("E1"), v("E3"), col(14), A.is_equal)
+        ts(v("msk"), v("iox", 0, 96), v("qf"), A.is_ge, 30000.0, A.mult)
+        yield
+
+    def to_list(ps, row, lo=0, n=512):
+        for q in range(16):
+            mm(ps, mat("FX", q), v(row, lo + q, lo + n, 16), q == 0, q == 15)
+
+    def digits(src, name="dh"):
+        ts(v("dg", 0, 32), src, 7, A.arith_shift_right)
+        ts(v("dg", 32, 64), src, 127, A.bitwise_and)
+        cp(v(name), v("dg"))
+
+    def rows(name):
+        for q in range(16):
+            mm(v("p6", q, 512, 16), mat("EH", q), v(name, 0, 32), True, False)
+            mm(v("p6", q, 512, 16), mat("EL", q), v(name, 32, 64), False, True)
+
+    def hash_sums(z, nb):
+        n = 16 * nb
+        for j, w in ((0, "WU"), (1, "WV")):
+            for q in range(16):
+                mm(v("p0", 32 * j, 32 * j + nb), mat(w, q), v(z, q, n, 16), q == 0, q == 15)
+
+    def hash_uv(nb):
+        ts(v("uva", 0, nb), v("p0", 0, nb), col(7), A.add)
+        yield
+        ts(v("uva", nb, 2 * nb), v("p0", 32, 32 + nb), col(8), A.add)
+        yield
+        ts(v("uv", nb, 3 * nb), v("uva", 0, 2 * nb), 4095, A.bitwise_and)
+        yield
+        tt(v("PR", 0, nb), v("uv", nb, 2 * nb), v("uv", 2 * nb, 3 * nb), A.mult)
+        yield
+        ts(v("T1", 0, nb), v("uv", nb, 2 * nb), 2048.0, A.is_ge, -4096.0, A.mult)
+        yield
+        ts(v("qi", 0, nb), v("PR", 0, nb), 5, A.arith_shift_right, 4095, A.bitwise_and)
+        yield
+        tt(v("uh", 0, nb), v("T1", 0, nb), v("uv", nb, 2 * nb), A.add)
+        yield
+        ts(v("qh", 0, nb), v("qi", 0, nb), -2048.0, A.add)
+        yield
+        ts(v("uv", 0, nb), v("uv", nb, 2 * nb), 16.0, A.mult)
+        yield
+
+    def hash_lists(nb, ps, lo, hi):
+        for m in range(lo, hi):
+            o = v(ps, (m - lo) * nb, (m - lo) * nb + nb)
+            mm(o, mat("KD", m), v("uh", 0, nb), True, False)
+            mm(o, v("ID"), v("qh", 0, nb), False, True)
+
+    def lists(ps, at, o, w):
+        ts(v("X", o, o + w), v(ps, at, at + w), 2048.0, A.add)
+        yield
+        ts(v("X2", o, o + w), v("X", o, o + w), 4095, A.bitwise_and)
+        yield
+        cp(v("HL", o, o + w), v("X2", o, o + w))
+        yield
+
+    def best(nb, keys):
+        cp(v("kI", 0, 2 * nb), keys)
+        yield
+        ts(v("kJ", 0, 2 * nb), v("kI", 0, 2 * nb), 255, A.bitwise_and)
+        yield
+        tt(v("k2", 0, 2 * nb), v("kJ", 0, 2 * nb), v("uv", 0, 2 * nb), A.mult)
+        yield
+        tt(v("k3", 0, nb), v("k2", 0, nb), v("k2", nb, 2 * nb), A.add)
+        yield
+        tt(v("k4", 0, nb), v("k3", 0, nb), v("qi", 0, nb), A.add)
+        yield
+        ts(v("Hh", 0, nb), v("k4", 0, nb), 4095, A.bitwise_and)
+        yield
+
+    def poor():
+        ts(v("nf"), v("KAB", 16, 544, 17), col(10), A.is_ge)
+        yield
+        tt(v("pw"), v("nf"), v("mu"), A.mult)
+        mm(v("p5", 0, 32), v("BD"), v("pw"))
+        mm(v("p5", 32, 64), v("GE"), v("pw"))
+        yield
+        ts(v("pen0"), v("pw"), 0.5, A.is_lt)
+        yield
+        tt(v("lf"), v("rc"), v("nf"), A.is_gt)
+        yield
+        tt(v("pen"), v("pen0"), v("tc1024"), A.mult)
+        yield
+        scan(v("cum"), v("on"), v("p5", 0, 32), 0.0, A.mult, A.add)
+        yield
+        ts(v("hx0"), v("lf"), -8192.0, A.mult, 8192.0 - 2048.0, A.add)
+        yield
+        tt(v("s1"), v("cum"), v("p5", 32, 64), A.subtract)
+        yield
+        tt(v("OF"), v("s1"), v("pen"), A.max)
+        yield
+        cp(v("OFu"), v("OF"))
+        yield
+
+    def laid():
+        ts(v("wl"), v("p5", 192, 224), 0.5, A.is_lt)
+        yield
+        tt(v("ld"), v("wl"), v("wm"), A.mult)
+        yield
+        tt(v("lo"), v("ld"), v("hm"), A.mult)
+        yield
+        tt(v("l2"), v("lo"), v("tc4096"), A.add)
+        yield
+        cp(v("lou"), v("l2"))
+        yield
+
+    def widths():
+        ts(v("f3"), v("Ci"), 3, A.bitwise_and)
+        tt(v("wv"), v("f3"), v("W4"), A.add)
+        mm(v("p5", 64, 96), v("BD"), v("wv"))
+        mm(v("p5", 96, 128), v("GE"), v("wv"))
+        yield
+        yield
+        scan(v("cw"), v("on"), v("p5", 64, 96), 0.0, A.mult, A.add)
+        tt(v("ee"), v("cw"), v("p5", 96, 128), A.subtract)
+        tt(v("ec"), v("ee"), v("wv"), A.add)
+        yield
+        ts(v("fi"), v("ee"), 0.2, A.mult, 512.0, A.min)
+        ts(v("nx"), v("ec"), 0.2, A.mult, 512.0, A.min)
+        tt(v("mu"), v("nx"), v("fi"), A.subtract)
+        yield
+        ts(v("rc"), v("mu"), 0.5, A.is_ge)
+        ts(v("pj"), v("mu"), 0.5, A.is_lt)
+        tt(v("pj2"), v("pj"), v("tc512"), A.mult)
+        tt(v("fo"), v("fi"), v("pj2"), A.max)
+        cp(v("fou"), v("fo"))
+        yield
+
+    def slots():
+        cp(ind(v("JW"), v("fou")), v("JV"))
+        scan(v("JS"), v("JW", 0, 512), v("JW", 0, 512), -512.0, A.max, A.max)
+
+    def slots_lists():
+        to_list(v("p4", 0, 32), "JS")
+        to_list(v("p4", 32, 64), "JW")
+
+    def slots2():
+        ts(v("jt"), v("p4", 32, 64), -256.5, A.is_lt, 512.0, A.mult)
+        ts(v("JB"), v("p4", 0, 32), 768.0, A.add)
+        tt(v("jj"), v("jt"), v("p4", 0, 32), A.add)
+        ts(v("JJ"), v("jj"), 256.0, A.add)
+
+    def numbers(t):
+        act(v("NG"), ind(v("RB%d" % t, 96, 192), v("ngu")))
+        yield
+        to_list(v("p4", 96, 128), "NG")
+        yield
+        ts(v("n1"), v("p4", 96, 128), 0.5, A.is_ge)
+        yield
+        tt(v("n3"), v("n1"), v("n2"), A.mult)
+        yield
+        tt(v("n5"), v("n3"), v("n4"), A.mult)
+        yield
+        tt(v("Ci"), v("n5"), v("idx"), A.add)
+        yield
+        tt(v("Cf"), v("n5"), v("idx"), A.add)
+        yield
+        digits(v("Ci"), "dn")
+        yield
+        rows("dn")
+        yield
+        if t < R - 1:
+            act(v("NW", 512, 1024), v("p6"))
+        yield
+
+    def put_numbers(t):
+        act(v("YC"), v("p6"))
+        dma("Y", "d3", T.yc[:, 512 * t:512 * t + 512], T.YC[2:128:16, :], [v("YC")], [])
+
+    def u_fix(k, c):
+        x = v("U", 1024 * k, 1024 * k + 1024)
+        if k % 2:
+            ts(x, x, col(c), A.add)
+        else:
+            act(x, x, AF.Identity, bias=col(c))
+        return x
+
+    def next_lists():
+        to_list(v("p0", 0, 32), "NR")
+        to_list(v("p0", 32, 64), "NR", 1)
+
+    def gather(m):
+        act(v("GS"), ind(v("U", 0, S), v("HL", 32 * m, 32 * m + 32)))
+
+    def diff_of(m):
+        o = 512 * (m % 2)
+        return v("AB%d" % (m // 2 % 3), o, o + 512)
+
+    def sum_up(k):
+        bank = "p7" if k % 2 else "p2"
+        for q in range(16):
+            mm(v(bank, 64 * (k // 2), 64 * (k // 2) + 64), mat("FD", q), v("AB%d" % (k % 3), q, 1024, 16), q == 0, q == 15)
+
+    def take(k):
+        bank, o = "p7" if k % 2 else "p2", 64 * (k // 2)
+        for j in (0, 1):
+            act(v("KD2", 2 * k + j, 544, 17), v(bank, o + 32 * j, o + 32 * j + 32))
+
+    def side(t):
+        for x in (numbers(t - 1) if t else setup_last()):
+            yield
+        for x in widths():
+            yield
+
+    for t in range(R):
+        last = t == R - 1
+        lender, asker = T.cores[(rank + 1 + t) % 8], T.cores[(rank - 1 - t) % 8]
+        cp(v("CL"), v("p0", 0, 64))
+        if t == 0:
+            cp(v("idx"), v("p0", 0, 32))
+        else:
+            tt(v("xt"), v("RB%d" % (t - 1), 96, 192), v("TS", 0, 96), A.mult)
+            tt(v("Tw", S + 96 * t - 96, S + 96 * t), v("xt"), v("RB%d" % (t - 1), 0, 96), A.add)
+        act(v("ZA"), ind(v("Tw", 0, W), v("CL", 0, 32)), AF.Identity, scale=col(0), bias=col(1))
+        todo = side(t)
+        if t:
+            next(todo, None)
+        tt(v("Z"), ind(v("Tw", 0, W), v("CL", 32, 64)), v("ZA"), A.min)
+        if t == 0:
+            setup_hash()
+            for k in range(4):
+                u_fix(k, 2)
+            setup_fill()
+        hash_sums("Z", NB)
+        if t:
+            next(todo, None)
+        if t:
+            weave(hash_uv(NB), (next(todo, None) for k in range(5)), 4)
+        else:
+            for x in hash_uv(NB):
+                pass
+        hash_lists(NB, "p1", 0, 8)
+        hash_lists(NB, "p3", 8, 16)
+        if t == 0:
+            setup_late()
+        else:
+            next(todo, None)
+        for x in lists("p1", 0, 0, 128):
+            pass
+        more = [lists("p3" if k > 1 else "p1", 128 * (k % 2), 128 * k, 128) for k in (1, 2, 3)]
+        gather(SG[0])
+        ready = []
+        for i, m in enumerate([m for m in range(16) if m not in SG]):
+            df = "DF%d" % (i % 3)
+            tt(v(df), ind(v("U", 0, S), v("HL", 32 * m, 32 * m + 32)), v("Z"), A.subtract)
+            act(diff_of(m), v(df), AF.Abs)
+            for k in ready:
+                take(k)
+            ready = []
+            done = [m // 2] if m % 2 else []
+            if m + 1 in SG:
+                mm(v("p4"), v("ID"), v("GS"), True, False)
+                mm(v("p4"), v("NI"), v("Z"), False, True)
+                act(diff_of(m + 1), v("p4"), AF.Abs)
+                done = [m // 2]
+            if i < 9:
+                next(more[i // 3])
+            if i == 6:
+                gather(SG[1])
+            if i >= 1:
+                next(todo, None)
+            for k in done:
+                sum_up(k)
+                ready.append(k)
+        for x in todo:
+            pass
+        for k in ready:
+            take(k)
+        slots()
+        scan(v("KAB", 0, 544), v("DA"), v("KD2"), 0.0, A.add, A.min)
+        scan(v("KAB", 544, 1088), v("DB"), v("KD2"), 0.0, A.add, A.min)
+        weave(best(NB, v("KAB", 16, 1088, 17)), poor())
+        tt(v("hh"), v("hx0"), v("Hh"), A.add)
+        tt(v("hx"), v("hx0"), v("Hh"), A.add)
+        for q in range(16):
+            mm(v("p1", q, 512, 16), mat("E1", q), v("hh"))
+        cp(ind(v("ZS"), v("OFu")), v("Z"))
+        send("az%d" % t, "lz", lender, T["ZR%d" % t][:, :], T.ZS[:, 0:96], [v("ZS", 0, 96)])
+        mm(v("p7"), v("ZM"), v("Z"), True, False)
+        ts(v("hc"), v("hx"), 2048.0, A.add)
+        cp(v("wm", 0, NS), v("lf", 0, NS))
+        tt(v("hm"), v("Hh"), v("tc4096"), A.subtract)
+        tt(v("a1"), v("Hh"), v("Cf"), A.subtract)
+        if not last:
+            act(v("TC"), ind(v("Tw", 0, W), v("CL", 0, 32)))
+        if t:
+            put_numbers(t - 1)
+        ts(v("HR"), v("p1"), 2048.0, A.add)
+        for b in range(NS, NB):
+            e = 512 * b
+            ts(v("EQ", e - 16 * b, e + 16), v("HR", 0, 16 * b + 16), v("hc", b, b + 1), A.is_equal)
+            add_up(v("LJ", 0, 16 * b), v("EQ", e - 16 * b, e), v("la", b, b + 1))
+        for b in range(NS):
+            e, w = 512 * b, 16 * NS - 16 * b
+            ts(v("EQ", e, e + w), v("HR", 16 * b, 16 * NS), v("hc", b, b + 1), A.is_equal)
+            if b < NS - 1:
+                mm(v("p7", 16 * b + 16, 16 * NS), v("BD"), v("EQ", e + 16, e + w), False, False)
+        for q in range(1, 16):
+            mm(v("p7", q, 512, 16), mat("LQ", q), v("EQ", q, 15872 + q + 1, 512), False, q == 15)
+        act(v("LS"), v("p7"))
+        zr = "ZR%d" % t
+        for k in range(4):
+            act(v("z4", 96 * k, 96 * k + 96), v(zr))
+        hash_sums(zr, NA)
+        to_list(v("p5", 192, 224), "LS")
+        if not last:
+            mm(v("p5", 224, 225), v("O16"), v("cum", 31, 32))
+        slots_lists()
+        if not last:
+            cp(ind(v("TS"), v("OFu")), v("TC"))
+        ts(v("wn", NS, NB), v("la", NS, NB), 0.5, A.is_lt)
+        tt(v("wm", NS, NB), v("wn", NS, NB), v("lf", NS, NB), A.mult)
+        weave(hash_uv(NA), laid(), 4)
+        hash_lists(NA, "p1", 0, 16)
+        cp(ind(v("U", 0, ZC), v("lou")), v("L255"))
+        if not last:
+            cp(v("Pi"), v("p5", 224, 225))
+        for x in lists("p1", 0, 0, 96):
+            pass
+        for k in range(4):
+            df, ab, o = "DF%d" % (k % 3), "AB%d" % (k // 2), 384 * (k % 2)
+            tt(v(df, 0, 384), ind(v("U", 0, S), v("HL", 24 * k, 24 * k + 24)), v("z4"), A.subtract)
+            act(v(ab, o, o + 384), v(df, 0, 384), AF.Abs)
+            if k % 2:
+                for q in range(16):
+                    mm(v("p2", 48 * (k // 2), 48 * (k // 2) + 48), mat("FD", q), v(ab, q, 768, 16), q == 0, q == 15)
+        for b in range(NA):
+            act(v("KE", 17 * b, 17 * b + 16), v("p2", b, 96, NA))
+        tt(v("a2"), v("a1"), v("ld"), A.mult)
+        ts(v("a3"), v("OF"), 95.5, A.is_lt)
+        ts(v("a4"), v("OF"), float(S + 96 * t), A.add)
+        tt(v("a5"), v("a4"), v("Cf"), A.subtract)
+        tt(v("a7"), v("a2"), v("Cf"), A.add)
+        tt(v("a6"), v("a5"), v("a3"), A.mult)
+        tt(v("Ai"), v("a7"), v("a6"), A.add)
+        digits(v("Ai"))
+        rows("dh")
+        slots2()
+        act(v("NW", 0, 512), v("p6"))
+        act(v("NR", 0, 512), ind(v("NW"), v("JJ")))
+        scan(v("KAB", 0, 102), v("DA", 0, 102), v("KE"), 0.0, A.add, A.min)
+        scan(v("KAB", 102, 204), v("DB", 0, 102), v("KE"), 0.0, A.add, A.min)
+        key = v("KAB", 16, 102, 17)
+
+        def fits():
+            ts(v("k6", 0, NA), key, col(10), A.is_ge, 8192.0, A.mult)
+            yield
+            ts(v("gt", 0, NA), key, col(10), A.is_lt)
+            yield
+        weave(best(NA, v("KAB", 16, 204, 17)), fits(), 1)
+        ts(v("k7", 0, NA), v("Hh", 0, NA), -2048.0, A.add)
+        tt(v("ha"), v("k6", 0, NA), v("k7", 0, NA), A.add)
+        for q in range(16):
+            mm(v("p1", q, 96, 16), mat("E1", q), v("ha"))
+        next_lists()
+        ts(v("gh", 0, NA), v("Hh", 0, NA), float(-ZC), A.add)
+        tt(v("gn", 0, NA), v("Hh", 0, NA), v("tc4096", 0, NA), A.subtract)
+        tt(v("Hd"), v("p1", 0, 96), v("msk"), A.add)
+        for b in range(NA):
+            if b:
+                ts(v("EA", 96 * b, 96 * b + 16 * b), v("p1", 0, 16 * b), v("k7", b, b + 1), A.is_equal)
+            ts(v("EA", 112 * b, 112 * b + 16), v("Hd", 16 * b, 16 * b + 16), v("k7", b, b + 1), A.is_equal)
+            add_up(v("Hj", 0, 16 * b + 16), v("EA", 96 * b, 112 * b + 16), v("la", 32 + b, 33 + b))
+        ts(v("gm0", 0, NA), v("la", 32, 32 + NA), 0.5, A.is_lt)
+        tt(v("gm", 0, NA), v("gm0", 0, NA), v("gt", 0, NA), A.mult)
+        tt(v("gl", 0, NA), v("gm", 0, NA), v("gh", 0, NA), A.mult)
+        ts(v("glu", 0, NA), v("gl", 0, NA), float(ZC), A.add)
+        act(v("SB", 96, 192), ind(v("FL"), v("glu", 0, NA)))
+        cp(v("SB", 0, 96), ind(v("Tw"), v("glu", 0, NA)))
+        send("ar%d" % t, "ly", asker, T["RB%d" % t][:, :], T.SB[:, :], [v("SB")])
+        act(v("SU"), ind(v("U"), v("glu", 0, NA)))
+        send("au%d" % t, "lx", asker, T.UP[:, 96 * t:96 * t + 96], T.SU[:, :], [v("SU")])
+        act(v("NB2"), ind(v("NW"), v("JB")))
+        if not last:
+            act(v("JW"), v("JP"))
+        to_list(v("p4", 64, 96), "NB2")
+        tt(v("go", 0, NA), v("gn", 0, NA), v("gm", 0, NA), A.mult)
+        tt(v("gp", 0, NA), v("go", 0, NA), v("tc4096", 0, NA), A.add)
+        cp(v("sou", 0, NA), v("gp", 0, NA))
+        cp(ind(v("U", 0, ZC), v("sou", 0, NA)), v("L255", 0, 96))
+        if not last:
+            ts(v("Pj"), v("Pi"), 63, A.bitwise_and)
+            tt(col(16), col(9), v("Pj"), A.add)
+            ts(col(10), col(16), 4081.0, A.min, 4096.0, A.mult)
+            ms(v("ZS", 0, 96), 1024.0)
+        base = float(S + 96 * t)
+        cp(v("idx"), v("p0", 0, 32))
+        ts(v("ngu"), v("idx"), -base, A.add, 0.0, A.max)
+        ts(v("n2"), v("idx"), base, A.is_ge)
+        if last:
+            for k in range(4):
+                x = u_fix(k, 3)
+                dma("Y", "d4", T.yu[:, 1024 * k:1024 * k + 1024], x[0], [x], [])
+        tt(v("n4"), v("p4", 64, 96), v("idx"), A.subtract)
+
+    for x in numbers(R - 1):
+        pass
+    put_numbers(R - 1)
+    ts(v("UP"), v("UP"), col(3), A.add)
+    dma("Y", "d5", T.yu[:, S:W], T.UP[:, :], [v("UP")], [])
+    for e, n in sorted(count.items()):
+        g.wait_ge(T.sem[SEM.get(e, e[1:])], n)

@@ -1,28 +1,33 @@
 from concourse.mybir import AluOpType, ActivationFunctionType
 
-NB, NA, S, W, R, NS = 32, 6, 4096, 4384, 3, 22
-ZC, UW = 4608, 4624
-SG = (1, 9)
+NB, NA, S, W, R, E = 32, 6, 4096, 4384, 3, 96
+SG = (1, 4, 6)
+NJ = 2
+OFS = 193.0
 F, B, I, H, U16 = "float32", "bfloat16", "int32", "float16", "uint16"
+M1, M128, M256, M4096 = 1.5 * 2 ** 23, 1.5 * 2 ** 30, 1.5 * 2 ** 31, 1.5 * 2 ** 35
 SCRATCH, PACK, PACKED = {}, {}, {}
-SEMAPHORES = ["sv", "ss", "sp", "sg", "d0", "d1", "d2", "d3", "d4", "d5", "dt", "lz", "ly", "lx"] + ["du%d" % t for t in range(4)]
+SEMAPHORES = ["sv", "ss", "sp", "sg", "d0", "d1", "d2", "d3", "d4", "d5", "d6", "dt", "lz", "ly", "lx"] + ["du%d" % t for t in range(4)]
 for _t in range(R):
-    SEMAPHORES += ["az%d" % _t, "ar%d" % _t, "au%d" % _t]
-    SCRATCH["ZR%d" % _t] = ("sbuf", [128, 96], B)
-    SCRATCH["RB%d" % _t] = ("sbuf", [128, 192], B)
+    SEMAPHORES += ["az%d" % _t, "au%d" % _t] + (["at%d" % _t] if _t < R - 1 else [])
+    SCRATCH["ZR%d" % _t] = ("sbuf", [128, 96], F)
+    SCRATCH["AB%d" % _t] = ("sbuf", [128, NB, 2, 16], B)
 for _n in range(8):
     SCRATCH["p%d" % _n] = ("psum", [128, 512], F)
 for _w, _d, _s in (
-        (UW, B, "U Tw FL"), (288, B, "UP"), (32, I, "CR"), (2048, B, "E2 E3 FX FD EH EL E1 LQ"), (2048, H, "WU WV KD"), (16384, B, "EQ"),
-        (512, F, "ior YC"), (544, F, "KD2 DA DB"), (1088, F, "KAB"), (102, F, "KE"), (512, B, "LJ"), (48, F, "la"), (2, I, "pi pq hwi"), (1, I, "kmi thi Pi Pj"), (1, F, "pf qf gf kmf thf"), (2, F, "hwf hwg hws hwm"),
-        (16, F, "io16 qm ql kq KM KS0 KS dA dB dC"), (16, I, "ki ka kb"), (128, F, "io8 io128 iox BF x1 x2 x3 x4 x5 x6 rep"), (128, B, "BD ID NI GE BH BL ZM"), (128, F, "O16"),
-        (96, F, "msk Hd Hj"), (32, F, "col tc tcq tc512 tc1024 tc4096 W40 W4 on idx T1 nf pen0 pen cum s1 OF lf hx hx0 hc wn wm wl ld hm lo l2 Cf cw ee ec mu rc pj pj2 fo jt jj a1 a2 a3 a4 a5 a6 a7 n1 n2 n3 n4 n5"),
-        (32, I, "PR qi k3 k4 Hh Ci f3 fi nx Ai"), (64, I, "uva kI kJ k2 dg"), (96, I, "uv"), (32, H, "uh qh hh"), (6, H, "ha"), (64, B, "dh dn"), (32, B, "pw wv"),
-        (32, U16, "OFu lou fou JJ JB ngu"), (8, U16, "glu sou"), (64, U16, "CL"), (512, U16, "HL HR"), (512, I, "X X2"),
-        (512, B, "JV L255 NB2 NG ZA Z TC GS LS JS DF0 DF1 DF2"), (1024, B, "JP NW JW AB0 AB1 AB2"), (528, B, "NR"), (1536, B, "ZS TS"), (384, B, "z4"), (576, F, "EA"),
-        (8, F, "k6 k7 gt gl gm gm0 gn go gp gh"), (192, B, "SB"), (96, B, "SU xt")):
+        (E + S + 512, F, "U"), (E + W, B, "Tw"), (E + S, B, "UO"), (288, B, "UP UQ"), (512, I, "C8 X X2"), (512, H, "c16"), (2048, B, "E1"), (2064, B, "Y"),
+        (2048, H, "KD"), (2048, F, "ZS"), (1024, F, "KAB"), (512, F, "ior YC LV PK DA DB HF"), (2304, B, "NE SC"), (576, B, "MK"), (1024, B, "JW"),
+        (512, B, "JO ZA Z GS NW D0 JS FG NG DF0 DF1 DF2"), (1536, B, "z16 AA"), (512, U16, "HL"), (192, H, "H0 H1 R2"), (192, F, "hr KE"), (192, I, "ua ub"),
+        (144, F, "io144"), (144, B, "B0 B8 FD FC FO FJ F0 F15"), (144, H, "WU WV"), (128, H, "RU RV"), (128, B, "BD BY ID NI DG GE"),
+        (128, F, "io8 iox BF SH1 SH2 O16 rep x1 x2"), (96, F, "t1 t2 T1a io96"), (96, I, "PRa kua qa Xa Xb"), (96, U16, "HA ZL"), (96, B, "ZRp SB SU L255"),
+        (2, I, "pi pq hwi"), (1, I, "kmi thi Pi Pj ei"), (1, F, "pf qf gf kmf thf e1 e2 e3 e4"), (2, F, "hwf hwg hws hwm"), (2, U16, "EN"),
+        (16, F, "io16 qm kq KM KS0 KS dA dB dC ecl ga"), (16, B, "mq"), (16, I, "ki kj ka kb"), (64, F, "rr"), (36, H, "G0 G1"), (36, F, "gr"), (33, F, "idx1"),
+        (40, F, "col"), (32, F, "tc tcq tc512 tc1024 tc4096 ntc W40 W4 on idx T1 nf pen0 pen cum ww OF lf hx0 r2 x2s hx nh n0 nlo la lb Cf Cb cw ee ec mu rc pj pj2 fo "
+                                "a1 a2 a3 a4 a5 dd Os Js df pl n4 w1 w2 w3 w4 yo"),
+        (32, I, "PR qi f3 fi nx Ci"), (64, I, "uva uv"), (32, H, "qh hh"), (8, H, "ha"), (32, B, "pw wv Dh Dl Ch Cl"), (32, U16, "OFu lou fou ngu Hs"),
+        (8, U16, "glu PL"), (64, U16, "CL"), (8, I, "pd"), (12, F, "ra"), (8, F, "k6 k7 s2 s3 ga1 ga2 ga3 gb pp")):
     for _n in _s.split():
-        if _w <= 64 and _n not in ("CR", "hwi", "kmi", "thi"):
+        if _w <= 64 and _n not in ("hwi", "kmi", "thi", "yo"):
             _k = "pk" + _d
             PACK[_n] = (_k, PACKED.get(_k, 0), _w)
             PACKED[_k] = PACKED.get(_k, 0) + (_w + 7) // 8 * 8
@@ -30,6 +35,8 @@ for _w, _d, _s in (
             SCRATCH[_n] = ("sbuf", [128, _w], _d)
 for _k, _w in PACKED.items():
     SCRATCH[_k] = ("sbuf", [128, _w], _k[2:])
+
+CYC, HOP, FAR = 0.83e-3, 0.17, 3.0
 
 
 def rank_program(g, core, T, topo):
@@ -39,109 +46,67 @@ def rank_program(g, core, T, topo):
     A, AF = AluOpType, ActivationFunctionType
     Q = {"V": g.vector, "S": g.scalar, "P": g.tensor, "G": g, "Y": g.sync}
     SEM = {"V": "sv", "S": "ss", "P": "sp", "G": "sg"}
-    count, known, snaps, rec = {}, {q: {} for q in Q}, {}, {}
+    calls = []
+
+    def is_bank(n):
+        return n[0] == "p" and n[1:].isdigit()
 
     def v(name, lo=None, hi=None, step=1, p=None):
         buf, at, w = PACK[name] if name in PACK else (name, 0, SCRATCH[name][1][1])
         lo = 0 if lo is None else lo
         hi = w if hi is None else hi
         rows = slice(None) if p is None else p
-        ap = T[buf][rows, at + lo:at + hi] if step == 1 else T[buf][rows, at + lo:at + hi:step]
-        return (ap, name, lo, hi, step)
+        if step < 0:
+            ap = T[buf][rows, hi - 1:(lo - 1 if lo else None):step]
+        else:
+            ap = T[buf][rows, at + lo:at + hi] if step == 1 else T[buf][rows, at + lo:at + hi:step]
+        reg = (name, 0, 512, 1) if is_bank(name) else (name, lo, hi, step)
+        return (ap, [reg], len(range(lo, hi, abs(step))), SCRATCH[buf][2] in (B, H, U16), None)
 
     def ind(win, off):
-        return (win[0].indirect(off[0]), (win, off))
-
-    def parts(x):
-        return list(x[1]) if len(x) == 2 else [x]
+        return (win[0].indirect(off[0]), win[1], 16 * off[2], win[3], off[1])
 
     def hit(a, b):
         if a[1] >= b[2] or b[1] >= a[2]:
             return False
         return not (a[3] == b[3] and a[3] > 1 and (a[1] - b[1]) % a[3])
 
-    def is_bank(n):
-        return n[0] == "p" and n[1:].isdigit()
-
-    def reg(x):
-        return (x[1], 0, 512, 1) if is_bank(x[1]) else (x[1], x[2], x[3], x[4])
-
-    def learn(q, e, n):
-        known[q][e] = max(known[q].get(e, 0), n)
-        for e2, n2 in snaps.get((e, n), {}).items():
-            known[q][e2] = max(known[q].get(e2, 0), n2)
-
-    def settle(q, reads, writes):
-        need = {}
-        for xs, isw in ((reads, False), (writes, True)):
-            for x in xs:
-                r = reg(x)
-                ps = is_bank(r[0])
-                for (o, e, n, w) in rec.get(r[0], []):
-                    if not hit(r, o):
-                        continue
-                    if e == q:
-                        if q == "P" or not (w or isw):
-                            continue
-                    elif not (w or isw or ps):
-                        continue
-                    need[e] = max(need.get(e, 0), count[e] if e[0] in "DL" else n)
-        for e, n in sorted(need.items(), key=lambda kv: -kv[1]):
-            if known[q].get(e, 0) < n:
-                Q[q].wait_ge(T.sem[SEM.get(e, e[1:])], n)
-                learn(q, e, n)
-
-    def note(e, n, reads, writes, snap):
-        snaps[(e, n)] = dict(snap)
-        for xs, isw in ((reads, False), (writes, True)):
-            for x in xs:
-                r = reg(x)
-                old = rec.setdefault(r[0], [])
-                if isw:
-                    old[:] = [o for o in old if not (o[0][1] >= r[1] and o[0][2] <= r[2] and r[3] == 1)]
-                old[:] = [o for o in old if not (o[0] == r and o[1] == e and o[3] == isw)]
-                old.append((r, e, n, isw))
-
-    def op(q, f, reads, writes):
-        rs = [p for x in reads if isinstance(x, tuple) for p in parts(x)]
-        ws = []
-        for x in writes:
-            ps = parts(x)
-            ws.append(ps[0])
-            rs += ps[1:]
-        settle(q, rs, ws)
-        count[q] = count.get(q, 0) + 1
-        f().then_inc(T.sem[SEM[q]], 1)
-        note(q, count[q], rs, ws, known[q])
-
-    def dma(q, sem, out, in_, reads, writes):
-        settle(q, reads, writes)
-        e = "D" + sem
-        count[e] = count.get(e, 0) + 16
-        Q[q].dma_start(out, in_).then_inc(T.sem[sem], 16)
-        note(e, count[e], reads, writes, known[q])
+    def add(q, f, reads, writes, cost, kind="C", sem=None, late=0.0, far=None):
+        rs = [r for x in reads if isinstance(x, tuple) for r in x[1]]
+        rs += [r for x in list(reads) + list(writes) if isinstance(x, tuple) and x[4] for r in x[4]]
+        calls.append(dict(q=q, f=f, rs=rs, ws=[r for x in writes for r in x[1]], cost=cost, kind=kind, sem=sem, late=late, far=far))
 
     def _(x):
         return x[0] if isinstance(x, tuple) else x
 
-    def ts(o, i, s1, op0, s2=None, op1=None):
-        rd = [i, s1, s2]
-        if op1 is None:
-            op("V", lambda: g.vector.tensor_scalar(out=_(o), in0=_(i), scalar1=_(s1), scalar2=None, op0=op0), rd, [o])
+    def op(q, f, o, ins, rate=None, more=()):
+        i = ins[0] if ins else o
+        if o[4]:
+            cost = 0.05 + 3.5 * o[2] * CYC
+        elif i[4]:
+            cost = 0.06 + 1.5 * i[2] * CYC
         else:
-            op("V", lambda: g.vector.tensor_scalar(out=_(o), in0=_(i), scalar1=_(s1), scalar2=_(s2), op0=op0, op1=op1), rd, [o])
+            cost = max(64, i[2] * (rate or (0.5 if all(x[3] for x in [o] + ins[:2] if isinstance(x, tuple) and x[2] > 1) else 1))) * CYC
+        add(q, f, ins, [o] + list(more), cost)
+
+    def ts(o, i, s1, op0, s2=None, op1=None):
+        if op1 is None:
+            op("V", lambda: g.vector.tensor_scalar(out=_(o), in0=_(i), scalar1=_(s1), scalar2=None, op0=op0), o, [i, s1])
+        else:
+            op("V", lambda: g.vector.tensor_scalar(out=_(o), in0=_(i), scalar1=_(s1), scalar2=_(s2), op0=op0, op1=op1), o, [i, s1, s2])
 
     def tt(o, a, b, op0):
-        op("V", lambda: g.vector.tensor_tensor(out=_(o), in0=_(a), in1=_(b), op=op0), [a, b], [o])
+        psum = is_bank(a[1][0][0]) or is_bank(b[1][0][0])
+        op("V", lambda: g.vector.tensor_tensor(out=_(o), in0=_(a), in1=_(b), op=op0), o, [a, b], 1 if psum else 2)
 
     def cp(o, i):
-        op("V", lambda: g.vector.tensor_copy(out=_(o), in_=_(i)), [i], [o])
+        op("V", lambda: g.vector.tensor_copy(out=_(o), in_=_(i)), o, [i])
 
     def ms(o, c):
-        op("V", lambda: g.vector.memset(_(o), c), [], [o])
+        op("V", lambda: g.vector.memset(_(o), c), o, [])
 
     def scan(o, a, b, init, op0, op1):
-        op("V", lambda: g.vector.tensor_tensor_scan(_(o), _(a), _(b), init, op0, op1), [a, b], [o])
+        op("V", lambda: g.vector.tensor_tensor_scan(_(o), _(a), _(b), init, op0, op1), o, [a, b])
 
     def act(o, i, func=AF.Copy, scale=None, bias=None):
         kw = {}
@@ -149,588 +114,542 @@ def rank_program(g, core, T, topo):
             kw["scale"] = _(scale)
         if bias is not None:
             kw["bias"] = _(bias)
-        op("S", lambda: g.scalar.activation(_(o), _(i), func, **kw), [i, scale, bias], [o])
-
-    def add_up(o, i, total):
-        op("S", lambda: g.scalar.activation(_(o), _(i), AF.Copy, accum_out=_(total)), [i], [o, total])
-
-    def weave(a, b, lead=0):
-        for k in range(lead):
-            next(a, None)
-        more = [a, b]
-        while more:
-            more = [x for x in more if next(x, more) is not more]
+        op("S", lambda: g.scalar.activation(_(o), _(i), func, **kw), o, [i, scale, bias], 1)
 
     def mm(o, l, r, start=True, stop=True):
-        op("P", lambda: g.tensor.matmul(_(o), _(l), _(r), start, stop), [l, r], [o])
+        add("P", lambda: g.tensor.matmul(_(o), _(l), _(r), start, stop), [l, r], [o], (1 if r[3] else 4) * max(64, r[2]) * CYC)
 
     def iota(o, pattern, base, cm, flag=True):
-        op("G", lambda: g.iota(_(o), pattern, base, cm, allow_small_or_imprecise_dtypes=True) if flag else g.iota(_(o), pattern, base, cm), [], [o])
+        add("G", lambda: g.iota(_(o), pattern, base, cm, allow_small_or_imprecise_dtypes=True) if flag else g.iota(_(o), pattern, base, cm), [], [o], 0.13 + 2 * o[2] * CYC)
+
+    def dma(q, sem, out, in_, reads, writes, late=2.0, first=False):
+        add(q, lambda: Q[q].dma_start(out, in_), reads, writes, 0.05, "F" if first else "D", sem, late)
+
+    def send(sem, lsem, dst, out, src):
+        es = topo.engines(core, dst)[:8]
+        rid, pid, se = topo.addr(dst)
+        add("G", lambda: g.remote_dma(out[0], src[0], T.sem[sem], T.sem[lsem], pid, rid, sum(1 << k for k in es)), [src], [], 0.6, "R", (lsem, len(es)), FAR, out[1])
 
     def col(j):
         return v("col", j, j + 1)
 
-    def mat(name, q):
-        return v(name, 128 * q, 128 * q + 128)
+    def mat(name, q, shift=0):
+        return v(name, 128 * q - shift, 128 * q + 128 - shift)
 
-    def send(sem, lsem, dst, out, in_, reads):
-        settle("G", reads, [])
-        es = topo.engines(core, dst)[:8]
-        rid, pid, se = topo.addr(dst)
-        e = "L" + lsem
-        count[e] = count.get(e, 0) + len(es)
-        g.remote_dma(out, in_, T.sem[sem], T.sem[lsem], pid, rid, sum(1 << k for k in es))
-        note(e, count[e], reads, [], known["G"])
+    def slid(name, q, p=None):
+        return v(name, 16 - q, 144 - q, p=p)
 
-    for t in range(R):
-        asker, lender = T.cores[(rank - 1 - t) % 8], T.cores[(rank + 1 + t) % 8]
-        for sem, src, ws in (("az%d" % t, asker, [v("ZR%d" % t)]), ("ar%d" % t, lender, [v("RB%d" % t)]), ("au%d" % t, lender, [v("UP", 96 * t, 96 * t + 96)])):
-            n = len(topo.engines(src, core)[:8])
-            count["A" + sem] = n
-            note("A" + sem, n, [], ws, {})
+    def half(k, j):
+        return (T["AB%d" % k][:, :, j, :], [("AB%d.%d" % (k, j), 0, 1, 1)], 512, True, None)
 
-    dma("Y", "d0", T.CR[:, :], T.c0[:, :], [], [v("CR")])
-    dma("S", "d1", T.hwi[:, :], T.hw[:, :], [], [v("hwi")])
-    dma("S", "d1", T.kmi[:, :], T.km[:, :], [], [v("kmi")])
+    def both(k, q):
+        return (T["AB%d" % k][:, :, :, q], [("AB%d.0" % k, 0, 1, 1), ("AB%d.1" % k, 0, 1, 1)], 64, True, None)
+
+    def to_list(ps, wt, row, dense=False):
+        for q in range(16):
+            mm(ps, slid(wt, q), v(row, 32 * q, 32 * q + 32) if dense else v(row, q, 512, 16), q == 0, q == 15)
+
+    P8 = slice(0, 8)
+    LO, HI, C256, CN256, LAID, ZSC, ZBI, CU, CV, TH = 0, 1, 2, 3, 4, 5, 6, 7, 8, 9
+    THR, TMP, LSC, LBI, FSC, FBI, JBI, FILL, EA, EG, EB, WC, B0C = 10, 12, 13, 14, 15, 16, 17, 18, 19, 20, 21, 22, 23
+
+    dma("Y", "d0", T.C8[0:8, :], T.c0[:, :], [], [v("C8")], 2.0, True)
+    dma("S", "d1", T.hwi[:, :], T.hw[:, :], [], [v("hwi")], 2.2, True)
+    dma("S", "d1", T.kmi[:, :], T.km[:, :], [], [v("kmi")], 2.2, True)
     for k in range(16):
         lo = 8 * k
-        dma("S" if k % 2 else "Y", "d2", T.Tw[lo:lo + 8, 0:S], T.tp[(lo ^ 8):(lo ^ 8) + 8, :], [], [v("Tw", 0, S)] if k == 15 else [])
-    dma("Y", "dt", T.thi[0:8, :], T.th[:, :], [], [v("thi")])
+        dma("S" if k % 2 else "Y", "d2", T.Tw[lo:lo + 8, E:E + S], T.tp[(lo ^ 8):(lo ^ 8) + 8, :], [], [v("Tw", E, E + S)] if k == 15 else [], 6.0, True)
+    dma("Y", "dt", T.thi[0:8, :], T.th[:, :], [], [v("thi")], 6.0, True)
     for k in range(4):
-        dma("Y", "du%d" % k, T.U[:, 1024 * k:1024 * k + 1024], T.us[:, 1024 * k:1024 * k + 1024], [], [v("U", 1024 * k, 1024 * k + 1024)])
+        x = v("UO", E + 1024 * k, E + 1024 * k + 1024)
+        dma("Y", "du%d" % k, x[0], T.us[:, 1024 * k:1024 * k + 1024], [], [x], 7.5 + 1.2 * k, True)
 
     iota(v("pi"), [[0, 2]], 0, 1, False)
+    iota(v("io144"), [[1, 144]], -16, 0)
     iota(v("io16"), [[1, 16]], 0, 0)
     iota(v("io8"), [[1, 8], [0, 16]], 0, 0)
     iota(v("iox"), [[0, 8], [1, 16]], 0, 0)
-    iota(v("E2"), [[-1, 16], [32, 8], [1, 16]], 0, 0)
-    iota(v("io128"), [[1, 128]], 0, 0)
-    iota(v("E3"), [[1, 16], [32, 8], [0, 16]], 0, 0)
     iota(v("tc"), [[16, 32]], 0, 0)
     iota(v("ior"), [[1, 512]], -256, 0)
-    iota(v("FL", 0, ZC), [[0, ZC]], 0, 0)
-    iota(v("FL", ZC, UW), [[0, UW - ZC]], 1, 0)
+    io128 = v("io144", 16, 144)
     cp(v("pf"), v("pi", 0, 1))
     ts(v("pq", 0, 1), v("pi", 0, 1), 4, A.arith_shift_right)
     ts(v("pq", 1, 2), v("pi", 0, 1), 15, A.bitwise_and)
     cp(v("gf"), v("pq", 0, 1))
     cp(v("qf"), v("pq", 1, 2))
     ts(v("qm"), v("io16"), v("qf"), A.is_equal)
+
+    def qm(q):
+        return v("qm", q, q + 1)
     ts(v("BD"), v("io8"), v("gf"), A.is_equal)
-    ts(v("x1"), v("iox"), 2.0, A.is_equal, 128.0, A.mult)
-    ts(v("x2"), v("iox"), 0.0, A.is_equal)
-    tt(v("x3"), v("x1"), v("x2"), A.add)
-    tt(v("BH"), v("x3"), v("BD"), A.mult)
-    for q in range(16):
-        act(mat("EH", q), v("BH"), scale=v("qm", q, q + 1))
-    ts(v("x4"), v("iox"), 2.0, A.is_equal)
-    ts(v("x5"), v("iox"), 1.0, A.is_equal)
-    tt(v("x6"), v("x4"), v("x5"), A.add)
-    tt(v("BL"), v("x6"), v("BD"), A.mult)
-    for q in range(16):
-        ts(mat("EL", q), v("BL"), v("qm", q, q + 1), A.mult)
-    ts(v("dg", 0, 32), v("CR"), 7, A.arith_shift_right)
-    ts(v("dg", 32, 64), v("CR"), 127, A.bitwise_and)
-    cp(v("dh"), v("dg"))
-    for q in range(16):
-        mm(v("p6", 32 * q, 32 * q + 32), mat("EH", q), v("dh", 0, 32), True, False)
-        mm(v("p6", 32 * q, 32 * q + 32), mat("EL", q), v("dh", 32, 64), False, True)
-    ms(v("NR", 512, 528), 0.0)
-    act(v("NR", 0, 512), v("p6"))
-    ts(col(0), v("qf"), 7.5, A.is_lt)
-    ts(col(4), v("qm", 0, 1), 128.0, A.mult)
-    tt(col(15), col(4), v("qm", 1, 2), A.add)
-    ts(col(13), v("gf"), 32.0, A.mult)
-    tt(col(14), col(13), v("qf"), A.add)
-    ts(v("FX"), v("E2"), col(13), A.is_equal, col(15), A.mult)
-    for j in (0, 1):
-        for q in range(16):
-            mm(v("p0", 32 * j, 32 * j + 32), mat("FX", q), v("NR", j + q, j + 512, 16), q == 0, q == 15)
     ts(v("BF"), v("io8"), v("gf"), A.is_equal)
-    ts(col(1), col(0), -512.0, A.mult, 256.0, A.add)
-    ts(col(2), col(0), -256.0, A.mult)
-    ts(col(3), col(0), 256.0, A.mult)
-    ts(col(5), col(0), -256.0, A.mult, 255.0, A.add)
-    ts(col(6), v("qm", 1, 2), -512.0, A.mult)
-    ms(v("Tw", S, UW), 0.0)
+    ts(v("ID"), io128, v("pf"), A.is_equal)
+    ts(v("NI"), io128, v("pf"), A.is_equal, -1.0, A.mult)
+    ts(col(LO), v("qf"), 7.5, A.is_lt)
+    ts(col(HI), v("qf"), 7.5, A.is_gt)
+    ts(col(C256), col(LO), 256.0, A.mult)
+    ts(col(CN256), col(LO), -256.0, A.mult)
+    ts(col(LAID), col(LO), -256.0, A.mult, 255.0, A.add)
+    ts(col(ZSC), col(LO), -255.0, A.mult, 256.0, A.add)
+    ts(col(ZBI), col(LO), -512.0, A.mult, 256.0, A.add)
+    ts(col(B0C), v("gf"), 16.0, A.mult)
+    ts(v("B0"), v("io144"), col(B0C), A.is_equal)
+    ts(v("e1", p=P8), v("pf", p=P8), 16.0, A.mult)
+    ts(v("B8", p=P8), v("io144", p=P8), v("e1", p=P8), A.is_equal)
+    ts(v("c16", p=P8), v("C8", p=P8), -2048.0, A.add)
+    for q in range(16):
+        mm(v("p7", 0, 32), slid("B8", q, P8), v("c16", q, 512, 16, P8), q == 0, q == 15)
+    ms(v("idx1", 32, 33), OFS)
+    ts(v("idx1", 0, 32), v("p7", 0, 32), 2048.0 + OFS, A.add)
+    ts(v("e2"), v("pf"), -1.0, A.add)
+    ts(v("e3"), v("qf"), 0.5, A.is_gt)
+    ts(v("SH1"), io128, v("e2"), A.is_equal, v("e3"), A.mult)
+    ts(v("e4"), v("pf"), 15.0, A.add)
+    ts(v("SH2"), io128, v("e4"), A.is_equal, qm(0), A.mult)
     cp(v("hwf"), v("hwi"))
     ts(v("hwg"), v("hwf"), 2048.0, A.is_ge, -4096.0, A.mult)
     tt(v("hws"), v("hwg"), v("hwf"), A.add)
-    ts(v("hwm"), v("hws"), col(3), A.mult)
+    ts(v("hwm"), v("hws"), col(C256), A.mult)
     cp(v("kmf"), v("kmi"))
     ts(v("kq"), v("qm"), v("kmf"), A.mult)
     mm(v("p5", 0, 2), v("BF"), v("hwm"))
     mm(v("p5", 2, 18), v("BF"), v("kq"))
-    ts(v("WU"), v("E2"), col(13), A.is_equal, v("hws", 0, 1), A.mult)
-    cp(v("col", 7, 9), v("p5", 0, 2))
+    cp(v("col", CU, CV + 1), v("p5", 0, 2))
     cp(v("KM"), v("p5", 2, 18))
+    for j, (a, b) in enumerate((("WU", "RU"), ("WV", "RV"))):
+        ts(v(a), v("B0"), v("hws", j, j + 1), A.mult)
+        ts(v(b), v("BD"), v("hws", j, j + 1), A.mult)
+    ts(v("KS0"), v("KM"), 2048.0, A.is_ge, -4096.0, A.mult)
+    tt(v("KS"), v("KS0"), v("KM"), A.add)
+    for m in range(16):
+        ts(mat("KD", m), v("ID"), v("KS", m, m + 1), A.mult)
+    ts(v("FD"), v("B0"), 4096.0, A.mult)
+    tt(col(FILL), qm(2), qm(8), A.add)
+    tt(col(TMP), qm(0), qm(1), A.add)
+    tt(col(WC), col(TMP), col(FILL), A.add)
+    for name, wt in (("FC", col(WC)), ("FO", col(FILL)), ("FJ", qm(6)), ("F0", qm(0)), ("F15", qm(15))):
+        act(v(name), v("B0"), scale=wt)
+    ts(v("ki"), v("KM"), -1.0, A.mult, v("KM", 15, 16), A.add)
+    ts(v("kj"), v("ki"), 4095, A.bitwise_and)
+    ts(v("ka"), v("kj"), 6, A.arith_shift_right)
+    ts(v("kb"), v("kj"), 63, A.bitwise_and)
+    ts(v("dC"), v("io16"), 256.0, A.mult, -3840.0, A.add)
+    for d, D, k in (("dA", "DA", "ka"), ("dB", "DB", "kb")):
+        tt(v(d), v("dC"), v(k), A.subtract)
+        tt(v(D, 1, 16), v(d, 0, 15), v(d, 1, 16), A.subtract)
+        ms(v(D, 0, 1), 33554432.0)
+        w = 16
+        while w < 512:
+            act(v(D, w, 2 * w), v(D, 0, w))
+            w *= 2
+    for a, b, n in (("H0", "H1", NB), ("G0", "G1", NA)):
+        for name, step, c in ((a, 0, 0.0), (a, 1, 1.0), (a, 2, 64.0), (a, 3, 1.0), (a, 5, 1.0), (b, 1, -1280.0), (b, 3, -1280.0), (b, 5, 0.5)):
+            ts(v(name, step, 6 * n, 6), v("tc", 0, n), 0.0, A.mult, c, A.add)
+    ts(v("rep", p=P8), v("io8", p=P8), v("pf", p=P8), A.is_equal)
+    cp(v("thf", p=P8), v("thi", p=P8))
+    mm(v("p5", 0, 1), v("rep", p=P8), v("thf", p=P8))
+    cp(col(TH), v("p5", 0, 1))
+    ts(col(THR), col(TH), 4096.0, A.mult, -3968.0, A.add)
+    ts(v("x1"), io128, v("pf"), A.is_le)
+    tt(v("GE"), v("x1"), v("BD"), A.mult)
+    ms(v("on"), 1.0)
+    ms(v("O16"), 0.0625)
+    ts(v("tcq"), v("tc"), v("qf"), A.add)
+    for n in (512, 1024, 4096):
+        ts(v("tc%d" % n), v("tcq"), float(n), A.add)
+    ts(v("ntc"), v("tc4096"), -1.0, A.mult)
+    ts(v("W40"), v("tcq"), 510.0, A.is_equal, 5112.0, A.mult)
+    ts(v("W4"), v("W40"), 4.0, A.add)
+    ts(v("x1"), v("iox"), 0.0, A.is_equal)
+    ts(v("x2"), v("iox"), 3.0, A.is_equal)
+    tt(v("x1"), v("x1"), v("x2"), A.add)
+    tt(v("BY"), v("x1"), v("BD"), A.mult)
+    ms(v("Y", 0, 16), 0.0)
+    for q in range(16):
+        act(mat("E1", q), v("BD"), scale=qm(q))
+        act(mat("Y", q, -16), v("BY"), scale=qm(q))
+    ts(col(TMP), col(HI), 2.0 ** -18, A.mult)
+    ts(v("DG"), v("ID"), col(TMP), A.mult)
+    ts(col(LSC), qm(0), 2.0 ** -24, A.mult)
+    ts(col(LBI), qm(0), 2.0 ** -16, A.mult, col(LAID), A.add)
+    act(v("LV"), v("ior"), AF.Identity, scale=col(LSC), bias=col(LBI))
+    ts(col(FSC), qm(0), 2.0 ** 24, A.mult)
+    ts(col(FBI), qm(0), 2.0 ** 24 - 256.0, A.mult)
+    ts(col(TMP + 20), qm(2), 128.0, A.mult)
+    ts(col(JBI), qm(8), 65.0, A.mult, col(TMP + 20), A.add)
+    act(v("JO"), v("ior"), AF.Identity, scale=qm(6), bias=col(JBI))
+    act(v("L255"), v("ior", 0, 96), AF.Identity, scale=0.0, bias=col(LAID))
+    ts(col(EA), col(HI), 1024.0, A.mult)
+    tt(col(EG), col(C256), col(HI), A.subtract)
+    tt(col(EB), col(LO), col(EA), A.subtract)
+    ms(v("MK"), 0.0)
+    ts(v("ga"), v("io16"), v("qf"), A.add)
+    ts(v("mq"), v("ga"), 15.5, A.is_lt, 16384.0, A.mult)
+    for i in range(8):
+        act(v("MK", 8 * i * (i + 1), 8 * i * (i + 1) + 16), v("mq"))
+    ts(v("ei"), v("pq", 1, 2), 7, A.bitwise_and)
+    ts(v("e2"), v("ei"), 8.0, A.mult, 8.0, A.add)
+    ts(v("e3"), v("ei"), 2.0, A.add, v("e2"), A.mult)
+    ts(v("e4"), col(HI), 576.0, A.mult, -1.0, A.add)
+    ts(v("EN", 0, 1), v("e3"), v("e4"), A.add)
+    ts(v("pd", 0, NA), v("tcq", 0, NA), 1.0 / 6.0, A.mult, -5.0 / 12.0, A.add)
+    ts(v("pp", 0, NA), v("pd", 0, NA), -95.0, A.mult)
+    ts(v("s2", 0, NA), v("tcq", 0, NA), 16.0, A.mult)
+    tt(v("s3", 0, NA), v("s2", 0, NA), v("pp", 0, NA), A.add)
+    cp(v("PL", 0, NA), v("s3", 0, NA))
+    cp(v("ZL"), v("io144", 16, 112))
+    ts(v("e1"), v("qf"), 6.0, A.mult)
+    ts(v("ecl"), v("io16"), v("e1"), A.add)
+    ms(v("U", E + S, E + S + 512), 0.0)
+    for k in range(4):
+        x, y = v("U", E + 1024 * k, E + 1024 * k + 1024), v("UO", E + 1024 * k, E + 1024 * k + 1024)
+        if k == 3:
+            ts(x, y, col(CN256), A.add)
+        else:
+            act(x, y, AF.Identity, bias=col(CN256))
 
-    def setup_hash():
-        ts(v("WV"), v("E2"), col(13), A.is_equal, v("hws", 1, 2), A.mult)
-        ts(v("KS0"), v("KM"), 2048.0, A.is_ge, -4096.0, A.mult)
-        ts(v("ID"), v("io128"), v("pf"), A.is_equal)
-        tt(v("KS"), v("KS0"), v("KM"), A.add)
-        for m in range(16):
-            ts(mat("KD", m), v("ID"), v("KS", m, m + 1), A.mult)
-        ts(v("NI"), v("ID"), -1.0, A.mult)
+    def best(n, keys, d0, d1, hr, rr, r2, x2, off, outs):
+        ts(v(rr, 0, 2 * n), v(keys, 15, 32 * n, 16), M256, A.add, M256 + 1280.0, A.subtract)
+        for j in (0, 1):
+            tt(v(d1, 2 * j, 6 * n, 6), v(keys, 16 * n * j + 15, 16 * n * (j + 1), 16), v(rr, n * j, n * j + n), A.subtract)
+        scan(v(hr, 0, 6 * n), v(d0, 0, 6 * n), v(d1, 0, 6 * n), 0.0, A.mult, A.add)
+        ts(v(r2, 0, n), v(hr, 5, 6 * n, 6), M4096, A.add, M4096, A.subtract)
+        tt(v(x2, 0, n), v(hr, 5, 6 * n, 6), v(off, 0, n), A.add)
+        for o in outs:
+            tt(v(o, 0, n), v(x2, 0, n), v(r2, 0, n), A.subtract)
 
-    def setup_fill():
-        act(v("NW", 512, 1024), v("p6"))
-        act(v("JV"), v("ior"), scale=v("qm", 1, 2))
-        act(v("JP"), v("E2", 0, 1024), AF.Identity, scale=0.0, bias=col(6))
-        act(v("JW"), v("JP"))
-        act(v("L255"), v("E2", 0, 512), AF.Identity, scale=0.0, bias=col(5))
+    def split(hi, lo, x):
+        ts(v(hi), v(x), M128, A.add, M128, A.subtract)
+        tt(v(lo), v(x), v(hi), A.subtract)
 
-    def setup_late():
-        ms(v("U", S, ZC), 0.0)
-        ts(v("U", ZC, UW), v("Tw", ZC, UW), col(2), A.add)
-        cp(v("Cf"), v("idx"))
-        cp(v("Ci"), v("idx"))
-        ts(v("FD"), v("E2"), col(13), A.is_equal, 4096.0, A.mult)
-        cp(v("ki"), v("KM"))
-        ts(v("ka"), v("ki"), 4, A.arith_shift_right)
-        ts(v("kb"), v("ki"), 15, A.bitwise_and)
-        ts(v("dC"), v("io16"), 256.0, A.mult)
-        tt(v("dB"), v("dC"), v("kb"), A.add)
-        tt(v("dA"), v("dC"), v("ka"), A.add)
-
-    def setup_last():
-        yield
-        for d, D in (("dA", "DA"), ("dB", "DB")):
-            tt(v(D, 1, 16), v(d, 0, 15), v(d, 1, 16), A.subtract)
-            ms(v(D, 0, 1), 33554432.0)
-            cp(v(D, 16, 17), v(d, 15, 16))
-            w = 17
-            while w < 544:
-                act(v(D, w, 2 * w), v(D, 0, w))
-                w *= 2
-        ms(v("KD2", 16, 544, 17), 67108864.0)
-        ms(v("KE", 16, 102, 17), 67108864.0)
-        yield
-        ts(v("rep", p=slice(0, 8)), v("io8", p=slice(0, 8)), v("pf", p=slice(0, 8)), A.is_equal)
-        cp(v("thf", p=slice(0, 8)), v("thi", p=slice(0, 8)))
-        mm(v("p5", 0, 1), v("rep", p=slice(0, 8)), v("thf", p=slice(0, 8)))
-        ts(v("x1"), v("io128"), v("pf"), A.is_le)
-        tt(v("GE"), v("x1"), v("BD"), A.mult)
-        ms(v("on"), 1.0)
-        ts(v("tcq"), v("tc"), v("qf"), A.add)
-        yield
-        for n in (512, 1024, 4096):
-            ts(v("tc%d" % n), v("tcq"), float(n), A.add)
-        ts(v("W40"), v("tcq"), 510.0, A.is_equal, 5112.0, A.mult)
-        ts(v("W4"), v("W40"), 4.0, A.add)
-        cp(col(9), v("p5", 0, 1))
-        ts(col(10), col(9), 4081.0, A.min, 4096.0, A.mult)
-        yield
-        ms(v("O16"), 0.0625)
-        ms(v("ZM"), 0.0)
-        ts(v("ql"), v("io16"), v("qf"), A.is_gt)
-        for q in range(1, 16):
-            act(mat("LQ", q), v("BD"), scale=v("ql", q, q + 1))
-        ms(v("ZS", 0, 96), 1024.0)
-        ms(v("TS", 0, 96), 0.0)
-        yield
-        ts(v("E1"), v("E3"), col(14), A.is_equal)
-        ts(v("msk"), v("iox", 0, 96), v("qf"), A.is_ge, 30000.0, A.mult)
-        yield
-
-    def to_list(ps, row, lo=0, n=512):
-        for q in range(16):
-            mm(ps, mat("FX", q), v(row, lo + q, lo + n, 16), q == 0, q == 15)
-
-    def digits(src, name="dh"):
-        ts(v("dg", 0, 32), src, 7, A.arith_shift_right)
-        ts(v("dg", 32, 64), src, 127, A.bitwise_and)
-        cp(v(name), v("dg"))
-
-    def rows(name):
-        for q in range(16):
-            mm(v("p6", q, 512, 16), mat("EH", q), v(name, 0, 32), True, False)
-            mm(v("p6", q, 512, 16), mat("EL", q), v(name, 32, 64), False, True)
-
-    def hash_sums(z, nb):
-        n = 16 * nb
-        for j, w in ((0, "WU"), (1, "WV")):
+    def rows(hi, lo, sh, sl):
+        for name, shift in ((hi, sh), (lo, sl)):
             for q in range(16):
-                mm(v("p0", 32 * j, 32 * j + nb), mat(w, q), v(z, q, n, 16), q == 0, q == 15)
+                mm(v("p6", q, 512, 16), mat("Y", q, shift - 16), v(name), False, name == "Dl" and q == 15)
 
-    def hash_uv(nb):
-        ts(v("uva", 0, nb), v("p0", 0, nb), col(7), A.add)
-        yield
-        ts(v("uva", nb, 2 * nb), v("p0", 32, 32 + nb), col(8), A.add)
-        yield
-        ts(v("uv", nb, 3 * nb), v("uva", 0, 2 * nb), 4095, A.bitwise_and)
-        yield
-        tt(v("PR", 0, nb), v("uv", nb, 2 * nb), v("uv", 2 * nb, 3 * nb), A.mult)
-        yield
-        ts(v("T1", 0, nb), v("uv", nb, 2 * nb), 2048.0, A.is_ge, -4096.0, A.mult)
-        yield
-        ts(v("qi", 0, nb), v("PR", 0, nb), 5, A.arith_shift_right, 4095, A.bitwise_and)
-        yield
-        tt(v("uh", 0, nb), v("T1", 0, nb), v("uv", nb, 2 * nb), A.add)
-        yield
-        ts(v("qh", 0, nb), v("qi", 0, nb), -2048.0, A.add)
-        yield
-        ts(v("uv", 0, nb), v("uv", nb, 2 * nb), 16.0, A.mult)
-        yield
+    def flags(t, dense):
+        act(v("NG"), ind(v("UP", 96 * t, 96 * t + 96), v("ngu")), AF.Relu, scale=-1.0 / 2048.0, bias=col(TMP + 21))
+        to_list(v("p7", 0, 32), "F0", "NG", dense)
+        tt(v("w4"), v("p7", 0, 32), v("n4"), A.mult)
+    ms(col(TMP + 21), -1.0)
 
-    def hash_lists(nb, ps, lo, hi):
-        for m in range(lo, hi):
-            o = v(ps, (m - lo) * nb, (m - lo) * nb + nb)
-            mm(o, mat("KD", m), v("uh", 0, nb), True, False)
-            mm(o, v("ID"), v("qh", 0, nb), False, True)
-
-    def lists(ps, at, o, w):
-        ts(v("X", o, o + w), v(ps, at, at + w), 2048.0, A.add)
-        yield
-        ts(v("X2", o, o + w), v("X", o, o + w), 4095, A.bitwise_and)
-        yield
-        cp(v("HL", o, o + w), v("X2", o, o + w))
-        yield
-
-    def best(nb, keys):
-        cp(v("kI", 0, 2 * nb), keys)
-        yield
-        ts(v("kJ", 0, 2 * nb), v("kI", 0, 2 * nb), 255, A.bitwise_and)
-        yield
-        tt(v("k2", 0, 2 * nb), v("kJ", 0, 2 * nb), v("uv", 0, 2 * nb), A.mult)
-        yield
-        tt(v("k3", 0, nb), v("k2", 0, nb), v("k2", nb, 2 * nb), A.add)
-        yield
-        tt(v("k4", 0, nb), v("k3", 0, nb), v("qi", 0, nb), A.add)
-        yield
-        ts(v("Hh", 0, nb), v("k4", 0, nb), 4095, A.bitwise_and)
-        yield
-
-    def poor():
-        ts(v("nf"), v("KAB", 16, 544, 17), col(10), A.is_ge)
-        yield
-        tt(v("pw"), v("nf"), v("mu"), A.mult)
-        mm(v("p5", 0, 32), v("BD"), v("pw"))
-        mm(v("p5", 32, 64), v("GE"), v("pw"))
-        yield
-        ts(v("pen0"), v("pw"), 0.5, A.is_lt)
-        yield
-        tt(v("lf"), v("rc"), v("nf"), A.is_gt)
-        yield
-        tt(v("pen"), v("pen0"), v("tc1024"), A.mult)
-        yield
-        scan(v("cum"), v("on"), v("p5", 0, 32), 0.0, A.mult, A.add)
-        yield
-        ts(v("hx0"), v("lf"), -8192.0, A.mult, 8192.0 - 2048.0, A.add)
-        yield
-        tt(v("s1"), v("cum"), v("p5", 32, 64), A.subtract)
-        yield
-        tt(v("OF"), v("s1"), v("pen"), A.max)
-        yield
-        cp(v("OFu"), v("OF"))
-        yield
-
-    def laid():
-        ts(v("wl"), v("p5", 192, 224), 0.5, A.is_lt)
-        yield
-        tt(v("ld"), v("wl"), v("wm"), A.mult)
-        yield
-        tt(v("lo"), v("ld"), v("hm"), A.mult)
-        yield
-        tt(v("l2"), v("lo"), v("tc4096"), A.add)
-        yield
-        cp(v("lou"), v("l2"))
-        yield
-
-    def widths():
+    for t in range(R):
+        last = t == R - 1
+        lender, asker = T.cores[(rank + 1 + t) % 8], T.cores[(rank - 1 - t) % 8]
+        base, thr = float(S + 96 * t), col(THR + t % 2)
+        stones = v("U", E, E + S)
+        ts(v("CL", 0, 32), v("idx1", 0, 32), -OFS, A.add)
+        mm(v("p7", 32, 64), v("SH1"), v("idx1", 0, 32), True, False)
+        mm(v("p7", 32, 64), v("SH2"), v("idx1", 1, 33), False, True)
+        ts(v("CL", 32, 64), v("p7", 32, 64), -OFS, A.add)
+        ts(v("idx"), v("idx1", 0, 32), -OFS, A.add)
+        tops = v("Tw", E, E + S + 96 * t)
+        act(v("ZA"), ind(tops, v("CL", 0, 32)), AF.Identity, scale=col(ZSC), bias=col(ZBI))
+        tt(v("Z"), ind(tops, v("CL", 32, 64)), v("ZA"), A.min)
+        for j, wt in ((0, "WU"), (1, "WV")):
+            to_list(v("p%d" % j, 0, 32), wt, "Z")
+            ts(v("uva", 32 * j, 32 * j + 32), v("p%d" % j, 0, 32), col(CU + j), A.add)
+            ts(v("uv", 32 * j, 32 * j + 32), v("uva", 32 * j, 32 * j + 32), 4095, A.bitwise_and)
+        uh = v("H0", 4, 6 * NB, 6)
+        ts(v("T1"), v("uv", 0, 32), 2048.0, A.is_ge, -4096.0, A.mult)
+        tt(uh, v("T1"), v("uv", 0, 32), A.add)
+        tt(v("PR"), v("uv", 0, 32), v("uv", 32, 64), A.mult)
+        ts(v("qi"), v("PR"), 5, A.arith_shift_right, 4095, A.bitwise_and)
+        ts(v("qh"), v("qi"), -2048.0, A.add)
+        for lo, hi, bank in ((0, 2, "p2"), (2, 8, "p3"), (8, 16, "p2")):
+            for i in range(lo, hi):
+                o = v(bank, 32 * i, 32 * i + 32)
+                mm(o, mat("KD", i // 2 + 8 * (i % 2)), uh, True, lo == 0)
+                if lo:
+                    mm(o, v("ID"), v("qh"), False, True)
+            if lo == 0:
+                for i in range(lo, hi):
+                    tt(v("X", 32 * i, 32 * i + 32), v(bank, 32 * i, 32 * i + 32), v("qi"), A.add)
+            else:
+                ts(v("X", 32 * lo, 32 * hi), v(bank, 32 * lo, 32 * hi), 2048.0, A.add)
+            ts(v("X2", 32 * lo, 32 * hi), v("X", 32 * lo, 32 * hi), 4095, A.bitwise_and)
+            cp(v("HL", 32 * lo, 32 * hi), v("X2", 32 * lo, 32 * hi))
+        ts(v("H1", 4, 6 * NB, 6), v("X2", 480, 512), -2048.0, A.add)
+        if t:
+            flags(t - 1, False)
+            tt(v("Cf"), v("idx"), v("w4"), A.subtract)
+            tt(v("Ci"), v("idx"), v("w4"), A.subtract)
+        else:
+            cp(v("Cf"), v("idx"))
+            cp(v("Ci"), v("idx"))
         ts(v("f3"), v("Ci"), 3, A.bitwise_and)
         tt(v("wv"), v("f3"), v("W4"), A.add)
-        mm(v("p5", 64, 96), v("BD"), v("wv"))
-        mm(v("p5", 96, 128), v("GE"), v("wv"))
-        yield
-        yield
-        scan(v("cw"), v("on"), v("p5", 64, 96), 0.0, A.mult, A.add)
-        tt(v("ee"), v("cw"), v("p5", 96, 128), A.subtract)
+        mm(v("p7", 64, 96), v("BD"), v("wv"))
+        mm(v("p7", 96, 128), v("GE"), v("wv"))
+        scan(v("cw"), v("on"), v("p7", 64, 96), 0.0, A.mult, A.add)
+        tt(v("ee"), v("cw"), v("p7", 96, 128), A.subtract)
         tt(v("ec"), v("ee"), v("wv"), A.add)
-        yield
         ts(v("fi"), v("ee"), 0.2, A.mult, 512.0, A.min)
         ts(v("nx"), v("ec"), 0.2, A.mult, 512.0, A.min)
         tt(v("mu"), v("nx"), v("fi"), A.subtract)
-        yield
         ts(v("rc"), v("mu"), 0.5, A.is_ge)
         ts(v("pj"), v("mu"), 0.5, A.is_lt)
         tt(v("pj2"), v("pj"), v("tc512"), A.mult)
         tt(v("fo"), v("fi"), v("pj2"), A.max)
         cp(v("fou"), v("fo"))
-        yield
-
-    def slots():
-        cp(ind(v("JW"), v("fou")), v("JV"))
-        scan(v("JS"), v("JW", 0, 512), v("JW", 0, 512), -512.0, A.max, A.max)
-
-    def slots_lists():
-        to_list(v("p4", 0, 32), "JS")
-        to_list(v("p4", 32, 64), "JW")
-
-    def slots2():
-        ts(v("jt"), v("p4", 32, 64), -256.5, A.is_lt, 512.0, A.mult)
-        ts(v("JB"), v("p4", 0, 32), 768.0, A.add)
-        tt(v("jj"), v("jt"), v("p4", 0, 32), A.add)
-        ts(v("JJ"), v("jj"), 256.0, A.add)
-
-    def numbers(t):
-        act(v("NG"), ind(v("RB%d" % t, 96, 192), v("ngu")))
-        yield
-        to_list(v("p4", 96, 128), "NG")
-        yield
-        ts(v("n1"), v("p4", 96, 128), 0.5, A.is_ge)
-        yield
-        tt(v("n3"), v("n1"), v("n2"), A.mult)
-        yield
-        tt(v("n5"), v("n3"), v("n4"), A.mult)
-        yield
-        tt(v("Ci"), v("n5"), v("idx"), A.add)
-        yield
-        tt(v("Cf"), v("n5"), v("idx"), A.add)
-        yield
-        digits(v("Ci"), "dn")
-        yield
-        rows("dn")
-        yield
-        if t < R - 1:
-            act(v("NW", 512, 1024), v("p6"))
-        yield
-
-    def put_numbers(t):
-        act(v("YC"), v("p6"))
-        dma("Y", "d3", T.yc[:, 512 * t:512 * t + 512], T.YC[2:128:16, :], [v("YC")], [])
-
-    def u_fix(k, c):
-        x = v("U", 1024 * k, 1024 * k + 1024)
-        if k % 2:
-            ts(x, x, col(c), A.add)
-        else:
-            act(x, x, AF.Identity, bias=col(c))
-        return x
-
-    def next_lists():
-        to_list(v("p0", 0, 32), "NR")
-        to_list(v("p0", 32, 64), "NR", 1)
-
-    def gather(m):
-        act(v("GS"), ind(v("U", 0, S), v("HL", 32 * m, 32 * m + 32)))
-
-    def diff_of(m):
-        o = 512 * (m % 2)
-        return v("AB%d" % (m // 2 % 3), o, o + 512)
-
-    def sum_up(k):
-        bank = "p7" if k % 2 else "p2"
+        ts(v("Cb"), v("Cf"), -base, A.add)
+        split("Ch", "Cl", "Cf")
+        mm(v("p6"), v("ID"), v("JO"), True, False)
+        rows("Ch", "Cl", 2, 5)
+        if not last:
+            mm(v("p0"), v("ID"), v("Z"), True, False)
+            mm(v("p0"), v("DG"), v("ZA"), False, True)
+            act(v("PK"), v("p0"))
+        n = 0
+        for k in range(8):
+            for j in (1, 0):
+                lst = v("HL", 64 * k + 32 * j, 64 * k + 32 * j + 32)
+                if j and k in SG:
+                    act(v("GS"), ind(stones, lst))
+                    mm(v("p5"), v("ID"), v("GS"), True, False)
+                    mm(v("p5"), v("NI"), v("Z"), False, True)
+                    act(half(k % 3, j), v("p5"), AF.Abs)
+                else:
+                    df = v("DF%d" % (n % 3))
+                    n += 1
+                    tt(df, ind(stones, lst), v("Z"), A.subtract)
+                    act(half(k % 3, j), df, AF.Abs)
+            for q in range(16):
+                mm(v("p4", k, 512, 8), slid("FD", q), both(k % 3, q), q == 0, q == 15)
+        scan(v("KAB", 0, 512), v("DA"), v("p4"), 0.0, A.add, A.min)
+        scan(v("KAB", 512, 1024), v("DB"), v("p4"), 0.0, A.add, A.min)
+        ts(v("nf"), v("KAB", 15, 512, 16), thr, A.is_ge)
+        tt(v("pw"), v("nf"), v("mu"), A.mult)
+        mm(v("p1", 0, 32), v("BD"), v("pw"))
+        mm(v("p1", 32, 64), v("GE"), v("pw"))
+        ts(v("pen0"), v("pw"), 0.5, A.is_lt)
+        tt(v("pen"), v("pen0"), v("tc1024"), A.mult)
+        scan(v("cum"), v("on"), v("p1", 0, 32), 0.0, A.mult, A.add)
+        tt(v("ww"), v("p1", 32, 64), v("pen"), A.subtract)
+        tt(v("OF"), v("cum"), v("ww"), A.subtract)
+        cp(v("OFu"), v("OF"))
+        ms(v("ZS", 0, 96), 1024.0)
+        cp(ind(v("ZS"), v("OFu")), v("Z" if last else "PK"))
+        zr = v("ZR%d" % t)
+        send("az%d" % t, "lz", lender, zr, v("ZS", 0, 96))
+        tt(v("lf"), v("rc"), v("nf"), A.is_gt)
+        ts(v("hx0"), v("lf"), -8192.0, A.mult, 8191.5, A.add)
+        best(NB, "KAB", "H0", "H1", "hr", "rr", "r2", "x2s", "hx0", ("hh", "hx"))
         for q in range(16):
-            mm(v(bank, 64 * (k // 2), 64 * (k // 2) + 64), mat("FD", q), v("AB%d" % (k % 3), q, 1024, 16), q == 0, q == 15)
-
-    def take(k):
-        bank, o = "p7" if k % 2 else "p2", 64 * (k // 2)
+            mm(v("p2", 15 - q, 512 - q, -16), mat("E1", q), v("hh"))
+        ts(v("nh"), v("hx"), -8192.0, A.mult)
+        ts(v("n0"), v("hx"), -1.0, A.mult, -2048.0, A.add)
+        tt(v("nlo"), v("n0"), v("ntc"), A.max)
+        for h in (1, 0):
+            for k in (2 * h + 1, 2 * h):
+                for i in range(8):
+                    b, o, a0, a1 = 8 * k + i, 576 * k + 8 * i * (i + 1), 496 - 128 * k - 16 * i, 512 - 128 * k
+                    act(v("NE", o, o + a1 - a0), v("p2", a0, a1), AF.Abs, scale=8192.0, bias=v("nh", b, b + 1))
+                scan(v("SC", 576 * k, 576 * k + 576), v("NE", 576 * k, 576 * k + 576), v("MK"), 0.0, A.min, A.max)
+            c0, c1 = 16 * h, 16 * h + 16
+            tt(v("la", c0, c1), ind(v("SC", 1152 * h, 1152 * h + 1152), v("EN", 0, 1)), v("tc4096", c0, c1), A.subtract)
+            tt(v("lb", c0, c1), v("la", c0, c1), v("nlo", c0, c1), A.min)
+            ts(v("lou", c0, c1), v("lb", c0, c1), -1.0, A.mult)
+            for k in (2 * h + 1, 2 * h):
+                cp(ind(v("U", E, E + S + 512), v("lou", 8 * k, 8 * k + 8)), v("LV", 128 * k, 128 * k + 128))
+        if not last:
+            mm(v("p7", 128, 129), v("O16"), v("cum", 31, 32))
+            cp(v("Pi"), v("p7", 128, 129))
+            ts(v("Pj"), v("Pi"), 63, A.bitwise_and)
+            tt(col(TMP), col(TH), v("Pj"), A.add)
+            ts(col(THR + (t + 1) % 2), col(TMP), 4096.0, A.mult, -3968.0, A.add)
+        tt(v("a1"), v("hx"), v("Cf"), A.subtract)
+        ts(v("a1"), v("a1"), 2048.0, A.add)
+        tt(v("a2"), v("a1"), v("lf"), A.mult)
+        tt(v("a3"), v("OF"), v("Cb"), A.subtract)
+        ts(v("a4"), v("OF"), 95.5, A.is_lt)
+        tt(v("a5"), v("a3"), v("a4"), A.mult)
+        tt(v("dd"), v("a2"), v("a5"), A.add)
+        split("Dh", "Dl", "dd")
+        rows("Dh", "Dl", 0, 1)
+        act(v("NW"), v("p6"))
+        if t:
+            act(v("YC"), v("p6"))
+            dma("Y", "d3", T.yc[:, 512 * t - 512:512 * t], T.YC[5:128:16, :], [v("YC")], [])
+        act(v("JW", 0, 512), v("JO"), scale=0.0)
+        for k in range(NJ):
+            w = NB // NJ
+            cp(ind(v("JW"), v("fou", w * k, w * k + w)), v("NW", 16 * w * k, 16 * w * k + 16 * w))
+        ts(v("D0"), v("JW", 0, 512), 0.0, A.is_equal, col(FILL), A.mult)
+        scan(v("JS"), v("D0"), v("JW", 0, 512), 0.0, A.mult, A.add)
+        to_list(v("p7", 0, 32), "FC", "JS")
+        ts(v("Hs"), v("p7", 0, 32), -OFS, A.add)
+        ts(v("ngu"), v("p7", 0, 32), -base - OFS, A.add)
+        pc = v("p7", 0, 32)
+        if last:
+            pc = v("p6", 64, 96)
+            to_list(pc, "FC", "JS", True)
+        to_list(v("p6", 0, 32), "FO", "JS", last)
+        to_list(v("p6", 32, 64), "FJ", "JS", last)
+        cp(v("Os"), v("p6", 0, 32))
+        cp(v("Js"), v("p6", 32, 64))
+        tt(v("df"), pc, v("Os"), A.subtract)
+        ts(v("pl"), pc, base + OFS, A.is_ge)
+        tt(v("n4"), v("pl"), v("df"), A.mult)
+        act(v("FG"), ind(v("U", E, E + S + 512), v("Hs")), AF.Identity, scale=col(FSC), bias=col(FBI))
+        to_list(v("p6", 96, 128), "F0", "FG", last)
+        tt(v("w1"), v("p6", 96, 128), v("Js"), A.is_equal)
+        tt(v("w2"), v("df"), v("n4"), A.subtract)
+        tt(v("a3"), v("Os"), v("n4"), A.add)
+        tt(v("w3"), v("w1"), v("w2"), A.mult)
+        tt(v("idx1", 0, 32), v("w3"), v("a3"), A.add)
+        ts(v("ZRp"), ind(zr, v("PL", 0, NA)), M1, A.add, M1, A.subtract)
+        mm(v("p3", 0, 96), v("RU"), v("ZRp"))
+        mm(v("p3", 96, 192), v("RV"), v("ZRp"))
         for j in (0, 1):
-            act(v("KD2", 2 * k + j, 544, 17), v(bank, o + 32 * j, o + 32 * j + 32))
+            ts(v("ua", 96 * j, 96 * j + 96), v("p3", 96 * j, 96 * j + 96), col(CU + j), A.add)
+        ts(v("ub"), v("ua"), 4095, A.bitwise_and)
+        tt(v("PRa"), v("ub", 0, 96), v("ub", 96, 192), A.mult)
+        ts(v("kua"), v("ub", 0, 96), v("kmf"), A.mult)
+        ts(v("qa"), v("PRa"), 5, A.arith_shift_right)
+        tt(v("Xa"), v("kua"), v("qa"), A.add)
+        ts(v("Xb"), v("Xa"), 4095, A.bitwise_and)
+        cp(v("HA"), v("Xb"))
+        ts(v("T1a"), v("ub", 0, 96), 2048.0, A.is_ge, -4096.0, A.mult)
+        tt(v("R2", 0, 192, 2), v("T1a"), v("ub", 0, 96), A.add)
+        ts(v("R2", 1, 192, 2), v("Xb"), -2048.0, A.add)
+        for q in range(16):
+            mm(v("p0", 0, 12), slid("F15", q), v("R2", 12 * q, 12 * q + 12), q == 0, q == 15)
+        cp(v("G0", 4, 36, 6), v("p0", 0, 12, 2))
+        cp(v("G1", 4, 36, 6), v("p0", 1, 12, 2))
+        if not last:
+            ts(v("t1"), ind(zr, v("PL", 0, NA)), col(EA), A.mult, col(EG), A.add)
+            act(v("t2"), v("ZRp"), scale=col(EB))
+            tt(v("Tw", 0, E), v("t1"), v("t2"), A.add)
+        ms(v("U", 0, E), -4096.0)
+        for k in range(4):
+            z = v("z16", 384 * k, 384 * k + 384)
+            act(z, ind(v("ZRp"), v("ZL", 24 * k, 24 * k + 24)))
+            df, ab = v("DF%d" % (k % 3), 0, 384), v("AA", 384 * k, 384 * k + 384)
+            tt(df, ind(stones, v("HA", 24 * k, 24 * k + 24)), z, A.subtract)
+            act(ab, df, AF.Abs)
+            for q in range(4 * k, 4 * k + 4):
+                mm(v("p5", 0, 96), slid("FD", q), v("AA", 96 * q, 96 * q + 96), q == 0, q == 15)
+        scan(v("KE", 0, 96), v("DA", 0, 96), v("p5", 0, 96), 0.0, A.add, A.min)
+        scan(v("KE", 96, 192), v("DB", 0, 96), v("p5", 0, 96), 0.0, A.add, A.min)
+        ts(v("k6", 0, NA), v("KE", 15, 96, 16), thr, A.is_ge, -8192.0, A.mult)
+        ts(v("k7", 0, NA), v("k6", 0, NA), -0.5, A.add)
+        best(NA, "KE", "G0", "G1", "gr", "ra", "s2", "s3", "k7", ("ha", "ga1"))
+        for q in range(16):
+            mm(v("p1", 15 - q, 96 - q, -16), mat("E1", q), v("ha", 0, NA))
+        ts(v("ga2", 0, NA), v("ga1", 0, NA), 2048.0 + E, A.add)
+        tt(v("ga3", 0, NA), v("ga2", 0, NA), v("ecl", 0, NA), A.max)
+        for b in range(NA):
+            o = 8 * b * (b + 1)
+            ts(v("NE", o, o + 16 * b + 16), v("p1", 80 - 16 * b, 96), v("ga1", b, b + 1), A.not_equal, 8192.0, A.mult)
+        scan(v("SC", 0, 336), v("NE", 0, 336), v("MK", 0, 336), 0.0, A.min, A.max)
+        tt(v("ga"), ind(v("SC", 0, 1152), v("EN", 0, 1)), v("ecl"), A.add)
+        tt(v("gb", 0, NA), v("ga", 0, NA), v("ga3", 0, NA), A.min)
+        glu = v("glu", 0, NA)
+        cp(glu, v("gb", 0, NA))
+        if not last:
+            cp(v("SB"), ind(v("Tw", 0, E + S), glu))
+            send("at%d" % t, "ly", asker, v("Tw", E + S + 96 * t, E + S + 96 * t + 96), v("SB"))
+        act(v("SU"), ind(v("U", 0, E + S), glu))
+        send("au%d" % t, "lx", asker, v("UP", 96 * t, 96 * t + 96), v("SU"))
+        if not last:
+            cp(ind(v("U", 0, E + S), glu), v("L255"))
+        else:
+            for k in range(4):
+                x, y = v("U", E + 1024 * k, E + 1024 * k + 1024), v("UO", E + 1024 * k, E + 1024 * k + 1024)
+                if k == 3:
+                    ts(y, x, col(C256), A.add)
+                else:
+                    act(y, x, AF.Identity, bias=col(C256))
+            ms(v("L255"), 255.0)
+            cp(ind(v("UO"), glu), v("L255"))
+            for k in range(4):
+                y = v("UO", E + 1024 * k, E + 1024 * k + 1024)
+                dma("S" if k % 2 else "Y", "d4", T.yu[:, 1024 * k:1024 * k + 1024], y[0], [y], [], 3.0 + k)
 
-    def side(t):
-        for x in (numbers(t - 1) if t else setup_last()):
-            yield
-        for x in widths():
-            yield
+    ts(v("idx"), v("idx1", 0, 32), -OFS, A.add)
+    flags(R - 1, True)
+    tt(v("yo"), v("idx"), v("w4"), A.subtract)
+    dma("Y", "d6", T.yc[:, 512 * R - 512:512 * R], T.yo[:, :], [v("yo")], [])
+    ts(v("UQ"), v("UP"), col(C256), A.add, 0.0, A.max)
+    dma("S", "d5", T.yu[:, S:W], T.UQ[:, :], [v("UQ")], [])
+
+    seen = {}
+    for n, c in enumerate(calls):
+        c["pre"] = {}
+        for xs, isw in ((c["rs"], False), (c["ws"], True)):
+            for r in xs:
+                for (o, k, w) in seen.get(r[0], []):
+                    d = calls[k]
+                    if hit(r, o) and (w or isw or (is_bank(r[0]) and d["q"] != c["q"])):
+                        wait = 0.0 if d["q"] == c["q"] == "P" else d["late"] * (1 if w else 3) + HOP
+                        c["pre"][k] = max(c["pre"].get(k, 0.0), wait)
+        for xs, isw in ((c["rs"], False), (c["ws"] + (c["far"] or []), True)):
+            for r in xs:
+                old = seen.setdefault(r[0], [])
+                if isw:
+                    old[:] = [o for o in old if not (o[0][1] >= r[1] and o[0][2] <= r[2] and r[3] == 1)]
+                old.append((r, n, isw))
+    for c in calls:
+        c["tail"] = c["cost"] + c["late"]
+    for n in range(len(calls) - 1, -1, -1):
+        for k, wait in calls[n]["pre"].items():
+            calls[k]["tail"] = max(calls[k]["tail"], calls[k]["cost"] + wait + calls[n]["tail"])
+    busy = {q: [] for q in Q}
+    for n in sorted(range(len(calls)), key=lambda n: (calls[n]["kind"] != "F", n if calls[n]["kind"] == "F" else -calls[n]["tail"], n)):
+        c = calls[n]
+        at = max([calls[k]["at"] + calls[k]["cost"] + wait for k, wait in c["pre"].items()] + [0.0])
+        line, i = busy[c["q"]], 0
+        while i < len(line) and line[i][0] < at + c["cost"] - 1e-9:
+            at = max(at, line[i][1])
+            i += 1
+        line.insert(i, (at, at + c["cost"]))
+        c["at"] = at
+
+    count, known, snaps, rec = {}, {q: {} for q in Q}, {}, {}
+
+    def settle(q, reads, writes):
+        need = {}
+        for xs, isw in ((reads, False), (writes, True)):
+            for r in xs:
+                for (o, e, n, w) in rec.get(r[0], []):
+                    if not hit(r, o) or (e == q and q == "P") or not (w or isw or (is_bank(r[0]) and e != q)):
+                        continue
+                    need[e] = max(need.get(e, 0), count[e] if e[0] in "DL" else n)
+        for e, n in sorted(need.items(), key=lambda kv: -kv[1]):
+            if known[q].get(e, 0) < n:
+                Q[q].wait_ge(T.sem[SEM.get(e, e[1:])], n)
+                known[q][e] = n
+                for e2, n2 in snaps.get((e, n), {}).items():
+                    known[q][e2] = max(known[q].get(e2, 0), n2)
+
+    def note(e, n, reads, writes, snap):
+        snaps[(e, n)] = dict(snap)
+        for xs, isw in ((reads, False), (writes, True)):
+            for r in xs:
+                old = rec.setdefault(r[0], [])
+                if isw:
+                    old[:] = [o for o in old if not (o[0][1] >= r[1] and o[0][2] <= r[2] and r[3] == 1)]
+                old[:] = [o for o in old if not (o[0] == r and o[1] == e and o[3] == isw)]
+                old.append((r, e, n, isw))
 
     for t in range(R):
-        last = t == R - 1
-        lender, asker = T.cores[(rank + 1 + t) % 8], T.cores[(rank - 1 - t) % 8]
-        cp(v("CL"), v("p0", 0, 64))
-        if t == 0:
-            cp(v("idx"), v("p0", 0, 32))
+        asker, lender = T.cores[(rank - 1 - t) % 8], T.cores[(rank + 1 + t) % 8]
+        for sem, src, ws in (("az%d" % t, asker, v("ZR%d" % t)), ("at%d" % t, lender, v("Tw", E + S + 96 * t, E + S + 96 * t + 96)), ("au%d" % t, lender, v("UP", 96 * t, 96 * t + 96))):
+            if sem in SEMAPHORES:
+                count["A" + sem] = len(topo.engines(src, core)[:8])
+                note("A" + sem, count["A" + sem], [], ws[1], {})
+    for n in sorted(range(len(calls)), key=lambda n: (calls[n]["at"], n)):
+        c = calls[n]
+        q = c["q"]
+        settle(q, c["rs"], c["ws"])
+        if c["kind"] == "R":
+            e, step = "L" + c["sem"][0], c["sem"][1]
+            c["f"]()
         else:
-            tt(v("xt"), v("RB%d" % (t - 1), 96, 192), v("TS", 0, 96), A.mult)
-            tt(v("Tw", S + 96 * t - 96, S + 96 * t), v("xt"), v("RB%d" % (t - 1), 0, 96), A.add)
-        act(v("ZA"), ind(v("Tw", 0, W), v("CL", 0, 32)), AF.Identity, scale=col(0), bias=col(1))
-        todo = side(t)
-        if t:
-            next(todo, None)
-        tt(v("Z"), ind(v("Tw", 0, W), v("CL", 32, 64)), v("ZA"), A.min)
-        if t == 0:
-            setup_hash()
-            for k in range(4):
-                u_fix(k, 2)
-            setup_fill()
-        hash_sums("Z", NB)
-        if t:
-            next(todo, None)
-        if t:
-            weave(hash_uv(NB), (next(todo, None) for k in range(5)), 4)
-        else:
-            for x in hash_uv(NB):
-                pass
-        hash_lists(NB, "p1", 0, 8)
-        hash_lists(NB, "p3", 8, 16)
-        if t == 0:
-            setup_late()
-        else:
-            next(todo, None)
-        for x in lists("p1", 0, 0, 128):
-            pass
-        more = [lists("p3" if k > 1 else "p1", 128 * (k % 2), 128 * k, 128) for k in (1, 2, 3)]
-        gather(SG[0])
-        ready = []
-        for i, m in enumerate([m for m in range(16) if m not in SG]):
-            df = "DF%d" % (i % 3)
-            tt(v(df), ind(v("U", 0, S), v("HL", 32 * m, 32 * m + 32)), v("Z"), A.subtract)
-            act(diff_of(m), v(df), AF.Abs)
-            for k in ready:
-                take(k)
-            ready = []
-            done = [m // 2] if m % 2 else []
-            if m + 1 in SG:
-                mm(v("p4"), v("ID"), v("GS"), True, False)
-                mm(v("p4"), v("NI"), v("Z"), False, True)
-                act(diff_of(m + 1), v("p4"), AF.Abs)
-                done = [m // 2]
-            if i < 9:
-                next(more[i // 3])
-            if i == 6:
-                gather(SG[1])
-            if i >= 1:
-                next(todo, None)
-            for k in done:
-                sum_up(k)
-                ready.append(k)
-        for x in todo:
-            pass
-        for k in ready:
-            take(k)
-        slots()
-        scan(v("KAB", 0, 544), v("DA"), v("KD2"), 0.0, A.add, A.min)
-        scan(v("KAB", 544, 1088), v("DB"), v("KD2"), 0.0, A.add, A.min)
-        weave(best(NB, v("KAB", 16, 1088, 17)), poor())
-        tt(v("hh"), v("hx0"), v("Hh"), A.add)
-        tt(v("hx"), v("hx0"), v("Hh"), A.add)
-        for q in range(16):
-            mm(v("p1", q, 512, 16), mat("E1", q), v("hh"))
-        cp(ind(v("ZS"), v("OFu")), v("Z"))
-        send("az%d" % t, "lz", lender, T["ZR%d" % t][:, :], T.ZS[:, 0:96], [v("ZS", 0, 96)])
-        mm(v("p7"), v("ZM"), v("Z"), True, False)
-        ts(v("hc"), v("hx"), 2048.0, A.add)
-        cp(v("wm", 0, NS), v("lf", 0, NS))
-        tt(v("hm"), v("Hh"), v("tc4096"), A.subtract)
-        tt(v("a1"), v("Hh"), v("Cf"), A.subtract)
-        if not last:
-            act(v("TC"), ind(v("Tw", 0, W), v("CL", 0, 32)))
-        if t:
-            put_numbers(t - 1)
-        ts(v("HR"), v("p1"), 2048.0, A.add)
-        for b in range(NS, NB):
-            e = 512 * b
-            ts(v("EQ", e - 16 * b, e + 16), v("HR", 0, 16 * b + 16), v("hc", b, b + 1), A.is_equal)
-            add_up(v("LJ", 0, 16 * b), v("EQ", e - 16 * b, e), v("la", b, b + 1))
-        for b in range(NS):
-            e, w = 512 * b, 16 * NS - 16 * b
-            ts(v("EQ", e, e + w), v("HR", 16 * b, 16 * NS), v("hc", b, b + 1), A.is_equal)
-            if b < NS - 1:
-                mm(v("p7", 16 * b + 16, 16 * NS), v("BD"), v("EQ", e + 16, e + w), False, False)
-        for q in range(1, 16):
-            mm(v("p7", q, 512, 16), mat("LQ", q), v("EQ", q, 15872 + q + 1, 512), False, q == 15)
-        act(v("LS"), v("p7"))
-        zr = "ZR%d" % t
-        for k in range(4):
-            act(v("z4", 96 * k, 96 * k + 96), v(zr))
-        hash_sums(zr, NA)
-        to_list(v("p5", 192, 224), "LS")
-        if not last:
-            mm(v("p5", 224, 225), v("O16"), v("cum", 31, 32))
-        slots_lists()
-        if not last:
-            cp(ind(v("TS"), v("OFu")), v("TC"))
-        ts(v("wn", NS, NB), v("la", NS, NB), 0.5, A.is_lt)
-        tt(v("wm", NS, NB), v("wn", NS, NB), v("lf", NS, NB), A.mult)
-        weave(hash_uv(NA), laid(), 4)
-        hash_lists(NA, "p1", 0, 16)
-        cp(ind(v("U", 0, ZC), v("lou")), v("L255"))
-        if not last:
-            cp(v("Pi"), v("p5", 224, 225))
-        for x in lists("p1", 0, 0, 96):
-            pass
-        for k in range(4):
-            df, ab, o = "DF%d" % (k % 3), "AB%d" % (k // 2), 384 * (k % 2)
-            tt(v(df, 0, 384), ind(v("U", 0, S), v("HL", 24 * k, 24 * k + 24)), v("z4"), A.subtract)
-            act(v(ab, o, o + 384), v(df, 0, 384), AF.Abs)
-            if k % 2:
-                for q in range(16):
-                    mm(v("p2", 48 * (k // 2), 48 * (k // 2) + 48), mat("FD", q), v(ab, q, 768, 16), q == 0, q == 15)
-        for b in range(NA):
-            act(v("KE", 17 * b, 17 * b + 16), v("p2", b, 96, NA))
-        tt(v("a2"), v("a1"), v("ld"), A.mult)
-        ts(v("a3"), v("OF"), 95.5, A.is_lt)
-        ts(v("a4"), v("OF"), float(S + 96 * t), A.add)
-        tt(v("a5"), v("a4"), v("Cf"), A.subtract)
-        tt(v("a7"), v("a2"), v("Cf"), A.add)
-        tt(v("a6"), v("a5"), v("a3"), A.mult)
-        tt(v("Ai"), v("a7"), v("a6"), A.add)
-        digits(v("Ai"))
-        rows("dh")
-        slots2()
-        act(v("NW", 0, 512), v("p6"))
-        act(v("NR", 0, 512), ind(v("NW"), v("JJ")))
-        scan(v("KAB", 0, 102), v("DA", 0, 102), v("KE"), 0.0, A.add, A.min)
-        scan(v("KAB", 102, 204), v("DB", 0, 102), v("KE"), 0.0, A.add, A.min)
-        key = v("KAB", 16, 102, 17)
-
-        def fits():
-            ts(v("k6", 0, NA), key, col(10), A.is_ge, 8192.0, A.mult)
-            yield
-            ts(v("gt", 0, NA), key, col(10), A.is_lt)
-            yield
-        weave(best(NA, v("KAB", 16, 204, 17)), fits(), 1)
-        ts(v("k7", 0, NA), v("Hh", 0, NA), -2048.0, A.add)
-        tt(v("ha"), v("k6", 0, NA), v("k7", 0, NA), A.add)
-        for q in range(16):
-            mm(v("p1", q, 96, 16), mat("E1", q), v("ha"))
-        next_lists()
-        ts(v("gh", 0, NA), v("Hh", 0, NA), float(-ZC), A.add)
-        tt(v("gn", 0, NA), v("Hh", 0, NA), v("tc4096", 0, NA), A.subtract)
-        tt(v("Hd"), v("p1", 0, 96), v("msk"), A.add)
-        for b in range(NA):
-            if b:
-                ts(v("EA", 96 * b, 96 * b + 16 * b), v("p1", 0, 16 * b), v("k7", b, b + 1), A.is_equal)
-            ts(v("EA", 112 * b, 112 * b + 16), v("Hd", 16 * b, 16 * b + 16), v("k7", b, b + 1), A.is_equal)
-            add_up(v("Hj", 0, 16 * b + 16), v("EA", 96 * b, 112 * b + 16), v("la", 32 + b, 33 + b))
-        ts(v("gm0", 0, NA), v("la", 32, 32 + NA), 0.5, A.is_lt)
-        tt(v("gm", 0, NA), v("gm0", 0, NA), v("gt", 0, NA), A.mult)
-        tt(v("gl", 0, NA), v("gm", 0, NA), v("gh", 0, NA), A.mult)
-        ts(v("glu", 0, NA), v("gl", 0, NA), float(ZC), A.add)
-        act(v("SB", 96, 192), ind(v("FL"), v("glu", 0, NA)))
-        cp(v("SB", 0, 96), ind(v("Tw"), v("glu", 0, NA)))
-        send("ar%d" % t, "ly", asker, T["RB%d" % t][:, :], T.SB[:, :], [v("SB")])
-        act(v("SU"), ind(v("U"), v("glu", 0, NA)))
-        send("au%d" % t, "lx", asker, T.UP[:, 96 * t:96 * t + 96], T.SU[:, :], [v("SU")])
-        act(v("NB2"), ind(v("NW"), v("JB")))
-        if not last:
-            act(v("JW"), v("JP"))
-        to_list(v("p4", 64, 96), "NB2")
-        tt(v("go", 0, NA), v("gn", 0, NA), v("gm", 0, NA), A.mult)
-        tt(v("gp", 0, NA), v("go", 0, NA), v("tc4096", 0, NA), A.add)
-        cp(v("sou", 0, NA), v("gp", 0, NA))
-        cp(ind(v("U", 0, ZC), v("sou", 0, NA)), v("L255", 0, 96))
-        if not last:
-            ts(v("Pj"), v("Pi"), 63, A.bitwise_and)
-            tt(col(16), col(9), v("Pj"), A.add)
-            ts(col(10), col(16), 4081.0, A.min, 4096.0, A.mult)
-            ms(v("ZS", 0, 96), 1024.0)
-        base = float(S + 96 * t)
-        cp(v("idx"), v("p0", 0, 32))
-        ts(v("ngu"), v("idx"), -base, A.add, 0.0, A.max)
-        ts(v("n2"), v("idx"), base, A.is_ge)
-        if last:
-            for k in range(4):
-                x = u_fix(k, 3)
-                dma("Y", "d4", T.yu[:, 1024 * k:1024 * k + 1024], x[0], [x], [])
-        tt(v("n4"), v("p4", 64, 96), v("idx"), A.subtract)
-
-    for x in numbers(R - 1):
-        pass
-    put_numbers(R - 1)
-    ts(v("UP"), v("UP"), col(3), A.add)
-    dma("Y", "d5", T.yu[:, S:W], T.UP[:, :], [v("UP")], [])
+            e, step = (q, 1) if c["kind"] == "C" else ("D" + c["sem"], 16)
+            c["f"]().then_inc(T.sem[SEM.get(e, e[1:])], step)
+        count[e] = count.get(e, 0) + step
+        note(e, count[e], c["rs"], c["ws"], known[q])
     for e, n in sorted(count.items()):
         g.wait_ge(T.sem[SEM.get(e, e[1:])], n)

@@ -1,9 +1,13 @@
 from concourse.mybir import AluOpType, ActivationFunctionType
 
-NB, NA, S, W, R, E = 32, 6, 4096, 4384, 3, 96
-SG = (1, 4, 6)
-NJ = 2
-OFS = 193.0
+NB, NA, S, W, R, E = 32, 6, 4096, 4384, 3, 128
+SG = (1, 3, 5)
+NAB = 4
+ZV = 128
+NZ = 1
+SA = ()
+N1 = 4
+PASSES = 2
 F, B, I, H, U16 = "float32", "bfloat16", "int32", "float16", "uint16"
 M1, M128, M256, M4096 = 1.5 * 2 ** 23, 1.5 * 2 ** 30, 1.5 * 2 ** 31, 1.5 * 2 ** 35
 SCRATCH, PACK, PACKED = {}, {}, {}
@@ -11,20 +15,21 @@ SEMAPHORES = ["sv", "ss", "sp", "sg", "d0", "d1", "d2", "d3", "d4", "d5", "d6", 
 for _t in range(R):
     SEMAPHORES += ["az%d" % _t, "au%d" % _t] + (["at%d" % _t] if _t < R - 1 else [])
     SCRATCH["ZR%d" % _t] = ("sbuf", [128, 96], F)
-    SCRATCH["AB%d" % _t] = ("sbuf", [128, NB, 2, 16], B)
+for _n in range(NAB):
+    SCRATCH["AB%d" % _n] = ("sbuf", [128, NB, 2, 16], B)
 for _n in range(8):
     SCRATCH["p%d" % _n] = ("psum", [128, 512], F)
 for _w, _d, _s in (
-        (E + S + 512, F, "U"), (E + W, B, "Tw"), (E + S, B, "UO"), (288, B, "UP UQ"), (512, I, "C8 X X2"), (512, H, "c16"), (2048, B, "E1"), (2064, B, "Y"),
-        (2048, H, "KD"), (2048, F, "ZS"), (1024, F, "KAB"), (512, F, "ior YC LV PK DA DB HF"), (2304, B, "NE SC"), (576, B, "MK"), (1024, B, "JW"),
-        (512, B, "JO ZA Z GS NW D0 JS FG NG DF0 DF1 DF2"), (1536, B, "z16 AA"), (512, U16, "HL"), (192, H, "H0 H1 R2"), (192, F, "hr KE"), (192, I, "ua ub"),
-        (144, F, "io144"), (144, B, "B0 B8 FD FC FO FJ F0 F15"), (144, H, "WU WV"), (128, H, "RU RV"), (128, B, "BD BY ID NI DG GE"),
-        (128, F, "io8 iox BF SH1 SH2 O16 rep x1 x2"), (96, F, "t1 t2 T1a io96"), (96, I, "PRa kua qa Xa Xb"), (96, U16, "HA ZL"), (96, B, "ZRp SB SU L255"),
+        (E + W, F, "U"), (E + W, B, "Tw"), (E + S, B, "UO"), (288, B, "UP UQ"), (512, I, "C8 X X2"), (512, H, "c16"), (2048, B, "E1"), (2064, B, "Y"),
+        (2048, H, "KD"), (2048, F, "ZS"), (1024, F, "KAB"), (512, F, "ior YC LV PK DA DB JV"), (2304, B, "NE SC"), (576, B, "MK"), (1024, F, "JW"),
+        (512, B, "DM ZA Z GS NW NR FG NG DF0 DF1 DF2"), (512, H, "JS"), (1536, B, "z16 AA"), (512, U16, "HL"), (192, H, "H0 H1 R2"), (192, F, "hr KE"), (192, I, "ua ub"),
+        (144, F, "io144"), (144, B, "B0 B8 FD FC FO FJ F0 F15"), (144, H, "WU WV"), (128, H, "RU RV"), (128, B, "BD BY ID NI DG GE ZM"),
+        (128, F, "io8 iox BF SH1 SH2 O16 rep x1 x2"), (96, F, "t1 t2 T1a io96"), (96, I, "PRa kua qa Xa Xb"), (96, U16, "HA ZL"), (96, B, "ZRp zn SB SU L255"), (96, H, "RX"),
         (2, I, "pi pq hwi"), (1, I, "kmi thi Pi Pj ei"), (1, F, "pf qf gf kmf thf e1 e2 e3 e4"), (2, F, "hwf hwg hws hwm"), (2, U16, "EN"),
-        (16, F, "io16 qm kq KM KS0 KS dA dB dC ecl ga"), (16, B, "mq"), (16, I, "ki kj ka kb"), (64, F, "rr"), (36, H, "G0 G1"), (36, F, "gr"), (33, F, "idx1"),
-        (40, F, "col"), (32, F, "tc tcq tc512 tc1024 tc4096 ntc W40 W4 on idx T1 nf pen0 pen cum ww OF lf hx0 r2 x2s hx nh n0 nlo la lb Cf Cb cw ee ec mu rc pj pj2 fo "
-                                "a1 a2 a3 a4 a5 dd Os Js df pl n4 w1 w2 w3 w4 yo"),
-        (32, I, "PR qi f3 fi nx Ci"), (64, I, "uva uv"), (32, H, "qh hh"), (8, H, "ha"), (32, B, "pw wv Dh Dl Ch Cl"), (32, U16, "OFu lou fou ngu Hs"),
+        (16, F, "io16 qm qr kq KM KS0 KS dA dB dC ga gm mq"), (16, I, "ki kj ka kb"), (64, F, "rr"), (36, H, "G0 G1"), (36, F, "gr"), (33, F, "idx1"),
+        (40, F, "col"), (32, F, "tc tcq tc512 tc1024 tcd W40 W4 on idx T1 nf pen0 pen cum ww OF lf hx0 r2 x2s hx nh n0 nlo la lb Cf Cb cw ee ec mu rc pj pj2 fo "
+                                "a1 a2 a3 a4 a5 dd Os Js d0 df fs jt jf pl n4 w1 w2 w3 w4 yo"),
+        (32, I, "PR qi f3 fi nx Ci"), (64, I, "uva uv"), (32, H, "qh hh"), (8, H, "ha"), (32, B, "pw wv Dh Dl Ch Cl"), (32, U16, "OFu lou fou ngu Hs JJ"),
         (8, U16, "glu PL"), (64, U16, "CL"), (8, I, "pd"), (12, F, "ra"), (8, F, "k6 k7 s2 s3 ga1 ga2 ga3 gb pp")):
     for _n in _s.split():
         if _w <= 64 and _n not in ("hwi", "kmi", "thi", "yo"):
@@ -37,6 +42,7 @@ for _k, _w in PACKED.items():
     SCRATCH[_k] = ("sbuf", [128, _w], _k[2:])
 
 CYC, HOP, FAR = 0.83e-3, 0.17, 3.0
+ORDER = {}
 
 
 def rank_program(g, core, T, topo):
@@ -71,10 +77,20 @@ def rank_program(g, core, T, topo):
             return False
         return not (a[3] == b[3] and a[3] > 1 and (a[1] - b[1]) % a[3])
 
-    def add(q, f, reads, writes, cost, kind="C", sem=None, late=0.0, far=None):
+    behind = []
+
+    def add(q, f, reads, writes, cost, kind="C", sem=None, late=0.0, far=None, join=False):
         rs = [r for x in reads if isinstance(x, tuple) for r in x[1]]
         rs += [r for x in list(reads) + list(writes) if isinstance(x, tuple) and x[4] for r in x[4]]
-        calls.append(dict(q=q, f=f, rs=rs, ws=[r for x in writes for r in x[1]], cost=cost, kind=kind, sem=sem, late=late, far=far))
+        ws = [r for x in writes for r in x[1]]
+        if join:
+            c = calls[-1]
+            c["parts"].append((f, rs, ws))
+            c["rs"] += [r for r in rs if r not in c["rs"]]
+            c["cost"] += cost
+            return
+        calls.append(dict(q=q, parts=[(f, rs, ws)], rs=list(rs) + [r for x in behind for r in x[1]], ws=ws, cost=cost, kind=kind, sem=sem, late=late, far=far))
+        del behind[:]
 
     def _(x):
         return x[0] if isinstance(x, tuple) else x
@@ -116,8 +132,8 @@ def rank_program(g, core, T, topo):
             kw["bias"] = _(bias)
         op("S", lambda: g.scalar.activation(_(o), _(i), func, **kw), o, [i, scale, bias], 1)
 
-    def mm(o, l, r, start=True, stop=True):
-        add("P", lambda: g.tensor.matmul(_(o), _(l), _(r), start, stop), [l, r], [o], (1 if r[3] else 4) * max(64, r[2]) * CYC)
+    def mm(o, l, r, start=True, stop=True, join=False):
+        add("P", lambda: g.tensor.matmul(_(o), _(l), _(r), start, stop), [l, r], [o], (1 if r[3] else 4) * max(64, r[2]) * CYC, join=join)
 
     def iota(o, pattern, base, cm, flag=True):
         add("G", lambda: g.iota(_(o), pattern, base, cm, allow_small_or_imprecise_dtypes=True) if flag else g.iota(_(o), pattern, base, cm), [], [o], 0.13 + 2 * o[2] * CYC)
@@ -147,7 +163,7 @@ def rank_program(g, core, T, topo):
 
     def to_list(ps, wt, row, dense=False):
         for q in range(16):
-            mm(ps, slid(wt, q), v(row, 32 * q, 32 * q + 32) if dense else v(row, q, 512, 16), q == 0, q == 15)
+            mm(ps, slid(wt, q), v(row, 32 * q, 32 * q + 32) if dense else v(row, q, 512, 16), q == 0, q == 15, q > 0)
 
     P8 = slice(0, 8)
     LO, HI, C256, CN256, LAID, ZSC, ZBI, CU, CV, TH = 0, 1, 2, 3, 4, 5, 6, 7, 8, 9
@@ -198,9 +214,10 @@ def rank_program(g, core, T, topo):
     ts(v("B8", p=P8), v("io144", p=P8), v("e1", p=P8), A.is_equal)
     ts(v("c16", p=P8), v("C8", p=P8), -2048.0, A.add)
     for q in range(16):
-        mm(v("p7", 0, 32), slid("B8", q, P8), v("c16", q, 512, 16, P8), q == 0, q == 15)
-    ms(v("idx1", 32, 33), OFS)
-    ts(v("idx1", 0, 32), v("p7", 0, 32), 2048.0 + OFS, A.add)
+        mm(v("p7", 0, 32), slid("B8", q, P8), v("c16", q, 512, 16, P8), q == 0, q == 15, q > 0)
+    ms(v("idx1", 32, 33), 0.0)
+    idx = v("idx1", 0, 32)
+    ts(idx, v("p7", 0, 32), 2048.0, A.add)
     ts(v("e2"), v("pf"), -1.0, A.add)
     ts(v("e3"), v("qf"), 0.5, A.is_gt)
     ts(v("SH1"), io128, v("e2"), A.is_equal, v("e3"), A.mult)
@@ -227,7 +244,8 @@ def rank_program(g, core, T, topo):
     tt(col(FILL), qm(2), qm(8), A.add)
     tt(col(TMP), qm(0), qm(1), A.add)
     tt(col(WC), col(TMP), col(FILL), A.add)
-    for name, wt in (("FC", col(WC)), ("FO", col(FILL)), ("FJ", qm(6)), ("F0", qm(0)), ("F15", qm(15))):
+    ts(col(TMP + 20), qm(1), 4.0, A.mult, qm(0), A.add)
+    for name, wt in (("FC", col(WC)), ("FO", col(FILL)), ("FJ", col(TMP + 20)), ("F0", qm(0)), ("F15", qm(15))):
         act(v(name), v("B0"), scale=wt)
     ts(v("ki"), v("KM"), -1.0, A.mult, v("KM", 15, 16), A.add)
     ts(v("kj"), v("ki"), 4095, A.bitwise_and)
@@ -255,9 +273,10 @@ def rank_program(g, core, T, topo):
     ms(v("on"), 1.0)
     ms(v("O16"), 0.0625)
     ts(v("tcq"), v("tc"), v("qf"), A.add)
-    for n in (512, 1024, 4096):
+    for n in (512, 1024):
         ts(v("tc%d" % n), v("tcq"), float(n), A.add)
-    ts(v("ntc"), v("tc4096"), -1.0, A.mult)
+    for k in range(4):
+        cp(v("tcd", 8 * k, 8 * k + 8), v("tcq", 0, 8))
     ts(v("W40"), v("tcq"), 510.0, A.is_equal, 5112.0, A.mult)
     ts(v("W4"), v("W40"), 4.0, A.add)
     ts(v("x1"), v("iox"), 0.0, A.is_equal)
@@ -275,18 +294,22 @@ def rank_program(g, core, T, topo):
     act(v("LV"), v("ior"), AF.Identity, scale=col(LSC), bias=col(LBI))
     ts(col(FSC), qm(0), 2.0 ** 24, A.mult)
     ts(col(FBI), qm(0), 2.0 ** 24 - 256.0, A.mult)
-    ts(col(TMP + 20), qm(2), 128.0, A.mult)
-    ts(col(JBI), qm(8), 65.0, A.mult, col(TMP + 20), A.add)
-    act(v("JO"), v("ior"), AF.Identity, scale=qm(6), bias=col(JBI))
+    ts(col(JBI), qm(0), 256.0, A.mult, 1024.0, A.add)
+    act(v("JV"), v("ior"), AF.Identity, scale=qm(0), bias=col(JBI))
+    act(v("DM"), v("ior"), AF.Identity, scale=0.0, bias=qm(0))
+    ms(v("ZM"), 0.0)
     act(v("L255"), v("ior", 0, 96), AF.Identity, scale=0.0, bias=col(LAID))
     ts(col(EA), col(HI), 1024.0, A.mult)
     tt(col(EG), col(C256), col(HI), A.subtract)
     tt(col(EB), col(LO), col(EA), A.subtract)
-    ms(v("MK"), 0.0)
     ts(v("ga"), v("io16"), v("qf"), A.add)
     ts(v("mq"), v("ga"), 15.5, A.is_lt, 16384.0, A.mult)
+    ts(v("qr"), v("ga"), 15.0, A.is_equal)
     for i in range(8):
-        act(v("MK", 8 * i * (i + 1), 8 * i * (i + 1) + 16), v("mq"))
+        o = 8 * i * (i + 1)
+        act(v("MK", o, o + 16), v("mq"), AF.Identity, bias=v("tcq", i, i + 1))
+        if i:
+            act(v("MK", o + 16, o + 16 * i + 16), v("ior", 0, 16 * i), AF.Identity, scale=0.0, bias=v("tcq", i, i + 1))
     ts(v("ei"), v("pq", 1, 2), 7, A.bitwise_and)
     ts(v("e2"), v("ei"), 8.0, A.mult, 8.0, A.add)
     ts(v("e3"), v("ei"), 2.0, A.add, v("e2"), A.mult)
@@ -298,9 +321,7 @@ def rank_program(g, core, T, topo):
     tt(v("s3", 0, NA), v("s2", 0, NA), v("pp", 0, NA), A.add)
     cp(v("PL", 0, NA), v("s3", 0, NA))
     cp(v("ZL"), v("io144", 16, 112))
-    ts(v("e1"), v("qf"), 6.0, A.mult)
-    ts(v("ecl"), v("io16"), v("e1"), A.add)
-    ms(v("U", E + S, E + S + 512), 0.0)
+    ms(v("U", E + S, E + W), 0.0)
     for k in range(4):
         x, y = v("U", E + 1024 * k, E + 1024 * k + 1024), v("UO", E + 1024 * k, E + 1024 * k + 1024)
         if k == 3:
@@ -325,27 +346,35 @@ def rank_program(g, core, T, topo):
     def rows(hi, lo, sh, sl):
         for name, shift in ((hi, sh), (lo, sl)):
             for q in range(16):
-                mm(v("p6", q, 512, 16), mat("Y", q, shift - 16), v(name), False, name == "Dl" and q == 15)
+                mm(v("p6", q, 512, 16), mat("Y", q, shift - 16), v(name), False, name == "Dl" and q == 15, q % 8 > 0)
 
     def flags(t, dense):
         act(v("NG"), ind(v("UP", 96 * t, 96 * t + 96), v("ngu")), AF.Relu, scale=-1.0 / 2048.0, bias=col(TMP + 21))
         to_list(v("p7", 0, 32), "F0", "NG", dense)
         tt(v("w4"), v("p7", 0, 32), v("n4"), A.mult)
     ms(col(TMP + 21), -1.0)
+    ms(col(TMP + 22), -4096.0)
+    ms(v("gm"), 0.0)
+    ms(v("Tw", 96, E), 0.0)
 
     for t in range(R):
         last = t == R - 1
         lender, asker = T.cores[(rank + 1 + t) % 8], T.cores[(rank - 1 - t) % 8]
         base, thr = float(S + 96 * t), col(THR + t % 2)
         stones = v("U", E, E + S)
-        ts(v("CL", 0, 32), v("idx1", 0, 32), -OFS, A.add)
-        mm(v("p7", 32, 64), v("SH1"), v("idx1", 0, 32), True, False)
-        mm(v("p7", 32, 64), v("SH2"), v("idx1", 1, 33), False, True)
-        ts(v("CL", 32, 64), v("p7", 32, 64), -OFS, A.add)
-        ts(v("idx"), v("idx1", 0, 32), -OFS, A.add)
+        cp(v("CL", 0, 32), idx)
+        mm(v("p7", 32, 64), v("SH1"), idx, True, False)
+        mm(v("p7", 32, 64), v("SH2"), v("idx1", 1, 33), False, True, True)
+        cp(v("CL", 32, 64), v("p7", 32, 64))
         tops = v("Tw", E, E + S + 96 * t)
-        act(v("ZA"), ind(tops, v("CL", 0, 32)), AF.Identity, scale=col(ZSC), bias=col(ZBI))
-        tt(v("Z"), ind(tops, v("CL", 32, 64)), v("ZA"), A.min)
+        cuts = (0, (512 - ZV) // 32 * 16, 512 - ZV, 512)
+        for a, b in zip(cuts, cuts[1:]):
+            if b == 512:
+                ts(v("ZA", a, b), ind(tops, v("CL", a // 16, b // 16)), col(ZSC), A.mult, col(ZBI), A.add)
+            else:
+                act(v("ZA", a, b), ind(tops, v("CL", a // 16, b // 16)), AF.Identity, scale=col(ZSC), bias=col(ZBI))
+        for a, b in ((0, cuts[1]), (cuts[1], 512)):
+            tt(v("Z", a, b), ind(tops, v("CL", 32 + a // 16, 32 + b // 16)), v("ZA", a, b), A.min)
         for j, wt in ((0, "WU"), (1, "WV")):
             to_list(v("p%d" % j, 0, 32), wt, "Z")
             ts(v("uva", 32 * j, 32 * j + 32), v("p%d" % j, 0, 32), col(CU + j), A.add)
@@ -356,12 +385,12 @@ def rank_program(g, core, T, topo):
         tt(v("PR"), v("uv", 0, 32), v("uv", 32, 64), A.mult)
         ts(v("qi"), v("PR"), 5, A.arith_shift_right, 4095, A.bitwise_and)
         ts(v("qh"), v("qi"), -2048.0, A.add)
-        for lo, hi, bank in ((0, 2, "p2"), (2, 8, "p3"), (8, 16, "p2")):
+        for lo, hi, bank in ((0, N1, "p2"), (N1, 16, "p3")):
             for i in range(lo, hi):
                 o = v(bank, 32 * i, 32 * i + 32)
-                mm(o, mat("KD", i // 2 + 8 * (i % 2)), uh, True, lo == 0)
+                mm(o, mat("KD", i // 2 + 8 * (i % 2)), uh, True, lo == 0, i > lo)
                 if lo:
-                    mm(o, v("ID"), v("qh"), False, True)
+                    mm(o, v("ID"), v("qh"), False, True, True)
             if lo == 0:
                 for i in range(lo, hi):
                     tt(v("X", 32 * i, 32 * i + 32), v(bank, 32 * i, 32 * i + 32), v("qi"), A.add)
@@ -372,11 +401,11 @@ def rank_program(g, core, T, topo):
         ts(v("H1", 4, 6 * NB, 6), v("X2", 480, 512), -2048.0, A.add)
         if t:
             flags(t - 1, False)
-            tt(v("Cf"), v("idx"), v("w4"), A.subtract)
-            tt(v("Ci"), v("idx"), v("w4"), A.subtract)
+            tt(v("Cf"), idx, v("w4"), A.subtract)
+            tt(v("Ci"), idx, v("w4"), A.subtract)
         else:
-            cp(v("Cf"), v("idx"))
-            cp(v("Ci"), v("idx"))
+            cp(v("Cf"), idx)
+            cp(v("Ci"), idx)
         ts(v("f3"), v("Ci"), 3, A.bitwise_and)
         tt(v("wv"), v("f3"), v("W4"), A.add)
         mm(v("p7", 64, 96), v("BD"), v("wv"))
@@ -392,10 +421,21 @@ def rank_program(g, core, T, topo):
         tt(v("pj2"), v("pj"), v("tc512"), A.mult)
         tt(v("fo"), v("fi"), v("pj2"), A.max)
         cp(v("fou"), v("fo"))
+        act(v("JW", 0, 512), v("ior"), scale=0.0)
+        act(ind(v("JW"), v("fou")), v("JV"), AF.Silu)
+        scan(v("JS"), v("DM"), v("JW", 0, 512), 0.0, A.mult, A.max)
+        for dense in range(1 + last):
+            pj = v("p7", 160, 192)
+            to_list(pj, "FJ", "JS", dense)
+            ts(v("jt"), pj, 4096.0, A.is_ge, -4096.0, A.mult)
+            tt(v("jf"), v("jt"), pj, A.add)
+            if not dense:
+                ts(v("JJ"), v("jf"), -1024.0, A.add)
+            if dense == last:
+                ts(v("fs"), pj, 4096.0, A.is_ge)
+                ts(v("Js"), v("jf"), -1280.0, A.add)
         ts(v("Cb"), v("Cf"), -base, A.add)
         split("Ch", "Cl", "Cf")
-        mm(v("p6"), v("ID"), v("JO"), True, False)
-        rows("Ch", "Cl", 2, 5)
         if not last:
             mm(v("p0"), v("ID"), v("Z"), True, False)
             mm(v("p0"), v("DG"), v("ZA"), False, True)
@@ -408,16 +448,19 @@ def rank_program(g, core, T, topo):
                     act(v("GS"), ind(stones, lst))
                     mm(v("p5"), v("ID"), v("GS"), True, False)
                     mm(v("p5"), v("NI"), v("Z"), False, True)
-                    act(half(k % 3, j), v("p5"), AF.Abs)
+                    act(half(k % NAB, j), v("p5"), AF.Abs)
                 else:
                     df = v("DF%d" % (n % 3))
                     n += 1
                     tt(df, ind(stones, lst), v("Z"), A.subtract)
-                    act(half(k % 3, j), df, AF.Abs)
+                    act(half(k % NAB, j), df, AF.Abs)
             for q in range(16):
-                mm(v("p4", k, 512, 8), slid("FD", q), both(k % 3, q), q == 0, q == 15)
+                mm(v("p4", k, 512, 8), slid("FD", q), both(k % NAB, q), q == 0, q == 15, q > 0)
         scan(v("KAB", 0, 512), v("DA"), v("p4"), 0.0, A.add, A.min)
         scan(v("KAB", 512, 1024), v("DB"), v("p4"), 0.0, A.add, A.min)
+        behind.append(v("p4"))
+        mm(v("p6"), v("ZM"), v("Z"), True, False)
+        rows("Ch", "Cl", 2, 5)
         ts(v("nf"), v("KAB", 15, 512, 16), thr, A.is_ge)
         tt(v("pw"), v("nf"), v("mu"), A.mult)
         mm(v("p1", 0, 32), v("BD"), v("pw"))
@@ -428,18 +471,22 @@ def rank_program(g, core, T, topo):
         tt(v("ww"), v("p1", 32, 64), v("pen"), A.subtract)
         tt(v("OF"), v("cum"), v("ww"), A.subtract)
         cp(v("OFu"), v("OF"))
-        ms(v("ZS", 0, 96), 1024.0)
-        cp(ind(v("ZS"), v("OFu")), v("Z" if last else "PK"))
-        zr = v("ZR%d" % t)
-        send("az%d" % t, "lz", lender, zr, v("ZS", 0, 96))
         tt(v("lf"), v("rc"), v("nf"), A.is_gt)
-        ts(v("hx0"), v("lf"), -8192.0, A.mult, 8191.5, A.add)
+        ts(v("hx0"), v("lf"), 8192.0, A.mult, -8192.5, A.add)
         best(NB, "KAB", "H0", "H1", "hr", "rr", "r2", "x2s", "hx0", ("hh", "hx"))
         for q in range(16):
-            mm(v("p2", 15 - q, 512 - q, -16), mat("E1", q), v("hh"))
+            mm(v("p2", 15 - q, 512 - q, -16), mat("E1", q), v("hh"), True, True, q > 0)
         ts(v("nh"), v("hx"), -8192.0, A.mult)
-        ts(v("n0"), v("hx"), -1.0, A.mult, -2048.0, A.add)
-        tt(v("nlo"), v("n0"), v("ntc"), A.max)
+        ms(v("ZS", 0, 96), 1024.0)
+        for k in range(NZ):
+            w = NB // NZ
+            if k == NZ - 1:
+                behind.append(v("nh"))
+            cp(ind(v("ZS"), v("OFu", w * k, w * k + w)), v("Z" if last else "PK", 16 * w * k, 16 * w * k + 16 * w))
+        zr = v("ZR%d" % t)
+        send("az%d" % t, "lz", lender, zr, v("ZS", 0, 96))
+        ts(v("n0"), v("hx"), 2048.0 + E, A.add)
+        tt(v("nlo"), v("n0"), v("tcd"), A.max)
         for h in (1, 0):
             for k in (2 * h + 1, 2 * h):
                 for i in range(8):
@@ -447,11 +494,10 @@ def rank_program(g, core, T, topo):
                     act(v("NE", o, o + a1 - a0), v("p2", a0, a1), AF.Abs, scale=8192.0, bias=v("nh", b, b + 1))
                 scan(v("SC", 576 * k, 576 * k + 576), v("NE", 576 * k, 576 * k + 576), v("MK"), 0.0, A.min, A.max)
             c0, c1 = 16 * h, 16 * h + 16
-            tt(v("la", c0, c1), ind(v("SC", 1152 * h, 1152 * h + 1152), v("EN", 0, 1)), v("tc4096", c0, c1), A.subtract)
-            tt(v("lb", c0, c1), v("la", c0, c1), v("nlo", c0, c1), A.min)
-            ts(v("lou", c0, c1), v("lb", c0, c1), -1.0, A.mult)
+            tt(v("la", c0, c1), ind(v("SC", 1152 * h, 1152 * h + 1152), v("EN", 0, 1)), v("nlo", c0, c1), A.min)
+            cp(v("lou", c0, c1), v("la", c0, c1))
             for k in (2 * h + 1, 2 * h):
-                cp(ind(v("U", E, E + S + 512), v("lou", 8 * k, 8 * k + 8)), v("LV", 128 * k, 128 * k + 128))
+                cp(ind(v("U", 0, E + S), v("lou", 8 * k, 8 * k + 8)), v("LV", 128 * k, 128 * k + 128))
         if not last:
             mm(v("p7", 128, 129), v("O16"), v("cum", 31, 32))
             cp(v("Pi"), v("p7", 128, 129))
@@ -471,29 +517,23 @@ def rank_program(g, core, T, topo):
         if t:
             act(v("YC"), v("p6"))
             dma("Y", "d3", T.yc[:, 512 * t - 512:512 * t], T.YC[5:128:16, :], [v("YC")], [])
-        act(v("JW", 0, 512), v("JO"), scale=0.0)
-        for k in range(NJ):
-            w = NB // NJ
-            cp(ind(v("JW"), v("fou", w * k, w * k + w)), v("NW", 16 * w * k, 16 * w * k + 16 * w))
-        ts(v("D0"), v("JW", 0, 512), 0.0, A.is_equal, col(FILL), A.mult)
-        scan(v("JS"), v("D0"), v("JW", 0, 512), 0.0, A.mult, A.add)
-        to_list(v("p7", 0, 32), "FC", "JS")
-        ts(v("Hs"), v("p7", 0, 32), -OFS, A.add)
-        ts(v("ngu"), v("p7", 0, 32), -base - OFS, A.add)
+        act(v("NR"), ind(v("NW"), v("JJ")))
+        to_list(v("p7", 0, 32), "FC", "NR")
+        cp(v("Hs"), v("p7", 0, 32))
+        ts(v("ngu"), v("p7", 0, 32), -base, A.add)
         pc = v("p7", 0, 32)
         if last:
             pc = v("p6", 64, 96)
-            to_list(pc, "FC", "JS", True)
-        to_list(v("p6", 0, 32), "FO", "JS", last)
-        to_list(v("p6", 32, 64), "FJ", "JS", last)
+            to_list(pc, "FC", "NR", True)
+        to_list(v("p6", 0, 32), "FO", "NR", last)
         cp(v("Os"), v("p6", 0, 32))
-        cp(v("Js"), v("p6", 32, 64))
-        tt(v("df"), pc, v("Os"), A.subtract)
-        ts(v("pl"), pc, base + OFS, A.is_ge)
+        tt(v("d0"), pc, v("Os"), A.subtract)
+        ts(v("pl"), pc, base, A.is_ge)
+        tt(v("df"), v("d0"), v("fs"), A.mult)
         tt(v("n4"), v("pl"), v("df"), A.mult)
-        act(v("FG"), ind(v("U", E, E + S + 512), v("Hs")), AF.Identity, scale=col(FSC), bias=col(FBI))
-        to_list(v("p6", 96, 128), "F0", "FG", last)
-        tt(v("w1"), v("p6", 96, 128), v("Js"), A.is_equal)
+        act(v("FG"), ind(v("U", E, E + W), v("Hs")), AF.Identity, scale=col(FSC), bias=col(FBI))
+        to_list(v("p2", 0, 32), "F0", "FG", last)
+        tt(v("w1"), v("p2", 0, 32), v("Js"), A.is_equal)
         tt(v("w2"), v("df"), v("n4"), A.subtract)
         tt(v("a3"), v("Os"), v("n4"), A.add)
         tt(v("w3"), v("w1"), v("w2"), A.mult)
@@ -514,39 +554,46 @@ def rank_program(g, core, T, topo):
         tt(v("R2", 0, 192, 2), v("T1a"), v("ub", 0, 96), A.add)
         ts(v("R2", 1, 192, 2), v("Xb"), -2048.0, A.add)
         for q in range(16):
-            mm(v("p0", 0, 12), slid("F15", q), v("R2", 12 * q, 12 * q + 12), q == 0, q == 15)
+            mm(v("p0", 0, 12), slid("F15", q), v("R2", 12 * q, 12 * q + 12), q == 0, q == 15, q > 0)
         cp(v("G0", 4, 36, 6), v("p0", 0, 12, 2))
         cp(v("G1", 4, 36, 6), v("p0", 1, 12, 2))
         if not last:
-            ts(v("t1"), ind(zr, v("PL", 0, NA)), col(EA), A.mult, col(EG), A.add)
-            act(v("t2"), v("ZRp"), scale=col(EB))
-            tt(v("Tw", 0, E), v("t1"), v("t2"), A.add)
-        ms(v("U", 0, E), -4096.0)
+            act(v("t1"), zr, AF.Identity, scale=col(EA), bias=col(EG))
+            ts(v("zn"), zr, M1, A.add, M1, A.subtract)
+            act(v("t2"), v("zn"), scale=col(EB))
+            tt(v("Tw", 0, 96), v("t1"), v("t2"), A.add)
+        act(v("U", 0, 96), v("ior", 0, 96), AF.Identity, scale=0.0, bias=col(TMP + 22))
         for k in range(4):
             z = v("z16", 384 * k, 384 * k + 384)
             act(z, ind(v("ZRp"), v("ZL", 24 * k, 24 * k + 24)))
             df, ab = v("DF%d" % (k % 3), 0, 384), v("AA", 384 * k, 384 * k + 384)
-            tt(df, ind(stones, v("HA", 24 * k, 24 * k + 24)), z, A.subtract)
-            act(ab, df, AF.Abs)
+            if k in SA:
+                act(v("GS", 0, 384), ind(stones, v("HA", 24 * k, 24 * k + 24)))
+                mm(v("p4", 0, 384), v("ID"), v("GS", 0, 384), True, False)
+                mm(v("p4", 0, 384), v("NI"), z, False, True)
+                act(ab, v("p4", 0, 384), AF.Abs)
+            else:
+                tt(df, ind(stones, v("HA", 24 * k, 24 * k + 24)), z, A.subtract)
+                act(ab, df, AF.Abs)
             for q in range(4 * k, 4 * k + 4):
-                mm(v("p5", 0, 96), slid("FD", q), v("AA", 96 * q, 96 * q + 96), q == 0, q == 15)
+                mm(v("p5", 0, 96), slid("FD", q), v("AA", 96 * q, 96 * q + 96), q == 0, q == 15, q % 4 > 0)
         scan(v("KE", 0, 96), v("DA", 0, 96), v("p5", 0, 96), 0.0, A.add, A.min)
         scan(v("KE", 96, 192), v("DB", 0, 96), v("p5", 0, 96), 0.0, A.add, A.min)
         ts(v("k6", 0, NA), v("KE", 15, 96, 16), thr, A.is_ge, -8192.0, A.mult)
         ts(v("k7", 0, NA), v("k6", 0, NA), -0.5, A.add)
-        best(NA, "KE", "G0", "G1", "gr", "ra", "s2", "s3", "k7", ("ha", "ga1"))
-        for q in range(16):
-            mm(v("p1", 15 - q, 96 - q, -16), mat("E1", q), v("ha", 0, NA))
+        best(NA, "KE", "G0", "G1", "gr", "ra", "s2", "s3", "k7", ("ga1",))
+        for b in range(NA):
+            ts(v("RX", 80 - 16 * b, 96 - 16 * b), v("qr"), v("ga1", b, b + 1), A.mult)
+        mm(v("p1", 0, 96), v("BD"), v("RX"))
         ts(v("ga2", 0, NA), v("ga1", 0, NA), 2048.0 + E, A.add)
-        tt(v("ga3", 0, NA), v("ga2", 0, NA), v("ecl", 0, NA), A.max)
+        tt(v("gm", 0, NA), v("ga2", 0, NA), v("tcq", 0, NA), A.max)
         for b in range(NA):
             o = 8 * b * (b + 1)
             ts(v("NE", o, o + 16 * b + 16), v("p1", 80 - 16 * b, 96), v("ga1", b, b + 1), A.not_equal, 8192.0, A.mult)
         scan(v("SC", 0, 336), v("NE", 0, 336), v("MK", 0, 336), 0.0, A.min, A.max)
-        tt(v("ga"), ind(v("SC", 0, 1152), v("EN", 0, 1)), v("ecl"), A.add)
-        tt(v("gb", 0, NA), v("ga", 0, NA), v("ga3", 0, NA), A.min)
+        tt(v("ga"), ind(v("SC", 0, 1152), v("EN", 0, 1)), v("gm"), A.min)
         glu = v("glu", 0, NA)
-        cp(glu, v("gb", 0, NA))
+        cp(glu, v("ga", 0, NA))
         if not last:
             cp(v("SB"), ind(v("Tw", 0, E + S), glu))
             send("at%d" % t, "ly", asker, v("Tw", E + S + 96 * t, E + S + 96 * t + 96), v("SB"))
@@ -555,9 +602,9 @@ def rank_program(g, core, T, topo):
         if not last:
             cp(ind(v("U", 0, E + S), glu), v("L255"))
         else:
-            for k in range(4):
-                x, y = v("U", E + 1024 * k, E + 1024 * k + 1024), v("UO", E + 1024 * k, E + 1024 * k + 1024)
-                if k == 3:
+            for k in range(16):
+                x, y = v("U", E + 256 * k, E + 256 * k + 256), v("UO", E + 256 * k, E + 256 * k + 256)
+                if k % 4 == 3:
                     ts(y, x, col(C256), A.add)
                 else:
                     act(y, x, AF.Identity, bias=col(C256))
@@ -567,9 +614,8 @@ def rank_program(g, core, T, topo):
                 y = v("UO", E + 1024 * k, E + 1024 * k + 1024)
                 dma("S" if k % 2 else "Y", "d4", T.yu[:, 1024 * k:1024 * k + 1024], y[0], [y], [], 3.0 + k)
 
-    ts(v("idx"), v("idx1", 0, 32), -OFS, A.add)
     flags(R - 1, True)
-    tt(v("yo"), v("idx"), v("w4"), A.subtract)
+    tt(v("yo"), idx, v("w4"), A.subtract)
     dma("Y", "d6", T.yc[:, 512 * R - 512:512 * R], T.yo[:, :], [v("yo")], [])
     ts(v("UQ"), v("UP"), col(C256), A.add, 0.0, A.max)
     dma("S", "d5", T.yu[:, S:W], T.UQ[:, :], [v("UQ")], [])
@@ -595,16 +641,38 @@ def rank_program(g, core, T, topo):
     for n in range(len(calls) - 1, -1, -1):
         for k, wait in calls[n]["pre"].items():
             calls[k]["tail"] = max(calls[k]["tail"], calls[k]["cost"] + wait + calls[n]["tail"])
-    busy = {q: [] for q in Q}
-    for n in sorted(range(len(calls)), key=lambda n: (calls[n]["kind"] != "F", n if calls[n]["kind"] == "F" else -calls[n]["tail"], n)):
-        c = calls[n]
-        at = max([calls[k]["at"] + calls[k]["cost"] + wait for k, wait in c["pre"].items()] + [0.0])
-        line, i = busy[c["q"]], 0
-        while i < len(line) and line[i][0] < at + c["cost"] - 1e-9:
-            at = max(at, line[i][1])
-            i += 1
-        line.insert(i, (at, at + c["cost"]))
-        c["at"] = at
+    for c in calls:
+        c["post"] = {}
+    for n, c in enumerate(calls):
+        for k, wait in c["pre"].items():
+            calls[k]["post"][n] = wait
+
+    def place(order, side):
+        busy, at = {q: [] for q in Q}, {}
+        for n in order:
+            c = calls[n]
+            t0 = max([at[k] + calls[k]["cost"] + wait for k, wait in c[side].items()] + [c["late"] if side == "post" else 0.0])
+            line = busy[c["q"]]
+            i = len(line)
+            while i and line[i - 1][1] > t0:
+                i -= 1
+            while i < len(line) and line[i][0] < t0 + c["cost"] - 1e-9:
+                t0 = max(t0, line[i][1])
+                i += 1
+            line.insert(i, (t0, t0 + c["cost"]))
+            at[n] = t0
+        return at
+    every = range(len(calls))
+    key = {n: -calls[n]["tail"] for n in every}
+    at = ORDER
+    for k in range(0 if ORDER else PASSES + 1):
+        at = place(sorted(every, key=lambda n: (calls[n]["kind"] != "F", n if calls[n]["kind"] == "F" else key[n], n)), "pre")
+        if k < PASSES:
+            back = place(sorted(every, key=lambda n: (-at[n] - calls[n]["cost"], -n)), "post")
+            key = {n: -back[n] - calls[n]["cost"] for n in every}
+    ORDER.update(at)
+    for n in every:
+        calls[n]["at"] = at[n]
 
     count, known, snaps, rec = {}, {q: {} for q in Q}, {}, {}
 
@@ -642,14 +710,15 @@ def rank_program(g, core, T, topo):
     for n in sorted(range(len(calls)), key=lambda n: (calls[n]["at"], n)):
         c = calls[n]
         q = c["q"]
-        settle(q, c["rs"], c["ws"])
-        if c["kind"] == "R":
-            e, step = "L" + c["sem"][0], c["sem"][1]
-            c["f"]()
-        else:
-            e, step = (q, 1) if c["kind"] == "C" else ("D" + c["sem"], 16)
-            c["f"]().then_inc(T.sem[SEM.get(e, e[1:])], step)
-        count[e] = count.get(e, 0) + step
-        note(e, count[e], c["rs"], c["ws"], known[q])
+        for f, rs, ws in c["parts"]:
+            settle(q, rs, ws)
+            if c["kind"] == "R":
+                e, step = "L" + c["sem"][0], c["sem"][1]
+                f()
+            else:
+                e, step = (q, 1) if c["kind"] == "C" else ("D" + c["sem"], 16)
+                f().then_inc(T.sem[SEM.get(e, e[1:])], step)
+            count[e] = count.get(e, 0) + step
+            note(e, count[e], rs, ws, known[q])
     for e, n in sorted(count.items()):
         g.wait_ge(T.sem[SEM.get(e, e[1:])], n)

@@ -1,35 +1,41 @@
-from concourse.mybir import AluOpType, ActivationFunctionType
+from concourse.mybir import AluOpType, ActivationFunctionType, AxisListType
 
-NB, NA, S, W, R, E = 32, 6, 4096, 4384, 3, 128
-SG = (1, 3, 5)
+NB, NA, S, W, R, E = 32, 6, 4096, 4384, 3, 256
+SG = {1: 32, 3: 32, 5: 32}
 NAB = 4
-ZV = 128
-NZ = 1
-SA = ()
+LAST = 22
+QA = (0, 5, 8, 13, 16)
+SA = (1,)
 N1 = 4
-PASSES = 2
+PASSES = 1
+U1 = 2.0
+U2 = 2.0
+FIRST = 2.0
+BC = 4
+RUN = 8 * BC * (BC + 1)
 F, B, I, H, U16 = "float32", "bfloat16", "int32", "float16", "uint16"
 M1, M128, M256, M4096 = 1.5 * 2 ** 23, 1.5 * 2 ** 30, 1.5 * 2 ** 31, 1.5 * 2 ** 35
 SCRATCH, PACK, PACKED = {}, {}, {}
-SEMAPHORES = ["sv", "ss", "sp", "sg", "d0", "d1", "d2", "d3", "d4", "d5", "d6", "dt", "lz", "ly", "lx"] + ["du%d" % t for t in range(4)]
+SEMAPHORES = ["sv", "ss", "sp", "sg", "d0", "d1", "d2", "d3", "d4", "d5", "d6", "dt", "lz", "ly", "lx", "lw"] + ["du%d" % t for t in range(4)]
 for _t in range(R):
-    SEMAPHORES += ["az%d" % _t, "au%d" % _t] + (["at%d" % _t] if _t < R - 1 else [])
-    SCRATCH["ZR%d" % _t] = ("sbuf", [128, 96], F)
+    SEMAPHORES += ["az%d" % _t, "au%d" % _t] + (["at%d" % _t, "ae%d" % _t] if _t < R - 1 else [])
+    SCRATCH["ZR%d" % _t] = ("sbuf", [128, 96], B)
 for _n in range(NAB):
     SCRATCH["AB%d" % _n] = ("sbuf", [128, NB, 2, 16], B)
 for _n in range(8):
     SCRATCH["p%d" % _n] = ("psum", [128, 512], F)
 for _w, _d, _s in (
         (E + W, F, "U"), (E + W, B, "Tw"), (E + S, B, "UO"), (288, B, "UP UQ"), (512, I, "C8 X X2"), (512, H, "c16"), (2048, B, "E1"), (2064, B, "Y"),
-        (2048, H, "KD"), (2048, F, "ZS"), (1024, F, "KAB"), (512, F, "ior YC LV PK DA DB JV"), (2304, B, "NE SC"), (576, B, "MK"), (1024, F, "JW"),
-        (512, B, "DM ZA Z GS NW NR FG NG DF0 DF1 DF2"), (512, H, "JS"), (1536, B, "z16 AA"), (512, U16, "HL"), (192, H, "H0 H1 R2"), (192, F, "hr KE"), (192, I, "ua ub"),
-        (144, F, "io144"), (144, B, "B0 B8 FD FC FO FJ F0 F15"), (144, H, "WU WV"), (128, H, "RU RV"), (128, B, "BD BY ID NI DG GE ZM"),
-        (128, F, "io8 iox BF SH1 SH2 O16 rep x1 x2"), (96, F, "t1 t2 T1a io96"), (96, I, "PRa kua qa Xa Xb"), (96, U16, "HA ZL"), (96, B, "ZRp zn SB SU L255"), (96, H, "RX"),
-        (2, I, "pi pq hwi"), (1, I, "kmi thi Pi Pj ei"), (1, F, "pf qf gf kmf thf e1 e2 e3 e4"), (2, F, "hwf hwg hws hwm"), (2, U16, "EN"),
+        (2048, H, "KD"), (2048, F, "ZS TS"), (1024, F, "KAB"), (512, F, "ior NW LV Zf Tf DA DB JV"), (2304, B, "NE SC"), (576, B, "MA"), (128, F, "la"), (48, F, "nlo"), (1024, F, "JW"),
+        (512, B, "DM GA GB Z GS NR FG NG DF0 DF1 DF2"), (512, H, "JS"), (1536, B, "z16 AA"), (512, U16, "HL"), (192, H, "H0 H1 R2"), (192, F, "hr KE"), (192, I, "ua ub"),
+        (144, F, "io144"), (144, B, "B0 B8 FD FC FO FJ F0 F15 IL IH"), (144, H, "WU WV WA WB"), (128, I, "uva uv"), (128, H, "u16"), (128, H, "RU RV"), (128, B, "BD BY ID NI GE LT ON ZM"),
+        (128, F, "io8 iox BF SH1 SH2 rep x1 x2"), (96, F, "T1a"), (96, I, "PRa kua qa Xa Xb"), (96, U16, "HA ZL"), (96, B, "ZB TB SB SU L255"), (96, H, "RX"),
+        (33, B, "pw"), (33, H, "pn"),
+        (2, I, "pi pq hwi"), (1, I, "kmi thi Pi Pj ei"), (1, F, "pf qf gf kmf thf e1 e2 e3 e4 Pf"), (2, F, "hwf hwg hws hwm"), (4, U16, "EN"),
         (16, F, "io16 qm qr kq KM KS0 KS dA dB dC ga gm mq"), (16, I, "ki kj ka kb"), (64, F, "rr"), (36, H, "G0 G1"), (36, F, "gr"), (33, F, "idx1"),
-        (40, F, "col"), (32, F, "tc tcq tc512 tc1024 tcd W40 W4 on idx T1 nf pen0 pen cum ww OF lf hx0 r2 x2s hx nh n0 nlo la lb Cf Cb cw ee ec mu rc pj pj2 fo "
+        (48, F, "col"), (32, F, "tc tcq tc512 nt1024 nrt c16f tcd W40 W4 on uf vf nf OF lf hx0 r2 x2s hx nh n0 Cf Cb cw ee ec mu rc pj pj2 fo "
                                 "a1 a2 a3 a4 a5 dd Os Js d0 df fs jt jf pl n4 w1 w2 w3 w4 yo"),
-        (32, I, "PR qi f3 fi nx Ci"), (64, I, "uva uv"), (32, H, "qh hh"), (8, H, "ha"), (32, B, "pw wv Dh Dl Ch Cl"), (32, U16, "OFu lou fou ngu Hs JJ"),
+        (32, I, "PR qi f3 fi nx Ci"), (32, H, "qh hh"), (8, H, "ha"), (32, B, "wv Dh Dl Ch Cl"), (32, U16, "OFu lou fou ngu Hs JJ"),
         (8, U16, "glu PL"), (64, U16, "CL"), (8, I, "pd"), (12, F, "ra"), (8, F, "k6 k7 s2 s3 ga1 ga2 ga3 gb pp")):
     for _n in _s.split():
         if _w <= 64 and _n not in ("hwi", "kmi", "thi", "yo"):
@@ -41,8 +47,71 @@ for _w, _d, _s in (
 for _k, _w in PACKED.items():
     SCRATCH[_k] = ("sbuf", [128, _w], _k[2:])
 
-CYC, HOP, FAR = 0.83e-3, 0.17, 3.0
+CYC, HOP, FAR = 0.83e-3, 0.17, 2.4
 ORDER = {}
+PACE = ((1.0, 1.0), (1.3, 1.35), (1.0, 0.7))
+TRIES, HEAT = 3000, 0.15
+
+
+def improve(calls, at):
+    every = range(len(calls))
+    post = [list(c["post"].items()) for c in calls]
+    costs = [[c["cost"] * (f if c["kind"] == "C" else 1) * (x if c["ind"] else 1) for c in calls] for f, x in PACE]
+    prev, nxt, tail = [None] * len(calls), [None] * len(calls), {}
+    for n in sorted(every, key=lambda n: (at[n], n)):
+        a = prev[n] = tail.get(calls[n]["q"])
+        if a is not None:
+            nxt[a] = n
+        tail[calls[n]["q"]] = n
+
+    def walk(cost):
+        left = [len(calls[n]["pre"]) + (prev[n] is not None) for n in every]
+        head, why, todo, end, last = [0.0] * len(calls), [None] * len(calls), [n for n in every if not left[n]], 0.0, None
+        while todo:
+            n = todo.pop()
+            e = head[n] + cost[n]
+            if e + calls[n]["late"] > end:
+                end, last = e + calls[n]["late"], n
+            for k, w in post[n] if nxt[n] is None else post[n] + [(nxt[n], 0.0)]:
+                if e + w > head[k]:
+                    head[k], why[k] = e + w, n
+                left[k] -= 1
+                if not left[k]:
+                    todo.append(k)
+        pairs = []
+        while why[last] is not None:
+            u = why[last]
+            if u == prev[last] and u not in calls[last]["pre"] and calls[u]["kind"] != "F":
+                pairs.append((u, last))
+            last = u
+        return end, head, pairs
+
+    def swap(u, w):
+        a, b = prev[u], nxt[w]
+        prev[w], nxt[w], prev[u], nxt[u] = a, u, w, b
+        if a is not None:
+            nxt[a] = w
+        if b is not None:
+            prev[b] = u
+
+    def look():
+        runs = [walk(c) for c in costs]
+        return sum(r[0] / f for r, (f, x) in zip(runs, PACE)), runs
+    now = best = look()
+    turn = 1
+    for it in range(TRIES):
+        turn = (turn * 1103515245 + 12345) % 2147483648
+        pairs = now[1][it % len(costs)][2]
+        if pairs:
+            u, w = pairs[(turn >> 8) % len(pairs)]
+            swap(u, w)
+            new = look()
+            if new[0] < now[0] + HEAT * (1 - it / TRIES) * ((turn >> 4) % 16) / 8:
+                now = new
+                best = min(best, now, key=lambda x: x[0])
+            else:
+                swap(w, u)
+    return dict(enumerate(best[1][0][1]))
 
 
 def rank_program(g, core, T, topo):
@@ -78,6 +147,7 @@ def rank_program(g, core, T, topo):
         return not (a[3] == b[3] and a[3] > 1 and (a[1] - b[1]) % a[3])
 
     behind = []
+    urge = []
 
     def add(q, f, reads, writes, cost, kind="C", sem=None, late=0.0, far=None, join=False):
         rs = [r for x in reads if isinstance(x, tuple) for r in x[1]]
@@ -89,8 +159,9 @@ def rank_program(g, core, T, topo):
             c["rs"] += [r for r in rs if r not in c["rs"]]
             c["cost"] += cost
             return
-        calls.append(dict(q=q, parts=[(f, rs, ws)], rs=list(rs) + [r for x in behind for r in x[1]], ws=ws, cost=cost, kind=kind, sem=sem, late=late, far=far))
-        del behind[:]
+        calls.append(dict(q=q, parts=[(f, rs, ws)], rs=list(rs) + [r for x in behind for r in x[1]], ws=ws, cost=cost, kind=kind, sem=sem, late=late, far=far, urge=sum(urge),
+                          ind=any(x[4] for x in list(reads) + list(writes) if isinstance(x, tuple))))
+        del behind[:], urge[:]
 
     def _(x):
         return x[0] if isinstance(x, tuple) else x
@@ -122,7 +193,7 @@ def rank_program(g, core, T, topo):
         op("V", lambda: g.vector.memset(_(o), c), o, [])
 
     def scan(o, a, b, init, op0, op1):
-        op("V", lambda: g.vector.tensor_tensor_scan(_(o), _(a), _(b), init, op0, op1), o, [a, b])
+        op("V", lambda: g.vector.tensor_tensor_scan(_(o), _(a), _(b), _(init), op0, op1), o, [a, b, init])
 
     def act(o, i, func=AF.Copy, scale=None, bias=None):
         kw = {}
@@ -141,10 +212,10 @@ def rank_program(g, core, T, topo):
     def dma(q, sem, out, in_, reads, writes, late=2.0, first=False):
         add(q, lambda: Q[q].dma_start(out, in_), reads, writes, 0.05, "F" if first else "D", sem, late)
 
-    def send(sem, lsem, dst, out, src):
+    def send(sem, lsem, dst, out, src, more=0.0):
         es = topo.engines(core, dst)[:8]
         rid, pid, se = topo.addr(dst)
-        add("G", lambda: g.remote_dma(out[0], src[0], T.sem[sem], T.sem[lsem], pid, rid, sum(1 << k for k in es)), [src], [], 0.6, "R", (lsem, len(es)), FAR, out[1])
+        add("G", lambda: g.remote_dma(out[0], src[0], T.sem[sem], T.sem[lsem], pid, rid, sum(1 << k for k in es)), [src], [], 0.6, "R", (lsem, len(es)), FAR + more, out[1])
 
     def col(j):
         return v("col", j, j + 1)
@@ -155,11 +226,11 @@ def rank_program(g, core, T, topo):
     def slid(name, q, p=None):
         return v(name, 16 - q, 144 - q, p=p)
 
-    def half(k, j):
-        return (T["AB%d" % k][:, :, j, :], [("AB%d.%d" % (k, j), 0, 1, 1)], 512, True, None)
+    def half(k, j, lo=0, hi=NB):
+        return (T["AB%d" % k][:, lo:hi, j, :], [("AB%d.%d" % (k, j), lo, hi, 1)], 16 * (hi - lo), True, None)
 
     def both(k, q):
-        return (T["AB%d" % k][:, :, :, q], [("AB%d.0" % k, 0, 1, 1), ("AB%d.1" % k, 0, 1, 1)], 64, True, None)
+        return (T["AB%d" % k][:, :, :, q], [("AB%d.0" % k, 0, NB, 1), ("AB%d.1" % k, 0, NB, 1)], 64, True, None)
 
     def to_list(ps, wt, row, dense=False):
         for q in range(16):
@@ -208,6 +279,9 @@ def rank_program(g, core, T, topo):
     ts(col(LAID), col(LO), -256.0, A.mult, 255.0, A.add)
     ts(col(ZSC), col(LO), -255.0, A.mult, 256.0, A.add)
     ts(col(ZBI), col(LO), -512.0, A.mult, 256.0, A.add)
+    ts(v("e2"), v("pf"), -8.0, A.add)
+    ts(v("IL"), v("io144"), v("e2"), A.is_equal, col(LO), A.mult)
+    ts(v("IH"), v("io144"), v("e2"), A.is_equal, col(HI), A.mult)
     ts(col(B0C), v("gf"), 16.0, A.mult)
     ts(v("B0"), v("io144"), col(B0C), A.is_equal)
     ts(v("e1", p=P8), v("pf", p=P8), 16.0, A.mult)
@@ -233,8 +307,10 @@ def rank_program(g, core, T, topo):
     mm(v("p5", 2, 18), v("BF"), v("kq"))
     cp(v("col", CU, CV + 1), v("p5", 0, 2))
     cp(v("KM"), v("p5", 2, 18))
-    for j, (a, b) in enumerate((("WU", "RU"), ("WV", "RV"))):
-        ts(v(a), v("B0"), v("hws", j, j + 1), A.mult)
+    for j, (a, b) in enumerate((("WA", "RU"), ("WB", "RV"))):
+        ts(v("WU", 8, 144), v("B0", 8, 144), v("hws", 0, 1), A.mult, col(LO + j), A.mult)
+        ts(v("WV", 8, 144), v("B0", 0, 136), v("hws", 1, 2), A.mult, col(LO + j), A.mult)
+        tt(v(a, 8, 144), v("WU", 8, 144), v("WV", 8, 144), A.add)
         ts(v(b), v("BD"), v("hws", j, j + 1), A.mult)
     ts(v("KS0"), v("KM"), 2048.0, A.is_ge, -4096.0, A.mult)
     tt(v("KS"), v("KS0"), v("KM"), A.add)
@@ -271,12 +347,13 @@ def rank_program(g, core, T, topo):
     ts(v("x1"), io128, v("pf"), A.is_le)
     tt(v("GE"), v("x1"), v("BD"), A.mult)
     ms(v("on"), 1.0)
-    ms(v("O16"), 0.0625)
+    tt(v("LT"), v("BD"), v("GE"), A.subtract)
+    ms(v("ON"), 1.0)
     ts(v("tcq"), v("tc"), v("qf"), A.add)
-    for n in (512, 1024):
-        ts(v("tc%d" % n), v("tcq"), float(n), A.add)
-    for k in range(4):
-        cp(v("tcd", 8 * k, 8 * k + 8), v("tcq", 0, 8))
+    ts(v("tc512"), v("tcq"), 512.0, A.add)
+    ts(v("nt1024"), v("tcq"), -1.0, A.mult, -1024.0, A.add)
+    for k in range(NB // BC):
+        cp(v("tcd", BC * k, BC * k + BC), v("tcq", 0, BC))
     ts(v("W40"), v("tcq"), 510.0, A.is_equal, 5112.0, A.mult)
     ts(v("W4"), v("W40"), 4.0, A.add)
     ts(v("x1"), v("iox"), 0.0, A.is_equal)
@@ -287,8 +364,6 @@ def rank_program(g, core, T, topo):
     for q in range(16):
         act(mat("E1", q), v("BD"), scale=qm(q))
         act(mat("Y", q, -16), v("BY"), scale=qm(q))
-    ts(col(TMP), col(HI), 2.0 ** -18, A.mult)
-    ts(v("DG"), v("ID"), col(TMP), A.mult)
     ts(col(LSC), qm(0), 2.0 ** -24, A.mult)
     ts(col(LBI), qm(0), 2.0 ** -16, A.mult, col(LAID), A.add)
     act(v("LV"), v("ior"), AF.Identity, scale=col(LSC), bias=col(LBI))
@@ -299,32 +374,29 @@ def rank_program(g, core, T, topo):
     act(v("DM"), v("ior"), AF.Identity, scale=0.0, bias=qm(0))
     ms(v("ZM"), 0.0)
     act(v("L255"), v("ior", 0, 96), AF.Identity, scale=0.0, bias=col(LAID))
-    ts(col(EA), col(HI), 1024.0, A.mult)
-    tt(col(EG), col(C256), col(HI), A.subtract)
-    tt(col(EB), col(LO), col(EA), A.subtract)
     ts(v("ga"), v("io16"), v("qf"), A.add)
     ts(v("mq"), v("ga"), 15.5, A.is_lt, 16384.0, A.mult)
     ts(v("qr"), v("ga"), 15.0, A.is_equal)
-    for i in range(8):
+    for i in range(max(BC, NA)):
         o = 8 * i * (i + 1)
-        act(v("MK", o, o + 16), v("mq"), AF.Identity, bias=v("tcq", i, i + 1))
+        act(v("MA", o, o + 16), v("mq"), AF.Identity, bias=v("tcq", i, i + 1))
         if i:
-            act(v("MK", o + 16, o + 16 * i + 16), v("ior", 0, 16 * i), AF.Identity, scale=0.0, bias=v("tcq", i, i + 1))
-    ts(v("ei"), v("pq", 1, 2), 7, A.bitwise_and)
-    ts(v("e2"), v("ei"), 8.0, A.mult, 8.0, A.add)
-    ts(v("e3"), v("ei"), 2.0, A.add, v("e2"), A.mult)
-    ts(v("e4"), col(HI), 576.0, A.mult, -1.0, A.add)
-    ts(v("EN", 0, 1), v("e3"), v("e4"), A.add)
+            act(v("MA", o + 16, o + 16 * i + 16), v("ior", 0, 16 * i), AF.Identity, scale=0.0, bias=v("tcq", i, i + 1))
+    for k, n in enumerate((BC, NA)):
+        ts(v("e1"), v("qf"), n - 1.0, A.min)
+        ts(v("e2"), v("e1"), 8.0, A.mult, 8.0, A.add)
+        ts(v("e3"), v("e1"), 2.0, A.add, v("e2"), A.mult)
+        ts(v("EN", 2 * k, 2 * k + 1), v("e3"), -1.0, A.add)
+    ms(v("nlo", 32, 48), 0.0)
     ts(v("pd", 0, NA), v("tcq", 0, NA), 1.0 / 6.0, A.mult, -5.0 / 12.0, A.add)
     ts(v("pp", 0, NA), v("pd", 0, NA), -95.0, A.mult)
     ts(v("s2", 0, NA), v("tcq", 0, NA), 16.0, A.mult)
     tt(v("s3", 0, NA), v("s2", 0, NA), v("pp", 0, NA), A.add)
     cp(v("PL", 0, NA), v("s3", 0, NA))
-    cp(v("ZL"), v("io144", 16, 112))
     ms(v("U", E + S, E + W), 0.0)
-    for k in range(4):
-        x, y = v("U", E + 1024 * k, E + 1024 * k + 1024), v("UO", E + 1024 * k, E + 1024 * k + 1024)
-        if k == 3:
+    for k in range(8):
+        x, y = v("U", E + 512 * k, E + 512 * k + 512), v("UO", E + 512 * k, E + 512 * k + 512)
+        if k == 7:
             ts(x, y, col(CN256), A.add)
         else:
             act(x, y, AF.Identity, bias=col(CN256))
@@ -349,48 +421,71 @@ def rank_program(g, core, T, topo):
                 mm(v("p6", q, 512, 16), mat("Y", q, shift - 16), v(name), False, name == "Dl" and q == 15, q % 8 > 0)
 
     def flags(t, dense):
-        act(v("NG"), ind(v("UP", 96 * t, 96 * t + 96), v("ngu")), AF.Relu, scale=-1.0 / 2048.0, bias=col(TMP + 21))
+        up = v("UP", 96 * t, 96 * t + 96)
+        if dense:
+            ts(v("NG", 0, 256), ind(up, v("ngu", 0, 16)), -2048.0, A.is_lt)
+            act(v("NG", 256, 512), ind(up, v("ngu", 16, 32)), AF.Relu, scale=-1.0 / 2048.0, bias=col(TMP + 21))
+        else:
+            act(v("NG"), ind(up, v("ngu")), AF.Relu, scale=-1.0 / 2048.0, bias=col(TMP + 21))
         to_list(v("p7", 0, 32), "F0", "NG", dense)
         tt(v("w4"), v("p7", 0, 32), v("n4"), A.mult)
     ms(col(TMP + 21), -1.0)
     ms(col(TMP + 22), -4096.0)
     ms(v("gm"), 0.0)
-    ms(v("Tw", 96, E), 0.0)
+    ms(col(TMP + 24), 2304.0)
+    ms(col(TMP + 25), 1280.0)
+    ts(col(EA), col(LO), 255.0 / 256.0, A.mult, 1.0 / 256.0, A.add)
+    ts(col(EG), col(LO), 257.0, A.mult, 1023.0, A.add)
+    ts(col(TMP + 26), col(CU), col(LO), A.mult)
+    ts(col(EB), col(CV), col(HI), A.mult, col(TMP + 26), A.add)
+    ts(col(TMP + 23), v("qf"), 1008.0, A.add)
+    ms(v("c16f"), 16.0)
+    ms(v("pw", 0, 1), 0.0)
+    ts(v("pn", 0, 1), v("qf"), 0.0, A.mult)
+    ms(v("TS", 0, 96), 1024.0)
+    for a in (96, 224):
+        ms(v("Tw", a, a + 32), 0.0)
+    ms(v("U", 0, E), 0.0)
 
     for t in range(R):
         last = t == R - 1
         lender, asker = T.cores[(rank + 1 + t) % 8], T.cores[(rank - 1 - t) % 8]
         base, thr = float(S + 96 * t), col(THR + t % 2)
-        stones = v("U", E, E + S)
+        stones, e0 = v("U", E, E + S), 0 if t == 1 else 128
         cp(v("CL", 0, 32), idx)
         mm(v("p7", 32, 64), v("SH1"), idx, True, False)
         mm(v("p7", 32, 64), v("SH2"), v("idx1", 1, 33), False, True, True)
         cp(v("CL", 32, 64), v("p7", 32, 64))
         tops = v("Tw", E, E + S + 96 * t)
-        cuts = (0, (512 - ZV) // 32 * 16, 512 - ZV, 512)
-        for a, b in zip(cuts, cuts[1:]):
-            if b == 512:
-                ts(v("ZA", a, b), ind(tops, v("CL", a // 16, b // 16)), col(ZSC), A.mult, col(ZBI), A.add)
-            else:
-                act(v("ZA", a, b), ind(tops, v("CL", a // 16, b // 16)), AF.Identity, scale=col(ZSC), bias=col(ZBI))
-        for a, b in ((0, cuts[1]), (cuts[1], 512)):
-            tt(v("Z", a, b), ind(tops, v("CL", 32 + a // 16, 32 + b // 16)), v("ZA", a, b), A.min)
-        for j, wt in ((0, "WU"), (1, "WV")):
-            to_list(v("p%d" % j, 0, 32), wt, "Z")
-            ts(v("uva", 32 * j, 32 * j + 32), v("p%d" % j, 0, 32), col(CU + j), A.add)
-            ts(v("uv", 32 * j, 32 * j + 32), v("uva", 32 * j, 32 * j + 32), 4095, A.bitwise_and)
+        act(v("GA"), ind(tops, v("CL", 0, 32)), AF.Identity, scale=col(ZSC), bias=col(ZBI))
+        cp(v("GB"), ind(tops, v("CL", 32, 64)))
+        tt(v("Z"), v("GA"), v("GB"), A.min)
+        act(v("Zf"), v("Z"), AF.Identity, bias=col(TMP + 25))
+        for k, (wt, z) in enumerate((("WA", "GA"), ("WB", "GB"))):
+            for r in range(8):
+                mm(v("p0", 0, 64), slid(wt, r), v(z, r, 512, 8), k + r == 0, k + r == 8, r > 0)
+        for j in (0, 1):
+            ts(v("uva", 64 * j, 64 * j + 64), v("p0", 0, 64), col(EB), A.add, 2048.0 * j, A.add)
+        ts(v("uv"), v("uva"), 4095, A.bitwise_and)
+        ts(v("u16"), v("uv"), -2048.0, A.add)
+        mm(v("p1", 0, 64), v("IL", 8, 136), v("u16", 0, 128, 2), True, False)
+        mm(v("p1", 0, 64), v("IL", 0, 128), v("u16", 1, 128, 2), False, True, True)
+        mm(v("p1", 64, 96), v("IH", 16, 144), v("u16", 0, 64, 2), True, False, True)
+        mm(v("p1", 64, 96), v("IH", 8, 136), v("u16", 1, 64, 2), False, True, True)
         uh = v("H0", 4, 6 * NB, 6)
-        ts(v("T1"), v("uv", 0, 32), 2048.0, A.is_ge, -4096.0, A.mult)
-        tt(uh, v("T1"), v("uv", 0, 32), A.add)
-        tt(v("PR"), v("uv", 0, 32), v("uv", 32, 64), A.mult)
+        cp(uh, v("p1", 32, 64))
+        ts(v("uf"), v("p1", 0, 32), 2048.0, A.add)
+        ts(v("vf"), v("p1", 64, 96), 2048.0, A.add)
+        tt(v("PR"), v("uf"), v("vf"), A.mult)
         ts(v("qi"), v("PR"), 5, A.arith_shift_right, 4095, A.bitwise_and)
         ts(v("qh"), v("qi"), -2048.0, A.add)
         for lo, hi, bank in ((0, N1, "p2"), (N1, 16, "p3")):
+            if lo:
+                mm(v(bank, 32 * lo, 32 * hi), v("ZM"), v("DM", 32 * lo, 32 * hi), True, False)
             for i in range(lo, hi):
-                o = v(bank, 32 * i, 32 * i + 32)
-                mm(o, mat("KD", i // 2 + 8 * (i % 2)), uh, True, lo == 0, i > lo)
-                if lo:
-                    mm(o, v("ID"), v("qh"), False, True, True)
+                mm(v(bank, 32 * i, 32 * i + 32), mat("KD", i // 2 + 8 * (i % 2)), uh, lo == 0, lo == 0, i % 4 > 0)
+            for i in range(lo, hi if lo else 0):
+                mm(v(bank, 32 * i, 32 * i + 32), v("ID"), v("qh"), False, i == hi - 1, i % 4 > 0)
             if lo == 0:
                 for i in range(lo, hi):
                     tt(v("X", 32 * i, 32 * i + 32), v(bank, 32 * i, 32 * i + 32), v("qi"), A.add)
@@ -420,9 +515,11 @@ def rank_program(g, core, T, topo):
         ts(v("pj"), v("mu"), 0.5, A.is_lt)
         tt(v("pj2"), v("pj"), v("tc512"), A.mult)
         tt(v("fo"), v("fi"), v("pj2"), A.max)
+        urge.append(U1)
         cp(v("fou"), v("fo"))
         act(v("JW", 0, 512), v("ior"), scale=0.0)
         act(ind(v("JW"), v("fou")), v("JV"), AF.Silu)
+        urge.append(U2)
         scan(v("JS"), v("DM"), v("JW", 0, 512), 0.0, A.mult, A.max)
         for dense in range(1 + last):
             pj = v("p7", 160, 192)
@@ -436,74 +533,66 @@ def rank_program(g, core, T, topo):
                 ts(v("Js"), v("jf"), -1280.0, A.add)
         ts(v("Cb"), v("Cf"), -base, A.add)
         split("Ch", "Cl", "Cf")
-        if not last:
-            mm(v("p0"), v("ID"), v("Z"), True, False)
-            mm(v("p0"), v("DG"), v("ZA"), False, True)
-            act(v("PK"), v("p0"))
+        tt(v("nrt"), v("rc"), v("nt1024"), A.mult)
         n = 0
         for k in range(8):
             for j in (1, 0):
-                lst = v("HL", 64 * k + 32 * j, 64 * k + 32 * j + 32)
-                if j and k in SG:
-                    act(v("GS"), ind(stones, lst))
-                    mm(v("p5"), v("ID"), v("GS"), True, False)
-                    mm(v("p5"), v("NI"), v("Z"), False, True)
-                    act(half(k % NAB, j), v("p5"), AF.Abs)
-                else:
-                    df = v("DF%d" % (n % 3))
+                o, cut = 64 * k + 32 * j, SG.get(k, 0) if j else 0
+                if cut:
+                    w = 16 * cut
+                    act(v("GS", 0, w), ind(stones, v("HL", o, o + cut)))
+                    mm(v("p5", 0, w), v("ID"), v("GS", 0, w), True, False)
+                    mm(v("p5", 0, w), v("NI"), v("Z", 0, w), False, True)
+                    act(half(k % NAB, j, 0, cut), v("p5", 0, w), AF.Abs)
+                cuts = (cut, LAST, NB) if k == 7 and not j else (cut, NB) if cut < NB else ()
+                for a, b in zip(cuts, cuts[1:]):
+                    df = v("DF%d" % (n % 3), 16 * a, 16 * b)
                     n += 1
-                    tt(df, ind(stones, lst), v("Z"), A.subtract)
-                    act(half(k % NAB, j), df, AF.Abs)
+                    tt(df, ind(stones, v("HL", o + a, o + b)), v("Z", 16 * a, 16 * b), A.subtract)
+                    act(half(k % NAB, j, a, b), df, AF.Abs)
             for q in range(16):
                 mm(v("p4", k, 512, 8), slid("FD", q), both(k % NAB, q), q == 0, q == 15, q > 0)
         scan(v("KAB", 0, 512), v("DA"), v("p4"), 0.0, A.add, A.min)
         scan(v("KAB", 512, 1024), v("DB"), v("p4"), 0.0, A.add, A.min)
-        behind.append(v("p4"))
+        behind.append(half(7 % NAB, 0))
         mm(v("p6"), v("ZM"), v("Z"), True, False)
         rows("Ch", "Cl", 2, 5)
         ts(v("nf"), v("KAB", 15, 512, 16), thr, A.is_ge)
-        tt(v("pw"), v("nf"), v("mu"), A.mult)
-        mm(v("p1", 0, 32), v("BD"), v("pw"))
-        mm(v("p1", 32, 64), v("GE"), v("pw"))
-        ts(v("pen0"), v("pw"), 0.5, A.is_lt)
-        tt(v("pen"), v("pen0"), v("tc1024"), A.mult)
-        scan(v("cum"), v("on"), v("p1", 0, 32), 0.0, A.mult, A.add)
-        tt(v("ww"), v("p1", 32, 64), v("pen"), A.subtract)
-        tt(v("OF"), v("cum"), v("ww"), A.subtract)
+        tt(v("pw", 1, 33), v("nf"), v("mu"), A.mult)
+        tt(v("pn", 1, 33), v("nf"), v("nrt"), A.mult)
+        for k, (a, b, o) in enumerate((("GE", "pw", 0), ("LT", "pw", 1), ("NI", "pn", 0), ("ID", "pn", 1))):
+            mm(v("p1", 0, 32), v(a), v(b, o, o + 32), k == 0, k == 3, k > 0)
+        scan(v("OF"), v("c16f"), v("p1", 0, 32), col(TMP + 23), A.add, A.add)
         cp(v("OFu"), v("OF"))
+        act(v("ZS", 0, 96), v("ior", 0, 96), AF.Identity, scale=0.0, bias=col(TMP + 24))
+        act(ind(v("ZS"), v("OFu")), v("Zf"), AF.Silu)
+        zr = v("ZR%d" % t)
+        ts(v("ZB"), ind(v("ZS", 0, 96), v("PL", 0, NA)), M1, A.add, M1 + 1280.0, A.subtract)
+        send("az%d" % t, "lz", lender, zr, v("ZB"), FIRST if t == 0 else 0.0)
         tt(v("lf"), v("rc"), v("nf"), A.is_gt)
         ts(v("hx0"), v("lf"), 8192.0, A.mult, -8192.5, A.add)
         best(NB, "KAB", "H0", "H1", "hr", "rr", "r2", "x2s", "hx0", ("hh", "hx"))
         for q in range(16):
             mm(v("p2", 15 - q, 512 - q, -16), mat("E1", q), v("hh"), True, True, q > 0)
         ts(v("nh"), v("hx"), -8192.0, A.mult)
-        ms(v("ZS", 0, 96), 1024.0)
-        for k in range(NZ):
-            w = NB // NZ
-            if k == NZ - 1:
-                behind.append(v("nh"))
-            cp(ind(v("ZS"), v("OFu", w * k, w * k + w)), v("Z" if last else "PK", 16 * w * k, 16 * w * k + 16 * w))
-        zr = v("ZR%d" % t)
-        send("az%d" % t, "lz", lender, zr, v("ZS", 0, 96))
-        ts(v("n0"), v("hx"), 2048.0 + E, A.add)
-        tt(v("nlo"), v("n0"), v("tcd"), A.max)
-        for h in (1, 0):
-            for k in (2 * h + 1, 2 * h):
-                for i in range(8):
-                    b, o, a0, a1 = 8 * k + i, 576 * k + 8 * i * (i + 1), 496 - 128 * k - 16 * i, 512 - 128 * k
-                    act(v("NE", o, o + a1 - a0), v("p2", a0, a1), AF.Abs, scale=8192.0, bias=v("nh", b, b + 1))
-                scan(v("SC", 576 * k, 576 * k + 576), v("NE", 576 * k, 576 * k + 576), v("MK"), 0.0, A.min, A.max)
-            c0, c1 = 16 * h, 16 * h + 16
-            tt(v("la", c0, c1), ind(v("SC", 1152 * h, 1152 * h + 1152), v("EN", 0, 1)), v("nlo", c0, c1), A.min)
-            cp(v("lou", c0, c1), v("la", c0, c1))
-            for k in (2 * h + 1, 2 * h):
-                cp(ind(v("U", 0, E + S), v("lou", 8 * k, 8 * k + 8)), v("LV", 128 * k, 128 * k + 128))
+        ts(v("n0"), v("hx"), 2048.0 + E - e0, A.add)
+        tt(v("nlo", 0, 32), v("n0"), v("tcd"), A.max)
+        for k in range(NB // BC - 1, -1, -1):
+            for i in range(BC):
+                b, o = BC * k + i, RUN * k + 8 * i * (i + 1)
+                a0, a1 = 496 - 16 * b, 512 - 16 * BC * k
+                act(v("NE", o, o + a1 - a0), v("p2", a0, a1), AF.Abs, scale=8192.0, bias=v("nh", b, b + 1))
+            o, c0 = RUN * k, BC * k
+            scan(v("SC", o, o + RUN), v("NE", o, o + RUN), v("MA", 0, RUN), 0.0, A.min, A.max)
+            tt(v("la", 16 * k, 16 * k + 16), ind(v("SC", o, o + RUN), v("EN", 0, 1)), v("nlo", c0, c0 + 16), A.min)
+            cp(v("lou", c0, c0 + BC), v("la", 16 * k, 16 * k + BC))
+            cp(ind(v("U", e0, E + S), v("lou", c0, c0 + BC)), v("LV", 16 * c0, 16 * c0 + 16 * BC))
         if not last:
-            mm(v("p7", 128, 129), v("O16"), v("cum", 31, 32))
-            cp(v("Pi"), v("p7", 128, 129))
-            ts(v("Pj"), v("Pi"), 63, A.bitwise_and)
-            tt(col(TMP), col(TH), v("Pj"), A.add)
-            ts(col(THR + (t + 1) % 2), col(TMP), 4096.0, A.mult, -3968.0, A.add)
+            act(v("Tf"), v("GA"), AF.Identity, scale=col(EA), bias=col(EG))
+            behind.append(v("NE"))
+            act(ind(v("TS"), v("OFu")), v("Tf"), AF.Silu)
+            ts(v("TB"), v("TS", 0, 96), M1, A.add, M1 + 1024.0, A.subtract)
+            send("ae%d" % t, "lw", lender, v("Tw", e0, e0 + 96), v("TB"))
         tt(v("a1"), v("hx"), v("Cf"), A.subtract)
         ts(v("a1"), v("a1"), 2048.0, A.add)
         tt(v("a2"), v("a1"), v("lf"), A.mult)
@@ -513,10 +602,11 @@ def rank_program(g, core, T, topo):
         tt(v("dd"), v("a2"), v("a5"), A.add)
         split("Dh", "Dl", "dd")
         rows("Dh", "Dl", 0, 1)
+        if not last:
+            behind.append(v("TS"))
         act(v("NW"), v("p6"))
         if t:
-            act(v("YC"), v("p6"))
-            dma("Y", "d3", T.yc[:, 512 * t - 512:512 * t], T.YC[5:128:16, :], [v("YC")], [])
+            dma("Y", "d3", T.yc[:, 512 * t - 512:512 * t], T.NW[5:128:16, :], [v("NW")], [])
         act(v("NR"), ind(v("NW"), v("JJ")))
         to_list(v("p7", 0, 32), "FC", "NR")
         cp(v("Hs"), v("p7", 0, 32))
@@ -538,9 +628,8 @@ def rank_program(g, core, T, topo):
         tt(v("a3"), v("Os"), v("n4"), A.add)
         tt(v("w3"), v("w1"), v("w2"), A.mult)
         tt(v("idx1", 0, 32), v("w3"), v("a3"), A.add)
-        ts(v("ZRp"), ind(zr, v("PL", 0, NA)), M1, A.add, M1, A.subtract)
-        mm(v("p3", 0, 96), v("RU"), v("ZRp"))
-        mm(v("p3", 96, 192), v("RV"), v("ZRp"))
+        mm(v("p3", 0, 96), v("RU"), zr)
+        mm(v("p3", 96, 192), v("RV"), zr, True, True, True)
         for j in (0, 1):
             ts(v("ua", 96 * j, 96 * j + 96), v("p3", 96 * j, 96 * j + 96), col(CU + j), A.add)
         ts(v("ub"), v("ua"), 4095, A.bitwise_and)
@@ -554,29 +643,28 @@ def rank_program(g, core, T, topo):
         tt(v("R2", 0, 192, 2), v("T1a"), v("ub", 0, 96), A.add)
         ts(v("R2", 1, 192, 2), v("Xb"), -2048.0, A.add)
         for q in range(16):
-            mm(v("p0", 0, 12), slid("F15", q), v("R2", 12 * q, 12 * q + 12), q == 0, q == 15, q > 0)
+            mm(v("p0", 0, 12), slid("F15", q), v("R2", 12 * q, 12 * q + 12), q == 0, q == 15, q % 4 > 0)
         cp(v("G0", 4, 36, 6), v("p0", 0, 12, 2))
         cp(v("G1", 4, 36, 6), v("p0", 1, 12, 2))
-        if not last:
-            act(v("t1"), zr, AF.Identity, scale=col(EA), bias=col(EG))
-            ts(v("zn"), zr, M1, A.add, M1, A.subtract)
-            act(v("t2"), v("zn"), scale=col(EB))
-            tt(v("Tw", 0, 96), v("t1"), v("t2"), A.add)
-        act(v("U", 0, 96), v("ior", 0, 96), AF.Identity, scale=0.0, bias=col(TMP + 22))
-        for k in range(4):
-            z = v("z16", 384 * k, 384 * k + 384)
-            act(z, ind(v("ZRp"), v("ZL", 24 * k, 24 * k + 24)))
-            df, ab = v("DF%d" % (k % 3), 0, 384), v("AA", 384 * k, 384 * k + 384)
+        act(v("U", e0, e0 + 96), v("ior", 0, 96), AF.Identity, scale=0.0, bias=col(TMP + 22))
+        for m in range(16):
+            if not last:
+                behind.append(v("TS"))
+            act(v("z16", m, 1536, 16), zr)
+        for k, (a, b) in enumerate(zip(QA, QA[1:])):
+            w = 96 * (b - a)
+            z = v("z16", 96 * a, 96 * b)
+            df, ab = v("DF%d" % (k % 3), 0, w), v("AA", 96 * a, 96 * b)
             if k in SA:
-                act(v("GS", 0, 384), ind(stones, v("HA", 24 * k, 24 * k + 24)))
-                mm(v("p4", 0, 384), v("ID"), v("GS", 0, 384), True, False)
-                mm(v("p4", 0, 384), v("NI"), z, False, True)
-                act(ab, v("p4", 0, 384), AF.Abs)
+                act(v("GS", 0, w), ind(stones, v("HA", 6 * a, 6 * b)))
+                mm(v("p4", 0, w), v("ID"), v("GS", 0, w), True, False)
+                mm(v("p4", 0, w), v("NI"), z, False, True, True)
+                act(ab, v("p4", 0, w), AF.Abs)
             else:
-                tt(df, ind(stones, v("HA", 24 * k, 24 * k + 24)), z, A.subtract)
+                tt(df, ind(stones, v("HA", 6 * a, 6 * b)), z, A.subtract)
                 act(ab, df, AF.Abs)
-            for q in range(4 * k, 4 * k + 4):
-                mm(v("p5", 0, 96), slid("FD", q), v("AA", 96 * q, 96 * q + 96), q == 0, q == 15, q % 4 > 0)
+            for q in range(a, b):
+                mm(v("p5", 0, 96), slid("FD", q), v("AA", 96 * q, 96 * q + 96), q == 0, q == 15, q > a)
         scan(v("KE", 0, 96), v("DA", 0, 96), v("p5", 0, 96), 0.0, A.add, A.min)
         scan(v("KE", 96, 192), v("DB", 0, 96), v("p5", 0, 96), 0.0, A.add, A.min)
         ts(v("k6", 0, NA), v("KE", 15, 96, 16), thr, A.is_ge, -8192.0, A.mult)
@@ -585,22 +673,34 @@ def rank_program(g, core, T, topo):
         for b in range(NA):
             ts(v("RX", 80 - 16 * b, 96 - 16 * b), v("qr"), v("ga1", b, b + 1), A.mult)
         mm(v("p1", 0, 96), v("BD"), v("RX"))
-        ts(v("ga2", 0, NA), v("ga1", 0, NA), 2048.0 + E, A.add)
+        mm(v("p3", 0, 96), v("BD"), v("RX"))
+        ts(v("ga3", 0, NA), v("ga1", 0, NA), -8192.0, A.mult)
+        ts(v("ga2", 0, NA), v("ga1", 0, NA), 2048.0 + E - e0, A.add)
         tt(v("gm", 0, NA), v("ga2", 0, NA), v("tcq", 0, NA), A.max)
         for b in range(NA):
             o = 8 * b * (b + 1)
-            ts(v("NE", o, o + 16 * b + 16), v("p1", 80 - 16 * b, 96), v("ga1", b, b + 1), A.not_equal, 8192.0, A.mult)
-        scan(v("SC", 0, 336), v("NE", 0, 336), v("MK", 0, 336), 0.0, A.min, A.max)
-        tt(v("ga"), ind(v("SC", 0, 1152), v("EN", 0, 1)), v("gm"), A.min)
+            if b in (0, 1, 5):
+                ts(v("NE", o, o + 16 * b + 16), v("p1", 80 - 16 * b, 96), v("ga1", b, b + 1), A.not_equal, 8192.0, A.mult)
+            else:
+                act(v("NE", o, o + 16 * b + 16), v("p3", 80 - 16 * b, 96), AF.Abs, scale=8192.0, bias=v("ga3", b, b + 1))
+        scan(v("SC", 0, 336), v("NE", 0, 336), v("MA", 0, 336), 0.0, A.min, A.max)
+        tt(v("ga"), ind(v("SC", 0, 336), v("EN", 2, 3)), v("gm"), A.min)
         glu = v("glu", 0, NA)
         cp(glu, v("ga", 0, NA))
         if not last:
-            cp(v("SB"), ind(v("Tw", 0, E + S), glu))
+            cp(v("SB"), ind(v("Tw", e0, E + S), glu))
             send("at%d" % t, "ly", asker, v("Tw", E + S + 96 * t, E + S + 96 * t + 96), v("SB"))
-        act(v("SU"), ind(v("U", 0, E + S), glu))
+        act(v("SU"), ind(v("U", e0, E + S), glu))
         send("au%d" % t, "lx", asker, v("UP", 96 * t, 96 * t + 96), v("SU"))
         if not last:
-            cp(ind(v("U", 0, E + S), glu), v("L255"))
+            cp(ind(v("U", e0, E + S), glu), v("L255"))
+            behind.append(v("SB"))
+            mm(v("p3", 0, 32), v("ON"), v("pw", 1, 33))
+            op("V", lambda: g.vector.tensor_reduce(_(v("Pf")), _(v("p3", 0, 32)), AxisListType.X, A.add), v("Pf"), [v("p3", 0, 32)])
+            cp(v("Pi"), v("Pf"))
+            ts(v("Pj"), v("Pi"), 63, A.bitwise_and)
+            tt(col(TMP), col(TH), v("Pj"), A.add)
+            ts(col(THR + (t + 1) % 2), col(TMP), 4096.0, A.mult, -3968.0, A.add)
         else:
             for k in range(16):
                 x, y = v("U", E + 256 * k, E + 256 * k + 256), v("UO", E + 256 * k, E + 256 * k + 256)
@@ -609,10 +709,9 @@ def rank_program(g, core, T, topo):
                 else:
                     act(y, x, AF.Identity, bias=col(C256))
             ms(v("L255"), 255.0)
-            cp(ind(v("UO"), glu), v("L255"))
-            for k in range(4):
-                y = v("UO", E + 1024 * k, E + 1024 * k + 1024)
-                dma("S" if k % 2 else "Y", "d4", T.yu[:, 1024 * k:1024 * k + 1024], y[0], [y], [], 3.0 + k)
+            cp(ind(v("UO", e0, E + S), glu), v("L255"))
+            y = v("UO", E, E + S)
+            dma("Y", "d4", T.yu[:, 0:S], y[0], [y], [], 6.0)
 
     flags(R - 1, True)
     tt(v("yo"), idx, v("w4"), A.subtract)
@@ -640,7 +739,7 @@ def rank_program(g, core, T, topo):
         c["tail"] = c["cost"] + c["late"]
     for n in range(len(calls) - 1, -1, -1):
         for k, wait in calls[n]["pre"].items():
-            calls[k]["tail"] = max(calls[k]["tail"], calls[k]["cost"] + wait + calls[n]["tail"])
+            calls[k]["tail"] = max(calls[k]["tail"], calls[k]["cost"] + calls[k]["urge"] + wait + calls[n]["tail"])
     for c in calls:
         c["post"] = {}
     for n, c in enumerate(calls):
@@ -652,6 +751,7 @@ def rank_program(g, core, T, topo):
         for n in order:
             c = calls[n]
             t0 = max([at[k] + calls[k]["cost"] + wait for k, wait in c[side].items()] + [c["late"] if side == "post" else 0.0])
+            t0 += c["urge"] if side == "post" else 0.0
             line = busy[c["q"]]
             i = len(line)
             while i and line[i - 1][1] > t0:
@@ -670,9 +770,10 @@ def rank_program(g, core, T, topo):
         if k < PASSES:
             back = place(sorted(every, key=lambda n: (-at[n] - calls[n]["cost"], -n)), "post")
             key = {n: -back[n] - calls[n]["cost"] for n in every}
-    ORDER.update(at)
+    if not ORDER:
+        ORDER.update(improve(calls, at))
     for n in every:
-        calls[n]["at"] = at[n]
+        calls[n]["at"] = ORDER[n]
 
     count, known, snaps, rec = {}, {q: {} for q in Q}, {}, {}
 
@@ -703,7 +804,8 @@ def rank_program(g, core, T, topo):
 
     for t in range(R):
         asker, lender = T.cores[(rank - 1 - t) % 8], T.cores[(rank + 1 + t) % 8]
-        for sem, src, ws in (("az%d" % t, asker, v("ZR%d" % t)), ("at%d" % t, lender, v("Tw", E + S + 96 * t, E + S + 96 * t + 96)), ("au%d" % t, lender, v("UP", 96 * t, 96 * t + 96))):
+        for sem, src, ws in (("az%d" % t, asker, v("ZR%d" % t)), ("at%d" % t, lender, v("Tw", E + S + 96 * t, E + S + 96 * t + 96)), ("au%d" % t, lender, v("UP", 96 * t, 96 * t + 96)),
+                             ("ae%d" % t, asker, v("Tw", 128 - 128 * t, 224 - 128 * t))):
             if sem in SEMAPHORES:
                 count["A" + sem] = len(topo.engines(src, core)[:8])
                 note("A" + sem, count["A" + sem], [], ws[1], {})

@@ -1,22 +1,34 @@
 from concourse.mybir import AluOpType, ActivationFunctionType, AxisListType
 
 NB, NA, S, W, R, E = 32, 6, 4096, 4384, 3, 256
-SG = {1: 32, 3: 32, 5: 32}
-NAB = 4
+SG = {3: 32, 4: 32, 5: 32, 6: 20}
+SUMS = (0, 1, 2, 3, 4, 5, 6, 7)
+LISTS = (11, 8, 0, 12, 13, 14, 9, 1, 10, 2, 3, 4, 5, 6, 7, 15)
+SP = ()
+NAB = 8
 LAST = 22
-QA = (0, 5, 8, 13, 16)
+QA = (0, 3, 6, 11, 14, 16)
 SA = (1,)
-N1 = 4
+N0 = 2
+PART = 16
+UV = (2, 5, 8, 11, 13, 15)
+AFTER = (0, 0, 1, 2)
+N1 = 7
+UL = (0, 1280, 2560, 3584, 4096)
+HS = 10
 PASSES = 1
 U1 = 2.0
 U2 = 2.0
+U3 = 0.5
+U4 = 1.0
 FIRST = 2.0
 BC = 4
+BATCH = (8, 6, 2, 0)
 RUN = 8 * BC * (BC + 1)
 F, B, I, H, U16 = "float32", "bfloat16", "int32", "float16", "uint16"
 M1, M128, M256, M4096 = 1.5 * 2 ** 23, 1.5 * 2 ** 30, 1.5 * 2 ** 31, 1.5 * 2 ** 35
 SCRATCH, PACK, PACKED = {}, {}, {}
-SEMAPHORES = ["sv", "ss", "sp", "sg", "d0", "d1", "d2", "d3", "d4", "d5", "d6", "dt", "lz", "ly", "lx", "lw"] + ["du%d" % t for t in range(4)]
+SEMAPHORES = ["sv", "ss", "sp", "sg", "d0", "d1", "d2", "d3", "d4", "d5", "d6", "dt", "lz", "ly", "lx", "lw"] + ["du%d" % t for t in range(4)] + ["da%d" % t for t in range(len(SG))]
 for _t in range(R):
     SEMAPHORES += ["az%d" % _t, "au%d" % _t] + (["at%d" % _t, "ae%d" % _t] if _t < R - 1 else [])
     SCRATCH["ZR%d" % _t] = ("sbuf", [128, 96], B)
@@ -26,37 +38,37 @@ for _n in range(8):
     SCRATCH["p%d" % _n] = ("psum", [128, 512], F)
 for _w, _d, _s in (
         (E + W, F, "U"), (E + W, B, "Tw"), (E + S, B, "UO"), (288, B, "UP UQ"), (512, I, "C8 X X2"), (512, H, "c16"), (2048, B, "E1"), (2064, B, "Y"),
-        (2048, H, "KD"), (2048, F, "ZS TS"), (1024, F, "KAB"), (512, F, "ior NW LV Zf Tf DA DB JV"), (2304, B, "NE SC"), (576, B, "MA"), (128, F, "la"), (48, F, "nlo"), (1024, F, "JW"),
-        (512, B, "DM GA GB Z GS NR FG NG DF0 DF1 DF2"), (512, H, "JS"), (1536, B, "z16 AA"), (512, U16, "HL"), (192, H, "H0 H1 R2"), (192, F, "hr KE"), (192, I, "ua ub"),
-        (144, F, "io144"), (144, B, "B0 B8 FD FC FO FJ F0 F15 IL IH"), (144, H, "WU WV WA WB"), (128, I, "uva uv"), (128, H, "u16"), (128, H, "RU RV"), (128, B, "BD BY ID NI GE LT ON ZM"),
-        (128, F, "io8 iox BF SH1 SH2 rep x1 x2"), (96, F, "T1a"), (96, I, "PRa kua qa Xa Xb"), (96, U16, "HA ZL"), (96, B, "ZB TB SB SU L255"), (96, H, "RX"),
+        (2048, H, "KD"), (2048, F, "ZS TS"), (1024, F, "KAB"), (512, F, "ior NW LV Zf Tf DA DB JV"), (RUN * (NB + 16) // BC, B, "NE SC"), (RUN * 16 // BC, B, "MK"), (576, B, "MA"), (512, B, "NZ GS0 GS1 GS2 GS3 GS4"), (128, F, "la"), (48, F, "nlo"), (1024, F, "JW"),
+        (512, B, "DM GA GB Z GS NR FG NG DF0 DF1 DF2 DF3 DF4"), (512, H, "JS"), (1536, B, "z16 AA"), (512, U16, "HL"), (192, H, "R2"), (192, F, "KE"), (288, I, "ua ub"), (HS * NB, F, "H0 H1 hr"), (HS * NA, F, "G0 G1 gr"), (16, I, "kw"), (16, F, "kx"), (1, I, "ci"),
+        (144, F, "io144"), (144, B, "B0 B8 FD FC FO FJ F0 F15 IL IH"), (144, H, "WU WV WA WB"), (128, I, "uva uv"), (128, H, "u16"), (128, H, "RU RV RK"), (128, B, "BD BY ID NI GE LT ON ZM"),
+        (128, F, "io8 iox BF SH1 SH2 rep x1 x2"), (96, F, "QR"), (96, I, "PRa kua qa Xa Xb"), (96, U16, "HA ZL"), (96, B, "ZB TB SB SU L255"), (96, H, "RX"),
         (33, B, "pw"), (33, H, "pn"),
         (2, I, "pi pq hwi"), (1, I, "kmi thi Pi Pj ei"), (1, F, "pf qf gf kmf thf e1 e2 e3 e4 Pf"), (2, F, "hwf hwg hws hwm"), (4, U16, "EN"),
-        (16, F, "io16 qm qr kq KM KS0 KS dA dB dC ga gm mq"), (16, I, "ki kj ka kb"), (64, F, "rr"), (36, H, "G0 G1"), (36, F, "gr"), (33, F, "idx1"),
-        (48, F, "col"), (32, F, "tc tcq tc512 nt1024 nrt c16f tcd W40 W4 on uf vf nf OF lf hx0 r2 x2s hx nh n0 Cf Cb cw ee ec mu rc pj pj2 fo "
-                                "a1 a2 a3 a4 a5 dd Os Js d0 df fs jt jf pl n4 w1 w2 w3 w4 yo"),
-        (32, I, "PR qi f3 fi nx Ci"), (32, H, "qh hh"), (8, H, "ha"), (32, B, "wv Dh Dl Ch Cl"), (32, U16, "OFu lou fou ngu Hs JJ"),
-        (8, U16, "glu PL"), (64, U16, "CL"), (8, I, "pd"), (12, F, "ra"), (8, F, "k6 k7 s2 s3 ga1 ga2 ga3 gb pp")):
+        (16, F, "io16 qm qr kq KM KS0 KS dA dB dC ga gm mq"), (16, I, "ki kj ka kb"), (64, F, "rr"), (33, F, "idx1"),
+        (48, F, "col"), (32, F, "tc tcq tc512 nt1024 nrt c16f tcd W40 W4 on uf vf nf OF lf hx nh n0 Ca Cf Cb cw ee ec mu rc pj pj2 fo "
+                                "a1 a2 a3 a4 a5 dd"), (64, F, "Os Js d0 df pl n4 w1 w2 w3 w4 a6 yi yo"),
+        (32, I, "PR qi f3 fi nx Ci"), (32, H, "qh hh uh"), (8, H, "ha"), (32, B, "wv Dh Dl Ch Cl"), (32, U16, "OFu lou fou ngu Hs JJ"),
+        (8, U16, "glu PL RL"), (64, U16, "CL"), (8, I, "pd"), (12, F, "ra"), (8, F, "k6 k7 s2 s3 ga1 ga2 ga3 gb pp")):
     for _n in _s.split():
-        if _w <= 64 and _n not in ("hwi", "kmi", "thi", "yo"):
+        if _w <= 144 and _n not in ("hwi", "kmi", "thi", "yo"):
             _k = "pk" + _d
             PACK[_n] = (_k, PACKED.get(_k, 0), _w)
-            PACKED[_k] = PACKED.get(_k, 0) + (_w + 7) // 8 * 8
+            PACKED[_k] = PACKED.get(_k, 0) + (_w + 15) // 16 * 16
         else:
             SCRATCH[_n] = ("sbuf", [128, _w], _d)
 for _k, _w in PACKED.items():
     SCRATCH[_k] = ("sbuf", [128, _w], _k[2:])
 
-CYC, HOP, FAR = 0.83e-3, 0.17, 2.4
+CYC, HOP, FAR = 0.83e-3, 0.18, 1.7
 ORDER = {}
-PACE = ((1.0, 1.0), (1.3, 1.35), (1.0, 0.7))
-TRIES, HEAT = 3000, 0.15
+PACE = ((1.0, (1, 1, 1), 1.0, 0.0), (1.3, (1, 1.3, 1.6), 1.5, 0.03), (1.0, (1, 0.7, 0.5), 0.6, 0.03), (1.2, (1, 0.75, 1.4), 1.0, 0.0))
+TRIES, HEAT = 13000, 0.05
 
 
 def improve(calls, at):
     every = range(len(calls))
-    post = [list(c["post"].items()) for c in calls]
-    costs = [[c["cost"] * (f if c["kind"] == "C" else 1) * (x if c["ind"] else 1) for c in calls] for f, x in PACE]
+    posts = [[[(k, w and w + hop + (far - 1 if c["kind"] == "R" else min(far - 1, 0) * 0.7) * c["late"]) for k, w in c["post"].items()] for c in calls] for f, x, far, hop in PACE]
+    costs = [[c["cost"] * (f if c["kind"] == "C" else 1) * x[c["ind"]] for c in calls] for f, x, far, hop in PACE]
     prev, nxt, tail = [None] * len(calls), [None] * len(calls), {}
     for n in sorted(every, key=lambda n: (at[n], n)):
         a = prev[n] = tail.get(calls[n]["q"])
@@ -64,20 +76,28 @@ def improve(calls, at):
             nxt[a] = n
         tail[calls[n]["q"]] = n
 
-    def walk(cost):
-        left = [len(calls[n]["pre"]) + (prev[n] is not None) for n in every]
+    def walk(cost, post):
+        left = [d + (p is not None) for d, p in zip(deg, prev)]
         head, why, todo, end, last = [0.0] * len(calls), [None] * len(calls), [n for n in every if not left[n]], 0.0, None
-        while todo:
-            n = todo.pop()
+        for n in todo:
             e = head[n] + cost[n]
-            if e + calls[n]["late"] > end:
-                end, last = e + calls[n]["late"], n
-            for k, w in post[n] if nxt[n] is None else post[n] + [(nxt[n], 0.0)]:
+            if e + late[n] > end:
+                end, last = e + late[n], n
+            for k, w in post[n]:
                 if e + w > head[k]:
                     head[k], why[k] = e + w, n
                 left[k] -= 1
                 if not left[k]:
                     todo.append(k)
+            k = nxt[n]
+            if k is not None:
+                if e > head[k]:
+                    head[k], why[k] = e, n
+                left[k] -= 1
+                if not left[k]:
+                    todo.append(k)
+        if len(todo) < len(calls):
+            return 1e9, head, []
         pairs = []
         while why[last] is not None:
             u = why[last]
@@ -86,31 +106,46 @@ def improve(calls, at):
             last = u
         return end, head, pairs
 
-    def swap(u, w):
-        a, b = prev[u], nxt[w]
-        prev[w], nxt[w], prev[u], nxt[u] = a, u, w, b
-        if a is not None:
-            nxt[a] = w
-        if b is not None:
-            prev[b] = u
+    def move(n, a, b):
+        for x, y in ((prev[n], nxt[n]), (a, n), (n, b)):
+            if x is not None:
+                nxt[x] = y
+            if y is not None:
+                prev[y] = x
 
-    def look():
-        runs = [walk(c) for c in costs]
-        return sum(r[0] / f for r, (f, x) in zip(runs, PACE)), runs
-    now = best = look()
+    def look(limit):
+        runs, total = [], 0.0
+        for cost, post, pace, least in zip(costs, posts, PACE, floor):
+            runs.append(walk(cost, post))
+            total += runs[-1][0] / pace[0]
+            if total + least > limit:
+                return 1e9, runs
+        return total, runs
+    deg, late, floor = [len(c["pre"]) for c in calls], [c["late"] for c in calls], [0.0] * len(PACE)
+    now = best = look(1e8)
     turn = 1
     for it in range(TRIES):
         turn = (turn * 1103515245 + 12345) % 2147483648
         pairs = now[1][it % len(costs)][2]
         if pairs:
             u, w = pairs[(turn >> 8) % len(pairs)]
-            swap(u, w)
-            new = look()
-            if new[0] < now[0] + HEAT * (1 - it / TRIES) * ((turn >> 4) % 16) / 8:
+            for k in range((1, 1, 2, 3, 5, 8)[(turn >> 16) % 6] - 1):
+                if turn & 64 and prev[u] is not None and calls[prev[u]]["kind"] != "F":
+                    u = prev[u]
+                elif not turn & 64 and nxt[w] is not None:
+                    w = nxt[w]
+            n, a, b = (w, prev[u], u) if turn & 64 else (u, w, nxt[w])
+            back = prev[n], nxt[n]
+            move(n, a, b)
+            parts = [r[0] / pace[0] - 1.0 for r, pace in zip(now[1], PACE)]
+            floor = [sum(parts[k + 1:]) for k in range(len(PACE))]
+            limit = now[0] + HEAT * (1 - it / TRIES) * ((turn >> 4) % 4) / 2
+            new = look(limit)
+            if new[0] <= limit:
                 now = new
                 best = min(best, now, key=lambda x: x[0])
             else:
-                swap(w, u)
+                move(n, back[0], back[1])
     return dict(enumerate(best[1][0][1]))
 
 
@@ -121,7 +156,7 @@ def rank_program(g, core, T, topo):
     A, AF = AluOpType, ActivationFunctionType
     Q = {"V": g.vector, "S": g.scalar, "P": g.tensor, "G": g, "Y": g.sync}
     SEM = {"V": "sv", "S": "ss", "P": "sp", "G": "sg"}
-    calls = []
+    calls, setup = [], []
 
     def is_bank(n):
         return n[0] == "p" and n[1:].isdigit()
@@ -160,7 +195,7 @@ def rank_program(g, core, T, topo):
             c["cost"] += cost
             return
         calls.append(dict(q=q, parts=[(f, rs, ws)], rs=list(rs) + [r for x in behind for r in x[1]], ws=ws, cost=cost, kind=kind, sem=sem, late=late, far=far, urge=sum(urge),
-                          ind=any(x[4] for x in list(reads) + list(writes) if isinstance(x, tuple))))
+                          ind=2 if any(x[4] for x in writes) else 1 if any(x[4] for x in reads if isinstance(x, tuple)) else 0))
         del behind[:], urge[:]
 
     def _(x):
@@ -176,8 +211,14 @@ def rank_program(g, core, T, topo):
             cost = max(64, i[2] * (rate or (0.5 if all(x[3] for x in [o] + ins[:2] if isinstance(x, tuple) and x[2] > 1) else 1))) * CYC
         add(q, f, ins, [o] + list(more), cost)
 
+    def plain(x):
+        n = x[1][0][0]
+        return SCRATCH[PACK[n][0] if n in PACK else n][2] in (F, B) and x[0].shape[0] == 128
+
     def ts(o, i, s1, op0, s2=None, op1=None):
-        if op1 is None:
+        if setup and plain(o) and plain(i) and (op0, op1) in ((A.mult, None), (A.mult, A.add), (A.add, None)):
+            act(o, i, AF.Identity, s1 if op0 == A.mult else None, s2 if op0 == A.mult else s1)
+        elif op1 is None:
             op("V", lambda: g.vector.tensor_scalar(out=_(o), in0=_(i), scalar1=_(s1), scalar2=None, op0=op0), o, [i, s1])
         else:
             op("V", lambda: g.vector.tensor_scalar(out=_(o), in0=_(i), scalar1=_(s1), scalar2=_(s2), op0=op0, op1=op1), o, [i, s1, s2])
@@ -190,7 +231,10 @@ def rank_program(g, core, T, topo):
         op("V", lambda: g.vector.tensor_copy(out=_(o), in_=_(i)), o, [i])
 
     def ms(o, c):
-        op("V", lambda: g.vector.memset(_(o), c), o, [])
+        if setup and plain(o):
+            act(o, v("ior", 0, o[2]), AF.Identity, 0.0, c)
+        else:
+            op("V", lambda: g.vector.memset(_(o), c), o, [])
 
     def scan(o, a, b, init, op0, op1):
         op("V", lambda: g.vector.tensor_tensor_scan(_(o), _(a), _(b), _(init), op0, op1), o, [a, b, init])
@@ -208,6 +252,9 @@ def rank_program(g, core, T, topo):
 
     def iota(o, pattern, base, cm, flag=True):
         add("G", lambda: g.iota(_(o), pattern, base, cm, allow_small_or_imprecise_dtypes=True) if flag else g.iota(_(o), pattern, base, cm), [], [o], 0.13 + 2 * o[2] * CYC)
+
+    def pick(o, i, pattern, cmp, base, cm):
+        add("G", lambda: g.affine_select(_(o), _(i), pattern, cmp, 0.0, base, cm), [i], [o], 0.17 + 2 * o[2] * CYC)
 
     def dma(q, sem, out, in_, reads, writes, late=2.0, first=False):
         add(q, lambda: Q[q].dma_start(out, in_), reads, writes, 0.05, "F" if first else "D", sem, late)
@@ -233,32 +280,32 @@ def rank_program(g, core, T, topo):
         return (T["AB%d" % k][:, :, :, q], [("AB%d.0" % k, 0, NB, 1), ("AB%d.1" % k, 0, NB, 1)], 64, True, None)
 
     def to_list(ps, wt, row, dense=False):
-        for q in range(16):
-            mm(ps, slid(wt, q), v(row, 32 * q, 32 * q + 32) if dense else v(row, q, 512, 16), q == 0, q == 15, q > 0)
+        for q in range(0, 16, 1 + dense):
+            mm(ps, slid(wt, q), v(row, 32 * q, 32 * q + 64) if dense else v(row, q, 512, 16), q == 0, q == 15 - dense, q % PART > 0)
 
     P8 = slice(0, 8)
     LO, HI, C256, CN256, LAID, ZSC, ZBI, CU, CV, TH = 0, 1, 2, 3, 4, 5, 6, 7, 8, 9
-    THR, TMP, LSC, LBI, FSC, FBI, JBI, FILL, EA, EG, EB, WC, B0C = 10, 12, 13, 14, 15, 16, 17, 18, 19, 20, 21, 22, 23
+    THR, TMP, LSC, LBI, FSC, FBI, JBI, FILL, EA, EG, EB, WC, B0C, CK = 10, 12, 13, 14, 15, 16, 17, 18, 19, 20, 21, 22, 23, 24
 
     dma("Y", "d0", T.C8[0:8, :], T.c0[:, :], [], [v("C8")], 2.0, True)
     dma("S", "d1", T.hwi[:, :], T.hw[:, :], [], [v("hwi")], 2.2, True)
-    dma("S", "d1", T.kmi[:, :], T.km[:, :], [], [v("kmi")], 2.2, True)
+    dma("Y", "d1", T.kmi[:, :], T.km[:, :], [], [v("kmi")], 2.2, True)
     for k in range(16):
         lo = 8 * k
-        dma("S" if k % 2 else "Y", "d2", T.Tw[lo:lo + 8, E:E + S], T.tp[(lo ^ 8):(lo ^ 8) + 8, :], [], [v("Tw", E, E + S)] if k == 15 else [], 6.0, True)
-    dma("Y", "dt", T.thi[0:8, :], T.th[:, :], [], [v("thi")], 6.0, True)
-    for k in range(4):
-        x = v("UO", E + 1024 * k, E + 1024 * k + 1024)
-        dma("Y", "du%d" % k, x[0], T.us[:, 1024 * k:1024 * k + 1024], [], [x], 7.5 + 1.2 * k, True)
+        dma("S" if k % 2 else "Y", "d2", T.Tw[lo:lo + 8, E:E + S], T.tp[(lo ^ 8):(lo ^ 8) + 8, :], [], [v("Tw", E, E + S)] if k == 15 else [], 7.0, True)
+    for k, (a, b) in enumerate(zip(UL, UL[1:])):
+        x = v("UO", E + a, E + b)
+        dma("Y", "du%d" % k, x[0], T.us[:, a:b], [], [x], 7.2 + 5.6 * b / S, True)
 
     iota(v("pi"), [[0, 2]], 0, 1, False)
     iota(v("io144"), [[1, 144]], -16, 0)
     iota(v("io16"), [[1, 16]], 0, 0)
     iota(v("io8"), [[1, 8], [0, 16]], 0, 0)
-    iota(v("iox"), [[0, 8], [1, 16]], 0, 0)
     iota(v("tc"), [[16, 32]], 0, 0)
     iota(v("ior"), [[1, 512]], -256, 0)
     io128 = v("io144", 16, 144)
+    behind.extend([v("ior"), v("tc")])
+    add("G", lambda: g.dma_start(T.thi[0:8, :], T.th[:, :]), [], [v("thi")], 3.0, "D", "dt", 2.0)
     cp(v("pf"), v("pi", 0, 1))
     ts(v("pq", 0, 1), v("pi", 0, 1), 4, A.arith_shift_right)
     ts(v("pq", 1, 2), v("pi", 0, 1), 15, A.bitwise_and)
@@ -316,11 +363,12 @@ def rank_program(g, core, T, topo):
     tt(v("KS"), v("KS0"), v("KM"), A.add)
     for m in range(16):
         ts(mat("KD", m), v("ID"), v("KS", m, m + 1), A.mult)
+    setup.append(1)
     ts(v("FD"), v("B0"), 4096.0, A.mult)
-    tt(col(FILL), qm(2), qm(8), A.add)
-    tt(col(TMP), qm(0), qm(1), A.add)
+    tt(col(FILL), qm(2), qm(4), A.add)
+    tt(col(TMP), qm(5), qm(7), A.add)
     tt(col(WC), col(TMP), col(FILL), A.add)
-    ts(col(TMP + 20), qm(1), 4.0, A.mult, qm(0), A.add)
+    ts(col(TMP + 20), qm(1), 1.0 / 1024.0, A.mult)
     for name, wt in (("FC", col(WC)), ("FO", col(FILL)), ("FJ", col(TMP + 20)), ("F0", qm(0)), ("F15", qm(15))):
         act(v(name), v("B0"), scale=wt)
     ts(v("ki"), v("KM"), -1.0, A.mult, v("KM", 15, 16), A.add)
@@ -336,9 +384,11 @@ def rank_program(g, core, T, topo):
         while w < 512:
             act(v(D, w, 2 * w), v(D, 0, w))
             w *= 2
+    ms(v("on"), 1.0)
     for a, b, n in (("H0", "H1", NB), ("G0", "G1", NA)):
-        for name, step, c in ((a, 0, 0.0), (a, 1, 1.0), (a, 2, 64.0), (a, 3, 1.0), (a, 5, 1.0), (b, 1, -1280.0), (b, 3, -1280.0), (b, 5, 0.5)):
-            ts(v(name, step, 6 * n, 6), v("tc", 0, n), 0.0, A.mult, c, A.add)
+        act(v(a, 0, HS * n), v("ior", 0, HS * n), AF.Identity, scale=0.0, bias=v("on", 0, 1))
+        for name, step, c in ((a, 0, 0.0), (a, 3, 64.0), (b, 1, M1), (b, 2, -M1), (b, 4, M1), (b, 5, -M1), (b, 7, M4096), (b, 8, -M4096)):
+            ms(v(name, step, HS * n, HS), c)
     ts(v("rep", p=P8), v("io8", p=P8), v("pf", p=P8), A.is_equal)
     cp(v("thf", p=P8), v("thi", p=P8))
     mm(v("p5", 0, 1), v("rep", p=P8), v("thf", p=P8))
@@ -346,7 +396,6 @@ def rank_program(g, core, T, topo):
     ts(col(THR), col(TH), 4096.0, A.mult, -3968.0, A.add)
     ts(v("x1"), io128, v("pf"), A.is_le)
     tt(v("GE"), v("x1"), v("BD"), A.mult)
-    ms(v("on"), 1.0)
     tt(v("LT"), v("BD"), v("GE"), A.subtract)
     ms(v("ON"), 1.0)
     ts(v("tcq"), v("tc"), v("qf"), A.add)
@@ -356,14 +405,10 @@ def rank_program(g, core, T, topo):
         cp(v("tcd", BC * k, BC * k + BC), v("tcq", 0, BC))
     ts(v("W40"), v("tcq"), 510.0, A.is_equal, 5112.0, A.mult)
     ts(v("W4"), v("W40"), 4.0, A.add)
-    ts(v("x1"), v("iox"), 0.0, A.is_equal)
-    ts(v("x2"), v("iox"), 3.0, A.is_equal)
-    tt(v("x1"), v("x1"), v("x2"), A.add)
-    tt(v("BY"), v("x1"), v("BD"), A.mult)
     ms(v("Y", 0, 16), 0.0)
-    for q in range(16):
-        act(mat("E1", q), v("BD"), scale=qm(q))
-        act(mat("Y", q, -16), v("BY"), scale=qm(q))
+    iota(v("E1"), [[0, 2048]], 1, 0)
+    pick(v("E1"), v("E1"), [[-1, 16], [-16, 8], [0, 16]], A.is_equal, 0, 1)
+    pick(v("Y", 16, 2064), v("E1"), [[0, 128], [-1, 16]], A.is_ge, 1, 0)
     ts(col(LSC), qm(0), 2.0 ** -24, A.mult)
     ts(col(LBI), qm(0), 2.0 ** -16, A.mult, col(LAID), A.add)
     act(v("LV"), v("ior"), AF.Identity, scale=col(LSC), bias=col(LBI))
@@ -377,16 +422,25 @@ def rank_program(g, core, T, topo):
     ts(v("ga"), v("io16"), v("qf"), A.add)
     ts(v("mq"), v("ga"), 15.5, A.is_lt, 16384.0, A.mult)
     ts(v("qr"), v("ga"), 15.0, A.is_equal)
+    for b in range(NA):
+        act(v("QR", 16 * b, 16 * b + 16), v("qr"))
+    ts(v("RL", 0, NA), v("io16", 0, NA), -1.0, A.mult, NA - 1.0, A.add)
     for i in range(max(BC, NA)):
         o = 8 * i * (i + 1)
         act(v("MA", o, o + 16), v("mq"), AF.Identity, bias=v("tcq", i, i + 1))
         if i:
             act(v("MA", o + 16, o + 16 * i + 16), v("ior", 0, 16 * i), AF.Identity, scale=0.0, bias=v("tcq", i, i + 1))
-    for k, n in enumerate((BC, NA)):
-        ts(v("e1"), v("qf"), n - 1.0, A.min)
-        ts(v("e2"), v("e1"), 8.0, A.mult, 8.0, A.add)
-        ts(v("e3"), v("e1"), 2.0, A.add, v("e2"), A.mult)
-        ts(v("EN", 2 * k, 2 * k + 1), v("e3"), -1.0, A.add)
+    for k in range(16 // BC):
+        act(v("MK", RUN * k, RUN * k + RUN), v("MA", 0, RUN))
+    act(v("SC", RUN * NB // BC, RUN * (NB + 16) // BC), v("MK"))
+    ts(v("ei"), v("pq", 1, 2), BC - 1, A.bitwise_and)
+    tt(v("e4"), v("qf"), v("ei"), A.subtract)
+    ts(v("e4"), v("e4"), float(RUN) / BC, A.mult, -1.0, A.add)
+    ts(v("e1"), v("qf"), NA - 1.0, A.min)
+    for k, (x, o) in enumerate((("ei", v("e4")), ("e1", -1.0))):
+        ts(v("e2"), v(x), 8.0, A.mult, 8.0, A.add)
+        ts(v("e3"), v(x), 2.0, A.add, v("e2"), A.mult)
+        ts(v("EN", 2 * k, 2 * k + 1), v("e3"), o, A.add)
     ms(v("nlo", 32, 48), 0.0)
     ts(v("pd", 0, NA), v("tcq", 0, NA), 1.0 / 6.0, A.mult, -5.0 / 12.0, A.add)
     ts(v("pp", 0, NA), v("pd", 0, NA), -95.0, A.mult)
@@ -394,22 +448,21 @@ def rank_program(g, core, T, topo):
     tt(v("s3", 0, NA), v("s2", 0, NA), v("pp", 0, NA), A.add)
     cp(v("PL", 0, NA), v("s3", 0, NA))
     ms(v("U", E + S, E + W), 0.0)
-    for k in range(8):
-        x, y = v("U", E + 512 * k, E + 512 * k + 512), v("UO", E + 512 * k, E + 512 * k + 512)
-        if k == 7:
+    del setup[:]
+    for k in range(16):
+        x, y = v("U", E + 256 * k, E + 256 * k + 256), v("UO", E + 256 * k, E + 256 * k + 256)
+        if k in UV:
             ts(x, y, col(CN256), A.add)
         else:
             act(x, y, AF.Identity, bias=col(CN256))
 
-    def best(n, keys, d0, d1, hr, rr, r2, x2, off, outs):
-        ts(v(rr, 0, 2 * n), v(keys, 15, 32 * n, 16), M256, A.add, M256 + 1280.0, A.subtract)
+    def best(n, keys, d0, d1, hr, rr, outs):
+        ts(v(rr, 0, 2 * n), v(keys, 15, 32 * n, 16), M256, A.add, M256, A.subtract)
         for j in (0, 1):
-            tt(v(d1, 2 * j, 6 * n, 6), v(keys, 16 * n * j + 15, 16 * n * (j + 1), 16), v(rr, n * j, n * j + n), A.subtract)
-        scan(v(hr, 0, 6 * n), v(d0, 0, 6 * n), v(d1, 0, 6 * n), 0.0, A.mult, A.add)
-        ts(v(r2, 0, n), v(hr, 5, 6 * n, 6), M4096, A.add, M4096, A.subtract)
-        tt(v(x2, 0, n), v(hr, 5, 6 * n, 6), v(off, 0, n), A.add)
+            tt(v(d1, 3 * j, HS * n, HS), v(keys, 16 * n * j + 15, 16 * n * (j + 1), 16), v(rr, n * j, n * j + n), A.subtract)
+        scan(v(hr, 0, HS * n), v(d0, 0, HS * n), v(d1, 0, HS * n), 0.0, A.mult, A.add)
         for o in outs:
-            tt(v(o, 0, n), v(x2, 0, n), v(r2, 0, n), A.subtract)
+            tt(v(o, 0, n), v(hr, 6, HS * n, HS), v(hr, 9, HS * n, HS), A.subtract)
 
     def split(hi, lo, x):
         ts(v(hi), v(x), M128, A.add, M128, A.subtract)
@@ -427,13 +480,29 @@ def rank_program(g, core, T, topo):
             act(v("NG", 256, 512), ind(up, v("ngu", 16, 32)), AF.Relu, scale=-1.0 / 2048.0, bias=col(TMP + 21))
         else:
             act(v("NG"), ind(up, v("ngu")), AF.Relu, scale=-1.0 / 2048.0, bias=col(TMP + 21))
-        to_list(v("p7", 0, 32), "F0", "NG", dense)
-        tt(v("w4"), v("p7", 0, 32), v("n4"), A.mult)
+        n = 64 if dense else NB
+        to_list(v("p7", 0, n), "F0", "NG", dense)
+        if not dense:
+            behind.append(v("vf"))
+        tt(v("w4", 0, n), v("p7", 0, n), v("n4", 0, n), A.mult)
+    setup.append(1)
     ms(col(TMP + 21), -1.0)
     ms(col(TMP + 22), -4096.0)
     ms(v("gm"), 0.0)
     ms(col(TMP + 24), 2304.0)
     ms(col(TMP + 25), 1280.0)
+    ms(col(TMP + 27), 0.5)
+    ts(v("kw"), v("KM"), v("hwf", 0, 1), A.mult)
+    ts(v("kw"), v("kw"), 4095, A.bitwise_and)
+    ts(v("kx"), v("kw"), 2048.0, A.is_ge, -4096.0, A.mult)
+    tt(v("kx"), v("kx"), v("kw"), A.add)
+    for k in range(8):
+        ts(v("RK", 16 * k, 16 * k + 16), v("kx"), v("BF", 16 * k, 16 * k + 1), A.mult)
+    cp(v("ci"), col(CU))
+    ts(v("ci"), v("ci"), 4095, A.bitwise_and)
+    ts(v("ci"), v("ci"), v("kmf"), A.mult)
+    ts(v("ci"), v("ci"), 4095, A.bitwise_and)
+    cp(col(CK), v("ci"))
     ts(col(EA), col(LO), 255.0 / 256.0, A.mult, 1.0 / 256.0, A.add)
     ts(col(EG), col(LO), 257.0, A.mult, 1023.0, A.add)
     ts(col(TMP + 26), col(CU), col(LO), A.mult)
@@ -446,6 +515,7 @@ def rank_program(g, core, T, topo):
     for a in (96, 224):
         ms(v("Tw", a, a + 32), 0.0)
     ms(v("U", 0, E), 0.0)
+    del setup[:]
 
     for t in range(R):
         last = t == R - 1
@@ -461,6 +531,7 @@ def rank_program(g, core, T, topo):
         cp(v("GB"), ind(tops, v("CL", 32, 64)))
         tt(v("Z"), v("GA"), v("GB"), A.min)
         act(v("Zf"), v("Z"), AF.Identity, bias=col(TMP + 25))
+        act(v("NZ"), v("Z"), scale=-1.0)
         for k, (wt, z) in enumerate((("WA", "GA"), ("WB", "GB"))):
             for r in range(8):
                 mm(v("p0", 0, 64), slid(wt, r), v(z, r, 512, 8), k + r == 0, k + r == 8, r > 0)
@@ -472,10 +543,11 @@ def rank_program(g, core, T, topo):
         mm(v("p1", 0, 64), v("IL", 0, 128), v("u16", 1, 128, 2), False, True, True)
         mm(v("p1", 64, 96), v("IH", 16, 144), v("u16", 0, 64, 2), True, False, True)
         mm(v("p1", 64, 96), v("IH", 8, 136), v("u16", 1, 64, 2), False, True, True)
-        uh = v("H0", 4, 6 * NB, 6)
+        uh = v("uh")
         cp(uh, v("p1", 32, 64))
         ts(v("uf"), v("p1", 0, 32), 2048.0, A.add)
         ts(v("vf"), v("p1", 64, 96), 2048.0, A.add)
+        act(v("H0", 6, HS * NB, HS), v("p1", 32, 64))
         tt(v("PR"), v("uf"), v("vf"), A.mult)
         ts(v("qi"), v("PR"), 5, A.arith_shift_right, 4095, A.bitwise_and)
         ts(v("qh"), v("qi"), -2048.0, A.add)
@@ -483,7 +555,7 @@ def rank_program(g, core, T, topo):
             if lo:
                 mm(v(bank, 32 * lo, 32 * hi), v("ZM"), v("DM", 32 * lo, 32 * hi), True, False)
             for i in range(lo, hi):
-                mm(v(bank, 32 * i, 32 * i + 32), mat("KD", i // 2 + 8 * (i % 2)), uh, lo == 0, lo == 0, i % 4 > 0)
+                mm(v(bank, 32 * i, 32 * i + 32), mat("KD", LISTS[i]), uh, lo == 0, lo == 0, i % 4 > 0)
             for i in range(lo, hi if lo else 0):
                 mm(v(bank, 32 * i, 32 * i + 32), v("ID"), v("qh"), False, i == hi - 1, i % 4 > 0)
             if lo == 0:
@@ -491,13 +563,15 @@ def rank_program(g, core, T, topo):
                     tt(v("X", 32 * i, 32 * i + 32), v(bank, 32 * i, 32 * i + 32), v("qi"), A.add)
             else:
                 ts(v("X", 32 * lo, 32 * hi), v(bank, 32 * lo, 32 * hi), 2048.0, A.add)
-            ts(v("X2", 32 * lo, 32 * hi), v("X", 32 * lo, 32 * hi), 4095, A.bitwise_and)
-            cp(v("HL", 32 * lo, 32 * hi), v("X2", 32 * lo, 32 * hi))
-        ts(v("H1", 4, 6 * NB, 6), v("X2", 480, 512), -2048.0, A.add)
+            for a, b in ((lo, hi),) if lo else ((0, N0), (N0, hi)):
+                ts(v("X2", 32 * a, 32 * b), v("X", 32 * a, 32 * b), 4095, A.bitwise_and)
+                urge.append(0.0 if a else U4)
+                cp(v("HL", 32 * a, 32 * b), v("X2", 32 * a, 32 * b))
+        ts(v("H1", 6, HS * NB, HS), v("X2", 32 * LISTS.index(15), 32 * LISTS.index(15) + 32), -2047.5, A.add)
         if t:
             flags(t - 1, False)
-            tt(v("Cf"), idx, v("w4"), A.subtract)
-            tt(v("Ci"), idx, v("w4"), A.subtract)
+            tt(v("Cf"), idx, v("w4", 0, NB), A.subtract)
+            tt(v("Ci"), idx, v("w4", 0, NB), A.subtract)
         else:
             cp(v("Cf"), idx)
             cp(v("Ci"), idx)
@@ -517,46 +591,58 @@ def rank_program(g, core, T, topo):
         tt(v("fo"), v("fi"), v("pj2"), A.max)
         urge.append(U1)
         cp(v("fou"), v("fo"))
+        if t:
+            behind.append(v("SU"))
         act(v("JW", 0, 512), v("ior"), scale=0.0)
         act(ind(v("JW"), v("fou")), v("JV"), AF.Silu)
         urge.append(U2)
         scan(v("JS"), v("DM"), v("JW", 0, 512), 0.0, A.mult, A.max)
-        for dense in range(1 + last):
-            pj = v("p7", 160, 192)
-            to_list(pj, "FJ", "JS", dense)
-            ts(v("jt"), pj, 4096.0, A.is_ge, -4096.0, A.mult)
-            tt(v("jf"), v("jt"), pj, A.add)
-            if not dense:
-                ts(v("JJ"), v("jf"), -1024.0, A.add)
-            if dense == last:
-                ts(v("fs"), pj, 4096.0, A.is_ge)
-                ts(v("Js"), v("jf"), -1280.0, A.add)
+        n2 = 64 if last else NB
+        to_list(v("p7", 160, 192), "F0", "JS")
+        ts(v("JJ"), v("p7", 160, 192), -1024.0, A.add)
+        if last:
+            to_list(v("p7", 160, 224), "F0", "JS", True)
+        ts(v("Js", 0, n2), v("p7", 160, 160 + n2), -1280.0, A.add)
+        fs = v("p7", 224, 224 + n2)
+        to_list(fs, "FJ", "JS", last)
         ts(v("Cb"), v("Cf"), -base, A.add)
         split("Ch", "Cl", "Cf")
         tt(v("nrt"), v("rc"), v("nt1024"), A.mult)
         n = 0
         for k in range(8):
             for j in (1, 0):
-                o, cut = 64 * k + 32 * j, SG.get(k, 0) if j else 0
+                o, cut = 32 * LISTS.index(k + 8 * j), SG.get(k, 0) if j else 0
                 if cut:
                     w = 16 * cut
-                    act(v("GS", 0, w), ind(stones, v("HL", o, o + cut)))
-                    mm(v("p5", 0, w), v("ID"), v("GS", 0, w), True, False)
-                    mm(v("p5", 0, w), v("NI"), v("Z", 0, w), False, True)
-                    act(half(k % NAB, j, 0, cut), v("p5", 0, w), AF.Abs)
+                    i = sorted(SG).index(k)
+                    gs = v("GS%d" % i, 0, w)
+                    if i:
+                        behind.append(half(AFTER[i - 1] // 2, 1 - AFTER[i - 1] % 2))
+                    act(gs, ind(stones, v("HL", o, o + cut)))
+                    if k in SP:
+                        mm(v("p5", 0, w), v("ID"), gs, True, False)
+                        mm(v("p5", 0, w), v("NI"), v("Z", 0, w), False, True)
+                        act(half(k % NAB, j, 0, cut), v("p5", 0, w), AF.Abs)
+                    else:
+                        nz = v("NZ", 0, w)
+                        add("G", lambda gs=gs, nz=nz: g.dma_start(gs[0], nz[0], accum_op=A.add), [gs, nz], [gs], 1.0, "D", "da%d" % i, 3.5)
+                        act(half(k % NAB, j, 0, cut), gs, AF.Abs)
                 cuts = (cut, LAST, NB) if k == 7 and not j else (cut, NB) if cut < NB else ()
                 for a, b in zip(cuts, cuts[1:]):
-                    df = v("DF%d" % (n % 3), 16 * a, 16 * b)
+                    df = v("DF%d" % (n % 5), 16 * a, 16 * b)
+                    if a == LAST:
+                        behind.append(v("DF%d" % ((n - 1) % 5)))
                     n += 1
                     tt(df, ind(stones, v("HL", o + a, o + b)), v("Z", 16 * a, 16 * b), A.subtract)
                     act(half(k % NAB, j, a, b), df, AF.Abs)
+        for k in SUMS:
             for q in range(16):
                 mm(v("p4", k, 512, 8), slid("FD", q), both(k % NAB, q), q == 0, q == 15, q > 0)
         scan(v("KAB", 0, 512), v("DA"), v("p4"), 0.0, A.add, A.min)
         scan(v("KAB", 512, 1024), v("DB"), v("p4"), 0.0, A.add, A.min)
         behind.append(half(7 % NAB, 0))
         mm(v("p6"), v("ZM"), v("Z"), True, False)
-        rows("Ch", "Cl", 2, 5)
+        rows("Ch", "Cl", 2, 3)
         ts(v("nf"), v("KAB", 15, 512, 16), thr, A.is_ge)
         tt(v("pw", 1, 33), v("nf"), v("mu"), A.mult)
         tt(v("pn", 1, 33), v("nf"), v("nrt"), A.mult)
@@ -570,83 +656,89 @@ def rank_program(g, core, T, topo):
         ts(v("ZB"), ind(v("ZS", 0, 96), v("PL", 0, NA)), M1, A.add, M1 + 1280.0, A.subtract)
         send("az%d" % t, "lz", lender, zr, v("ZB"), FIRST if t == 0 else 0.0)
         tt(v("lf"), v("rc"), v("nf"), A.is_gt)
-        ts(v("hx0"), v("lf"), 8192.0, A.mult, -8192.5, A.add)
-        best(NB, "KAB", "H0", "H1", "hr", "rr", "r2", "x2s", "hx0", ("hh", "hx"))
+        ts(v("H1", 9, HS * NB, HS), v("lf"), -8192.0, A.mult, 8191.5, A.add)
+        best(NB, "KAB", "H0", "H1", "hr", "rr", ("hh", "hx"))
         for q in range(16):
             mm(v("p2", 15 - q, 512 - q, -16), mat("E1", q), v("hh"), True, True, q > 0)
         ts(v("nh"), v("hx"), -8192.0, A.mult)
-        ts(v("n0"), v("hx"), 2048.0 + E - e0, A.add)
+        ts(v("n0"), v("hx"), 2047.0 + E - e0, A.add)
         tt(v("nlo", 0, 32), v("n0"), v("tcd"), A.max)
-        for k in range(NB // BC - 1, -1, -1):
-            for i in range(BC):
-                b, o = BC * k + i, RUN * k + 8 * i * (i + 1)
-                a0, a1 = 496 - 16 * b, 512 - 16 * BC * k
-                act(v("NE", o, o + a1 - a0), v("p2", a0, a1), AF.Abs, scale=8192.0, bias=v("nh", b, b + 1))
-            o, c0 = RUN * k, BC * k
-            scan(v("SC", o, o + RUN), v("NE", o, o + RUN), v("MA", 0, RUN), 0.0, A.min, A.max)
-            tt(v("la", 16 * k, 16 * k + 16), ind(v("SC", o, o + RUN), v("EN", 0, 1)), v("nlo", c0, c0 + 16), A.min)
-            cp(v("lou", c0, c0 + BC), v("la", 16 * k, 16 * k + BC))
-            cp(ind(v("U", e0, E + S), v("lou", c0, c0 + BC)), v("LV", 16 * c0, 16 * c0 + 16 * BC))
+        for hi, lo in zip(BATCH, BATCH[1:]):
+            for k in range(hi - 1, lo - 1, -1):
+                for i in range(BC):
+                    b, o = BC * k + i, RUN * k + 8 * i * (i + 1)
+                    a0, a1 = 496 - 16 * b, 512 - 16 * BC * k
+                    act(v("NE", o, o + a1 - a0), v("p2", a0, a1), AF.Abs, scale=8192.0, bias=v("nh", b, b + 1))
+            o, w, c0, c1 = RUN * lo, RUN * (hi - lo), BC * lo, BC * hi
+            scan(v("SC", o, o + w), v("NE", o, o + w), v("MK", 0, w), 0.0, A.min, A.max)
+            tt(v("la", 16 * lo, 16 * lo + 16), ind(v("SC", o, o + RUN * 16 // BC), v("EN", 0, 1)), v("nlo", c0, c0 + 16), A.min)
+            cp(v("lou", c0, c1), v("la", 16 * lo, 16 * lo + c1 - c0))
+            for k in range(hi - 1, lo - 1, -1):
+                cp(ind(v("U", e0, E + S), v("lou", BC * k, BC * k + BC)), v("LV", 16 * BC * k, 16 * BC * k + 16 * BC))
         if not last:
             act(v("Tf"), v("GA"), AF.Identity, scale=col(EA), bias=col(EG))
             behind.append(v("NE"))
             act(ind(v("TS"), v("OFu")), v("Tf"), AF.Silu)
             ts(v("TB"), v("TS", 0, 96), M1, A.add, M1 + 1024.0, A.subtract)
             send("ae%d" % t, "lw", lender, v("Tw", e0, e0 + 96), v("TB"))
-        tt(v("a1"), v("hx"), v("Cf"), A.subtract)
-        ts(v("a1"), v("a1"), 2048.0, A.add)
+        ts(v("Ca"), v("Cf"), -2047.0, A.add)
+        tt(v("a1"), v("hx"), v("Ca"), A.subtract)
         tt(v("a2"), v("a1"), v("lf"), A.mult)
         tt(v("a3"), v("OF"), v("Cb"), A.subtract)
         ts(v("a4"), v("OF"), 95.5, A.is_lt)
         tt(v("a5"), v("a3"), v("a4"), A.mult)
         tt(v("dd"), v("a2"), v("a5"), A.add)
         split("Dh", "Dl", "dd")
-        rows("Dh", "Dl", 0, 1)
+        rows("Dh", "Dl", 5, 7)
         if not last:
             behind.append(v("TS"))
         act(v("NW"), v("p6"))
         if t:
-            dma("Y", "d3", T.yc[:, 512 * t - 512:512 * t], T.NW[5:128:16, :], [v("NW")], [])
+            dma("Y", "d3", T.yc[:, 512 * t - 512:512 * t], T.NW[3:128:16, :], [v("NW")], [])
         act(v("NR"), ind(v("NW"), v("JJ")))
         to_list(v("p7", 0, 32), "FC", "NR")
         cp(v("Hs"), v("p7", 0, 32))
         ts(v("ngu"), v("p7", 0, 32), -base, A.add)
         pc = v("p7", 0, 32)
         if last:
-            pc = v("p6", 64, 96)
+            pc = v("p6", 64, 128)
             to_list(pc, "FC", "NR", True)
-        to_list(v("p6", 0, 32), "FO", "NR", last)
-        cp(v("Os"), v("p6", 0, 32))
-        tt(v("d0"), pc, v("Os"), A.subtract)
-        ts(v("pl"), pc, base, A.is_ge)
-        tt(v("df"), v("d0"), v("fs"), A.mult)
-        tt(v("n4"), v("pl"), v("df"), A.mult)
+        to_list(v("p6", 0, n2), "FO", "NR", last)
+        Os, Js, d0, df, pl, n4, w1, w2, w3, a6 = (v(x, 0, n2) for x in "Os Js d0 df pl n4 w1 w2 w3 a6".split())
+        cp(Os, v("p6", 0, n2))
+        tt(d0, pc, Os, A.subtract)
+        ts(pl, pc, base, A.is_ge)
+        tt(df, d0, fs, A.mult)
+        tt(n4, pl, df, A.mult)
         act(v("FG"), ind(v("U", E, E + W), v("Hs")), AF.Identity, scale=col(FSC), bias=col(FBI))
-        to_list(v("p2", 0, 32), "F0", "FG", last)
-        tt(v("w1"), v("p2", 0, 32), v("Js"), A.is_equal)
-        tt(v("w2"), v("df"), v("n4"), A.subtract)
-        tt(v("a3"), v("Os"), v("n4"), A.add)
-        tt(v("w3"), v("w1"), v("w2"), A.mult)
-        tt(v("idx1", 0, 32), v("w3"), v("a3"), A.add)
+        to_list(v("p2", 0, n2), "F0", "FG", last)
+        tt(w1, v("p2", 0, n2), Js, A.is_equal)
+        tt(w2, df, n4, A.subtract)
+        tt(a6, Os, n4, A.add)
+        tt(w3, w1, w2, A.mult)
+        tt(v("yi") if last else idx, w3, a6, A.add)
         mm(v("p3", 0, 96), v("RU"), zr)
         mm(v("p3", 96, 192), v("RV"), zr, True, True, True)
-        for j in (0, 1):
-            ts(v("ua", 96 * j, 96 * j + 96), v("p3", 96 * j, 96 * j + 96), col(CU + j), A.add)
-        ts(v("ub"), v("ua"), 4095, A.bitwise_and)
+        mm(v("p3", 192, 288), v("RK"), zr, True, True, True)
+        for j, c in enumerate((CU, CV, CK)):
+            ts(v("ua", 96 * j, 96 * j + 96), v("p3", 96 * j, 96 * j + 96), col(c), A.add)
+        ts(v("ub", 0, 192), v("ua", 0, 192), 4095, A.bitwise_and)
+        ts(v("ub", 192, 288), v("ua", 192, 288), 4095, A.bitwise_and)
         tt(v("PRa"), v("ub", 0, 96), v("ub", 96, 192), A.mult)
-        ts(v("kua"), v("ub", 0, 96), v("kmf"), A.mult)
-        ts(v("qa"), v("PRa"), 5, A.arith_shift_right)
-        tt(v("Xa"), v("kua"), v("qa"), A.add)
-        ts(v("Xb"), v("Xa"), 4095, A.bitwise_and)
+        ts(v("kua"), v("ub", 192, 288), 32.0, A.mult, -131072.0, A.add)
+        tt(v("Xa"), v("kua"), v("PRa"), A.add)
+        ts(v("Xb"), v("Xa"), 5, A.arith_shift_right, 4095, A.bitwise_and)
         cp(v("HA"), v("Xb"))
-        ts(v("T1a"), v("ub", 0, 96), 2048.0, A.is_ge, -4096.0, A.mult)
-        tt(v("R2", 0, 192, 2), v("T1a"), v("ub", 0, 96), A.add)
+        urge.append(U3)
+        ts(v("R2", 0, 192, 2), v("ub", 0, 96), -2048.0, A.add)
+        urge.append(U3)
         ts(v("R2", 1, 192, 2), v("Xb"), -2048.0, A.add)
         for q in range(16):
             mm(v("p0", 0, 12), slid("F15", q), v("R2", 12 * q, 12 * q + 12), q == 0, q == 15, q % 4 > 0)
-        cp(v("G0", 4, 36, 6), v("p0", 0, 12, 2))
-        cp(v("G1", 4, 36, 6), v("p0", 1, 12, 2))
-        act(v("U", e0, e0 + 96), v("ior", 0, 96), AF.Identity, scale=0.0, bias=col(TMP + 22))
+        ts(v("gb", 0, NA), v("p0", 0, 12, 2), 0.0, A.is_lt, 4096.0, A.mult)
+        ts(v("k7", 0, NA), v("p0", 0, 12, 2), -2048.0, A.add)
+        tt(v("G0", 6, HS * NA, HS), v("gb", 0, NA), v("k7", 0, NA), A.add)
+        act(v("G1", 6, HS * NA, HS), v("p0", 1, 12, 2), AF.Identity, bias=col(TMP + 27))
         for m in range(16):
             if not last:
                 behind.append(v("TS"))
@@ -654,28 +746,29 @@ def rank_program(g, core, T, topo):
         for k, (a, b) in enumerate(zip(QA, QA[1:])):
             w = 96 * (b - a)
             z = v("z16", 96 * a, 96 * b)
-            df, ab = v("DF%d" % (k % 3), 0, w), v("AA", 96 * a, 96 * b)
+            df, ab = v("DF%d" % k, 0, w), v("AA", 96 * a, 96 * b)
             if k in SA:
                 act(v("GS", 0, w), ind(stones, v("HA", 6 * a, 6 * b)))
-                mm(v("p4", 0, w), v("ID"), v("GS", 0, w), True, False)
-                mm(v("p4", 0, w), v("NI"), z, False, True, True)
+                mm(v("p4", 0, w), v("NI"), z, True, False)
+                mm(v("p4", 0, w), v("ID"), v("GS", 0, w), False, True)
                 act(ab, v("p4", 0, w), AF.Abs)
             else:
                 tt(df, ind(stones, v("HA", 6 * a, 6 * b)), z, A.subtract)
                 act(ab, df, AF.Abs)
             for q in range(a, b):
                 mm(v("p5", 0, 96), slid("FD", q), v("AA", 96 * q, 96 * q + 96), q == 0, q == 15, q > a)
+        behind.append(v("AA"))
+        act(v("U", e0, e0 + 96), v("ior", 0, 96), AF.Identity, scale=0.0, bias=col(TMP + 22))
         scan(v("KE", 0, 96), v("DA", 0, 96), v("p5", 0, 96), 0.0, A.add, A.min)
         scan(v("KE", 96, 192), v("DB", 0, 96), v("p5", 0, 96), 0.0, A.add, A.min)
-        ts(v("k6", 0, NA), v("KE", 15, 96, 16), thr, A.is_ge, -8192.0, A.mult)
-        ts(v("k7", 0, NA), v("k6", 0, NA), -0.5, A.add)
-        best(NA, "KE", "G0", "G1", "gr", "ra", "s2", "s3", "k7", ("ga1",))
-        for b in range(NA):
-            ts(v("RX", 80 - 16 * b, 96 - 16 * b), v("qr"), v("ga1", b, b + 1), A.mult)
+        ts(v("k6", 0, NA), v("KE", 15, 96, 16), thr, A.is_ge, 8192.0, A.mult)
+        ts(v("G1", 9, HS * NA, HS), v("k6", 0, NA), -0.5, A.add)
+        best(NA, "KE", "G0", "G1", "gr", "ra", ("ga1",))
+        tt(v("RX"), ind(v("ga1", 0, NA), v("RL", 0, NA)), v("QR"), A.mult)
         mm(v("p1", 0, 96), v("BD"), v("RX"))
         mm(v("p3", 0, 96), v("BD"), v("RX"))
         ts(v("ga3", 0, NA), v("ga1", 0, NA), -8192.0, A.mult)
-        ts(v("ga2", 0, NA), v("ga1", 0, NA), 2048.0 + E - e0, A.add)
+        ts(v("ga2", 0, NA), v("ga1", 0, NA), 2047.0 + E - e0, A.add)
         tt(v("gm", 0, NA), v("ga2", 0, NA), v("tcq", 0, NA), A.max)
         for b in range(NA):
             o = 8 * b * (b + 1)
@@ -714,8 +807,8 @@ def rank_program(g, core, T, topo):
             dma("Y", "d4", T.yu[:, 0:S], y[0], [y], [], 6.0)
 
     flags(R - 1, True)
-    tt(v("yo"), idx, v("w4"), A.subtract)
-    dma("Y", "d6", T.yc[:, 512 * R - 512:512 * R], T.yo[:, :], [v("yo")], [])
+    tt(v("yo"), v("yi"), v("w4"), A.subtract)
+    dma("Y", "d6", T.yc[:, 512 * R - 512:512 * R], T.yo[0:128:2, :], [v("yo")], [])
     ts(v("UQ"), v("UP"), col(C256), A.add, 0.0, A.max)
     dma("S", "d5", T.yu[:, S:W], T.UQ[:, :], [v("UQ")], [])
 

from concourse.mybir import AluOpType, ActivationFunctionType, AxisListType

NB, NA, S, W, R, E = 32, 6, 4096, 4384, 3, 256
SG = {3: 32, 4: 32, 5: 32, 6: 20}
SUMS = (0, 1, 2, 3, 4, 5, 6, 7)
LISTS = (11, 8, 0, 12, 13, 14, 9, 1, 10, 2, 3, 4, 5, 6, 7, 15)
SP = ()
NAB = 8
LAST = 22
QA = (0, 3, 6, 11, 14, 16)
SA = (1,)
N0 = 2
PART = 16
UV = (2, 5, 8, 11, 13, 15)
AFTER = (0, 0, 1, 2)
N1 = 7
UL = (0, 1280, 2560, 3584, 4096)
HS = 10
PASSES = 1
U1 = 2.0
U2 = 2.0
U3 = 0.5
U4 = 1.0
FIRST = 2.0
BC = 4
BATCH = (8, 6, 2, 0)
RUN = 8 * BC * (BC + 1)
F, B, I, H, U16 = "float32", "bfloat16", "int32", "float16", "uint16"
M1, M128, M256, M4096 = 1.5 * 2 ** 23, 1.5 * 2 ** 30, 1.5 * 2 ** 31, 1.5 * 2 ** 35
SCRATCH, PACK, PACKED = {}, {}, {}
SEMAPHORES = ["sv", "ss", "sp", "sg", "d0", "d1", "d2", "d3", "d4", "d5", "d6", "dt", "lz", "ly", "lx", "lw"] + ["du%d" % t for t in range(4)] + ["da%d" % t for t in range(len(SG))]
for _t in range(R):
    SEMAPHORES += ["az%d" % _t, "au%d" % _t] + (["at%d" % _t, "ae%d" % _t] if _t < R - 1 else [])
    SCRATCH["ZR%d" % _t] = ("sbuf", [128, 96], B)
for _n in range(NAB):
    SCRATCH["AB%d" % _n] = ("sbuf", [128, NB, 2, 16], B)
for _n in range(8):
    SCRATCH["p%d" % _n] = ("psum", [128, 512], F)
for _w, _d, _s in (
        (E + W, F, "U"), (E + W, B, "Tw"), (E + S, B, "UO"), (288, B, "UP UQ"), (512, I, "C8 X X2"), (512, H, "c16"), (2048, B, "E1"), (2064, B, "Y"),
        (2048, H, "KD"), (2048, F, "ZS TS"), (1024, F, "KAB"), (512, F, "ior NW LV Zf Tf DA DB JV"), (RUN * (NB + 16) // BC, B, "NE SC"), (RUN * 16 // BC, B, "MK"), (576, B, "MA"), (512, B, "NZ GS0 GS1 GS2 GS3 GS4"), (128, F, "la"), (48, F, "nlo"), (1024, F, "JW"),
        (512, B, "DM GA GB Z GS NR FG NG DF0 DF1 DF2 DF3 DF4"), (512, H, "JS"), (1536, B, "z16 AA"), (512, U16, "HL"), (192, H, "R2"), (192, F, "KE"), (288, I, "ua ub"), (HS * NB, F, "H0 H1 hr"), (HS * NA, F, "G0 G1 gr"), (16, I, "kw"), (16, F, "kx"), (1, I, "ci"),
        (144, F, "io144"), (144, B, "B0 B8 FD FC FO FJ F0 F15 IL IH"), (144, H, "WU WV WA WB"), (128, I, "uva uv"), (128, H, "u16"), (128, H, "RU RV RK"), (128, B, "BD BY ID NI GE LT ON ZM"),
        (128, F, "io8 iox BF SH1 SH2 rep x1 x2"), (96, F, "QR"), (96, I, "PRa kua qa Xa Xb"), (96, U16, "HA ZL"), (96, B, "ZB TB SB SU L255"), (96, H, "RX"),
        (33, B, "pw"), (33, H, "pn"),
        (2, I, "pi pq hwi"), (1, I, "kmi thi Pi Pj ei"), (1, F, "pf qf gf kmf thf e1 e2 e3 e4 Pf"), (2, F, "hwf hwg hws hwm"), (4, U16, "EN"),
        (16, F, "io16 qm qr kq KM KS0 KS dA dB dC ga gm mq"), (16, I, "ki kj ka kb"), (64, F, "rr"), (33, F, "idx1"),
        (48, F, "col"), (32, F, "tc tcq tc512 nt1024 nrt c16f tcd W40 W4 on uf vf nf OF lf hx nh n0 Ca Cf Cb cw ee ec mu rc pj pj2 fo "
                                "a1 a2 a3 a4 a5 dd"), (64, F, "Os Js d0 df pl n4 w1 w2 w3 w4 a6 yi yo"),
        (32, I, "PR qi f3 fi nx Ci"), (32, H, "qh hh uh"), (8, H, "ha"), (32, B, "wv Dh Dl Ch Cl"), (32, U16, "OFu lou fou ngu Hs JJ"),
        (8, U16, "glu PL RL"), (64, U16, "CL"), (8, I, "pd"), (12, F, "ra"), (8, F, "k6 k7 s2 s3 ga1 ga2 ga3 gb pp")):
    for _n in _s.split():
        if _w <= 144 and _n not in ("hwi", "kmi", "thi", "yo"):
            _k = "pk" + _d
            PACK[_n] = (_k, PACKED.get(_k, 0), _w)
            PACKED[_k] = PACKED.get(_k, 0) + (_w + 15) // 16 * 16
        else:
            SCRATCH[_n] = ("sbuf", [128, _w], _d)
for _k, _w in PACKED.items():
    SCRATCH[_k] = ("sbuf", [128, _w], _k[2:])

CYC, HOP, FAR = 0.83e-3, 0.18, 1.7
ORDER = {}
PACE = ((1.0, (1, 1, 1), 1.0, 0.0), (1.3, (1, 1.3, 1.6), 1.5, 0.03), (1.0, (1, 0.7, 0.5), 0.6, 0.03), (1.2, (1, 0.75, 1.4), 1.0, 0.0))
TRIES, HEAT = 13000, 0.05


def improve(calls, at):
    every = range(len(calls))
    posts = [[[(k, w and w + hop + (far - 1 if c["kind"] == "R" else min(far - 1, 0) * 0.7) * c["late"]) for k, w in c["post"].items()] for c in calls] for f, x, far, hop in PACE]
    costs = [[c["cost"] * (f if c["kind"] == "C" else 1) * x[c["ind"]] for c in calls] for f, x, far, hop in PACE]
    prev, nxt, tail = [None] * len(calls), [None] * len(calls), {}
    for n in sorted(every, key=lambda n: (at[n], n)):
        a = prev[n] = tail.get(calls[n]["q"])
        if a is not None:
            nxt[a] = n
        tail[calls[n]["q"]] = n

    def walk(cost, post):
        left = [d + (p is not None) for d, p in zip(deg, prev)]
        head, why, todo, end, last = [0.0] * len(calls), [None] * len(calls), [n for n in every if not left[n]], 0.0, None
        for n in todo:
            e = head[n] + cost[n]
            if e + late[n] > end:
                end, last = e + late[n], n
            for k, w in post[n]:
                if e + w > head[k]:
                    head[k], why[k] = e + w, n
                left[k] -= 1
                if not left[k]:
                    todo.append(k)
            k = nxt[n]
            if k is not None:
                if e > head[k]:
                    head[k], why[k] = e, n
                left[k] -= 1
                if not left[k]:
                    todo.append(k)
        if len(todo) < len(calls):
            return 1e9, head, []
        pairs = []
        while why[last] is not None:
            u = why[last]
            if u == prev[last] and u not in calls[last]["pre"] and calls[u]["kind"] != "F":
                pairs.append((u, last))
            last = u
        return end, head, pairs

    def move(n, a, b):
        for x, y in ((prev[n], nxt[n]), (a, n), (n, b)):
            if x is not None:
                nxt[x] = y
            if y is not None:
                prev[y] = x

    def look(limit):
        runs, total = [], 0.0
        for cost, post, pace, least in zip(costs, posts, PACE, floor):
            runs.append(walk(cost, post))
            total += runs[-1][0] / pace[0]
            if total + least > limit:
                return 1e9, runs
        return total, runs
    deg, late, floor = [len(c["pre"]) for c in calls], [c["late"] for c in calls], [0.0] * len(PACE)
    now = best = look(1e8)
    turn = 1
    for it in range(TRIES):
        turn = (turn * 1103515245 + 12345) % 2147483648
        pairs = now[1][it % len(costs)][2]
        if pairs:
            u, w = pairs[(turn >> 8) % len(pairs)]
            for k in range((1, 1, 2, 3, 5, 8)[(turn >> 16) % 6] - 1):
                if turn & 64 and prev[u] is not None and calls[prev[u]]["kind"] != "F":
                    u = prev[u]
                elif not turn & 64 and nxt[w] is not None:
                    w = nxt[w]
            n, a, b = (w, prev[u], u) if turn & 64 else (u, w, nxt[w])
            back = prev[n], nxt[n]
            move(n, a, b)
            parts = [r[0] / pace[0] - 1.0 for r, pace in zip(now[1], PACE)]
            floor = [sum(parts[k + 1:]) for k in range(len(PACE))]
            limit = now[0] + HEAT * (1 - it / TRIES) * ((turn >> 4) % 4) / 2
            new = look(limit)
            if new[0] <= limit:
                now = new
                best = min(best, now, key=lambda x: x[0])
            else:
                move(n, back[0], back[1])
    return dict(enumerate(best[1][0][1]))


def rank_program(g, core, T, topo):
    rank = T.rank_of(core)
    if rank is None:
        return
    A, AF = AluOpType, ActivationFunctionType
    Q = {"V": g.vector, "S": g.scalar, "P": g.tensor, "G": g, "Y": g.sync}
    SEM = {"V": "sv", "S": "ss", "P": "sp", "G": "sg"}
    calls, setup = [], []

    def is_bank(n):
        return n[0] == "p" and n[1:].isdigit()

    def v(name, lo=None, hi=None, step=1, p=None):
        buf, at, w = PACK[name] if name in PACK else (name, 0, SCRATCH[name][1][1])
        lo = 0 if lo is None else lo
        hi = w if hi is None else hi
        rows = slice(None) if p is None else p
        if step < 0:
            ap = T[buf][rows, hi - 1:(lo - 1 if lo else None):step]
        else:
            ap = T[buf][rows, at + lo:at + hi] if step == 1 else T[buf][rows, at + lo:at + hi:step]
        reg = (name, 0, 512, 1) if is_bank(name) else (name, lo, hi, step)
        return (ap, [reg], len(range(lo, hi, abs(step))), SCRATCH[buf][2] in (B, H, U16), None)

    def ind(win, off):
        return (win[0].indirect(off[0]), win[1], 16 * off[2], win[3], off[1])

    def hit(a, b):
        if a[1] >= b[2] or b[1] >= a[2]:
            return False
        return not (a[3] == b[3] and a[3] > 1 and (a[1] - b[1]) % a[3])

    behind = []
    urge = []

    def add(q, f, reads, writes, cost, kind="C", sem=None, late=0.0, far=None, join=False):
        rs = [r for x in reads if isinstance(x, tuple) for r in x[1]]
        rs += [r for x in list(reads) + list(writes) if isinstance(x, tuple) and x[4] for r in x[4]]
        ws = [r for x in writes for r in x[1]]
        if join:
            c = calls[-1]
            c["parts"].append((f, rs, ws))
            c["rs"] += [r for r in rs if r not in c["rs"]]
            c["cost"] += cost
            return
        calls.append(dict(q=q, parts=[(f, rs, ws)], rs=list(rs) + [r for x in behind for r in x[1]], ws=ws, cost=cost, kind=kind, sem=sem, late=late, far=far, urge=sum(urge),
                          ind=2 if any(x[4] for x in writes) else 1 if any(x[4] for x in reads if isinstance(x, tuple)) else 0))
        del behind[:], urge[:]

    def _(x):
        return x[0] if isinstance(x, tuple) else x

    def op(q, f, o, ins, rate=None, more=()):
        i = ins[0] if ins else o
        if o[4]:
            cost = 0.05 + 3.5 * o[2] * CYC
        elif i[4]:
            cost = 0.06 + 1.5 * i[2] * CYC
        else:
            cost = max(64, i[2] * (rate or (0.5 if all(x[3] for x in [o] + ins[:2] if isinstance(x, tuple) and x[2] > 1) else 1))) * CYC
        add(q, f, ins, [o] + list(more), cost)

    def plain(x):
        n = x[1][0][0]
        return SCRATCH[PACK[n][0] if n in PACK else n][2] in (F, B) and x[0].shape[0] == 128

    def ts(o, i, s1, op0, s2=None, op1=None):
        if setup and plain(o) and plain(i) and (op0, op1) in ((A.mult, None), (A.mult, A.add), (A.add, None)):
            act(o, i, AF.Identity, s1 if op0 == A.mult else None, s2 if op0 == A.mult else s1)
        elif op1 is None:
            op("V", lambda: g.vector.tensor_scalar(out=_(o), in0=_(i), scalar1=_(s1), scalar2=None, op0=op0), o, [i, s1])
        else:
            op("V", lambda: g.vector.tensor_scalar(out=_(o), in0=_(i), scalar1=_(s1), scalar2=_(s2), op0=op0, op1=op1), o, [i, s1, s2])

    def tt(o, a, b, op0):
        psum = is_bank(a[1][0][0]) or is_bank(b[1][0][0])
        op("V", lambda: g.vector.tensor_tensor(out=_(o), in0=_(a), in1=_(b), op=op0), o, [a, b], 1 if psum else 2)

    def cp(o, i):
        op("V", lambda: g.vector.tensor_copy(out=_(o), in_=_(i)), o, [i])

    def ms(o, c):
        if setup and plain(o):
            act(o, v("ior", 0, o[2]), AF.Identity, 0.0, c)
        else:
            op("V", lambda: g.vector.memset(_(o), c), o, [])

    def scan(o, a, b, init, op0, op1):
        op("V", lambda: g.vector.tensor_tensor_scan(_(o), _(a), _(b), _(init), op0, op1), o, [a, b, init])

    def act(o, i, func=AF.Copy, scale=None, bias=None):
        kw = {}
        if scale is not None:
            kw["scale"] = _(scale)
        if bias is not None:
            kw["bias"] = _(bias)
        op("S", lambda: g.scalar.activation(_(o), _(i), func, **kw), o, [i, scale, bias], 1)

    def mm(o, l, r, start=True, stop=True, join=False):
        add("P", lambda: g.tensor.matmul(_(o), _(l), _(r), start, stop), [l, r], [o], (1 if r[3] else 4) * max(64, r[2]) * CYC, join=join)

    def iota(o, pattern, base, cm, flag=True):
        add("G", lambda: g.iota(_(o), pattern, base, cm, allow_small_or_imprecise_dtypes=True) if flag else g.iota(_(o), pattern, base, cm), [], [o], 0.13 + 2 * o[2] * CYC)

    def pick(o, i, pattern, cmp, base, cm):
        add("G", lambda: g.affine_select(_(o), _(i), pattern, cmp, 0.0, base, cm), [i], [o], 0.17 + 2 * o[2] * CYC)

    def dma(q, sem, out, in_, reads, writes, late=2.0, first=False):
        add(q, lambda: Q[q].dma_start(out, in_), reads, writes, 0.05, "F" if first else "D", sem, late)

    def send(sem, lsem, dst, out, src, more=0.0):
        es = topo.engines(core, dst)[:8]
        rid, pid, se = topo.addr(dst)
        add("G", lambda: g.remote_dma(out[0], src[0], T.sem[sem], T.sem[lsem], pid, rid, sum(1 << k for k in es)), [src], [], 0.6, "R", (lsem, len(es)), FAR + more, out[1])

    def col(j):
        return v("col", j, j + 1)

    def mat(name, q, shift=0):
        return v(name, 128 * q - shift, 128 * q + 128 - shift)

    def slid(name, q, p=None):
        return v(name, 16 - q, 144 - q, p=p)

    def half(k, j, lo=0, hi=NB):
        return (T["AB%d" % k][:, lo:hi, j, :], [("AB%d.%d" % (k, j), lo, hi, 1)], 16 * (hi - lo), True, None)

    def both(k, q):
        return (T["AB%d" % k][:, :, :, q], [("AB%d.0" % k, 0, NB, 1), ("AB%d.1" % k, 0, NB, 1)], 64, True, None)

    def to_list(ps, wt, row, dense=False):
        for q in range(0, 16, 1 + dense):
            mm(ps, slid(wt, q), v(row, 32 * q, 32 * q + 64) if dense else v(row, q, 512, 16), q == 0, q == 15 - dense, q % PART > 0)

    P8 = slice(0, 8)
    LO, HI, C256, CN256, LAID, ZSC, ZBI, CU, CV, TH = 0, 1, 2, 3, 4, 5, 6, 7, 8, 9
    THR, TMP, LSC, LBI, FSC, FBI, JBI, FILL, EA, EG, EB, WC, B0C, CK = 10, 12, 13, 14, 15, 16, 17, 18, 19, 20, 21, 22, 23, 24

    dma("Y", "d0", T.C8[0:8, :], T.c0[:, :], [], [v("C8")], 2.0, True)
    dma("S", "d1", T.hwi[:, :], T.hw[:, :], [], [v("hwi")], 2.2, True)
    dma("Y", "d1", T.kmi[:, :], T.km[:, :], [], [v("kmi")], 2.2, True)
    for k in range(16):
        lo = 8 * k
        dma("S" if k % 2 else "Y", "d2", T.Tw[lo:lo + 8, E:E + S], T.tp[(lo ^ 8):(lo ^ 8) + 8, :], [], [v("Tw", E, E + S)] if k == 15 else [], 7.0, True)
    for k, (a, b) in enumerate(zip(UL, UL[1:])):
        x = v("UO", E + a, E + b)
        dma("Y", "du%d" % k, x[0], T.us[:, a:b], [], [x], 7.2 + 5.6 * b / S, True)

    iota(v("pi"), [[0, 2]], 0, 1, False)
    iota(v("io144"), [[1, 144]], -16, 0)
    iota(v("io16"), [[1, 16]], 0, 0)
    iota(v("io8"), [[1, 8], [0, 16]], 0, 0)
    iota(v("tc"), [[16, 32]], 0, 0)
    iota(v("ior"), [[1, 512]], -256, 0)
    io128 = v("io144", 16, 144)
    behind.extend([v("ior"), v("tc")])
    add("G", lambda: g.dma_start(T.thi[0:8, :], T.th[:, :]), [], [v("thi")], 3.0, "D", "dt", 2.0)
    cp(v("pf"), v("pi", 0, 1))
    ts(v("pq", 0, 1), v("pi", 0, 1), 4, A.arith_shift_right)
    ts(v("pq", 1, 2), v("pi", 0, 1), 15, A.bitwise_and)
    cp(v("gf"), v("pq", 0, 1))
    cp(v("qf"), v("pq", 1, 2))
    ts(v("qm"), v("io16"), v("qf"), A.is_equal)

    def qm(q):
        return v("qm", q, q + 1)
    ts(v("BD"), v("io8"), v("gf"), A.is_equal)
    ts(v("BF"), v("io8"), v("gf"), A.is_equal)
    ts(v("ID"), io128, v("pf"), A.is_equal)
    ts(v("NI"), io128, v("pf"), A.is_equal, -1.0, A.mult)
    ts(col(LO), v("qf"), 7.5, A.is_lt)
    ts(col(HI), v("qf"), 7.5, A.is_gt)
    ts(col(C256), col(LO), 256.0, A.mult)
    ts(col(CN256), col(LO), -256.0, A.mult)
    ts(col(LAID), col(LO), -256.0, A.mult, 255.0, A.add)
    ts(col(ZSC), col(LO), -255.0, A.mult, 256.0, A.add)
    ts(col(ZBI), col(LO), -512.0, A.mult, 256.0, A.add)
    ts(v("e2"), v("pf"), -8.0, A.add)
    ts(v("IL"), v("io144"), v("e2"), A.is_equal, col(LO), A.mult)
    ts(v("IH"), v("io144"), v("e2"), A.is_equal, col(HI), A.mult)
    ts(col(B0C), v("gf"), 16.0, A.mult)
    ts(v("B0"), v("io144"), col(B0C), A.is_equal)
    ts(v("e1", p=P8), v("pf", p=P8), 16.0, A.mult)
    ts(v("B8", p=P8), v("io144", p=P8), v("e1", p=P8), A.is_equal)
    ts(v("c16", p=P8), v("C8", p=P8), -2048.0, A.add)
    for q in range(16):
        mm(v("p7", 0, 32), slid("B8", q, P8), v("c16", q, 512, 16, P8), q == 0, q == 15, q > 0)
    ms(v("idx1", 32, 33), 0.0)
    idx = v("idx1", 0, 32)
    ts(idx, v("p7", 0, 32), 2048.0, A.add)
    ts(v("e2"), v("pf"), -1.0, A.add)
    ts(v("e3"), v("qf"), 0.5, A.is_gt)
    ts(v("SH1"), io128, v("e2"), A.is_equal, v("e3"), A.mult)
    ts(v("e4"), v("pf"), 15.0, A.add)
    ts(v("SH2"), io128, v("e4"), A.is_equal, qm(0), A.mult)
    cp(v("hwf"), v("hwi"))
    ts(v("hwg"), v("hwf"), 2048.0, A.is_ge, -4096.0, A.mult)
    tt(v("hws"), v("hwg"), v("hwf"), A.add)
    ts(v("hwm"), v("hws"), col(C256), A.mult)
    cp(v("kmf"), v("kmi"))
    ts(v("kq"), v("qm"), v("kmf"), A.mult)
    mm(v("p5", 0, 2), v("BF"), v("hwm"))
    mm(v("p5", 2, 18), v("BF"), v("kq"))
    cp(v("col", CU, CV + 1), v("p5", 0, 2))
    cp(v("KM"), v("p5", 2, 18))
    for j, (a, b) in enumerate((("WA", "RU"), ("WB", "RV"))):
        ts(v("WU", 8, 144), v("B0", 8, 144), v("hws", 0, 1), A.mult, col(LO + j), A.mult)
        ts(v("WV", 8, 144), v("B0", 0, 136), v("hws", 1, 2), A.mult, col(LO + j), A.mult)
        tt(v(a, 8, 144), v("WU", 8, 144), v("WV", 8, 144), A.add)
        ts(v(b), v("BD"), v("hws", j, j + 1), A.mult)
    ts(v("KS0"), v("KM"), 2048.0, A.is_ge, -4096.0, A.mult)
    tt(v("KS"), v("KS0"), v("KM"), A.add)
    for m in range(16):
        ts(mat("KD", m), v("ID"), v("KS", m, m + 1), A.mult)
    setup.append(1)
    ts(v("FD"), v("B0"), 4096.0, A.mult)
    tt(col(FILL), qm(2), qm(4), A.add)
    tt(col(TMP), qm(5), qm(7), A.add)
    tt(col(WC), col(TMP), col(FILL), A.add)
    ts(col(TMP + 20), qm(1), 1.0 / 1024.0, A.mult)
    for name, wt in (("FC", col(WC)), ("FO", col(FILL)), ("FJ", col(TMP + 20)), ("F0", qm(0)), ("F15", qm(15))):
        act(v(name), v("B0"), scale=wt)
    ts(v("ki"), v("KM"), -1.0, A.mult, v("KM", 15, 16), A.add)
    ts(v("kj"), v("ki"), 4095, A.bitwise_and)
    ts(v("ka"), v("kj"), 6, A.arith_shift_right)
    ts(v("kb"), v("kj"), 63, A.bitwise_and)
    ts(v("dC"), v("io16"), 256.0, A.mult, -3840.0, A.add)
    for d, D, k in (("dA", "DA", "ka"), ("dB", "DB", "kb")):
        tt(v(d), v("dC"), v(k), A.subtract)
        tt(v(D, 1, 16), v(d, 0, 15), v(d, 1, 16), A.subtract)
        ms(v(D, 0, 1), 33554432.0)
        w = 16
        while w < 512:
            act(v(D, w, 2 * w), v(D, 0, w))
            w *= 2
    ms(v("on"), 1.0)
    for a, b, n in (("H0", "H1", NB), ("G0", "G1", NA)):
        act(v(a, 0, HS * n), v("ior", 0, HS * n), AF.Identity, scale=0.0, bias=v("on", 0, 1))
        for name, step, c in ((a, 0, 0.0), (a, 3, 64.0), (b, 1, M1), (b, 2, -M1), (b, 4, M1), (b, 5, -M1), (b, 7, M4096), (b, 8, -M4096)):
            ms(v(name, step, HS * n, HS), c)
    ts(v("rep", p=P8), v("io8", p=P8), v("pf", p=P8), A.is_equal)
    cp(v("thf", p=P8), v("thi", p=P8))
    mm(v("p5", 0, 1), v("rep", p=P8), v("thf", p=P8))
    cp(col(TH), v("p5", 0, 1))
    ts(col(THR), col(TH), 4096.0, A.mult, -3968.0, A.add)
    ts(v("x1"), io128, v("pf"), A.is_le)
    tt(v("GE"), v("x1"), v("BD"), A.mult)
    tt(v("LT"), v("BD"), v("GE"), A.subtract)
    ms(v("ON"), 1.0)
    ts(v("tcq"), v("tc"), v("qf"), A.add)
    ts(v("tc512"), v("tcq"), 512.0, A.add)
    ts(v("nt1024"), v("tcq"), -1.0, A.mult, -1024.0, A.add)
    for k in range(NB // BC):
        cp(v("tcd", BC * k, BC * k + BC), v("tcq", 0, BC))
    ts(v("W40"), v("tcq"), 510.0, A.is_equal, 5112.0, A.mult)
    ts(v("W4"), v("W40"), 4.0, A.add)
    ms(v("Y", 0, 16), 0.0)
    iota(v("E1"), [[0, 2048]], 1, 0)
    pick(v("E1"), v("E1"), [[-1, 16], [-16, 8], [0, 16]], A.is_equal, 0, 1)
    pick(v("Y", 16, 2064), v("E1"), [[0, 128], [-1, 16]], A.is_ge, 1, 0)
    ts(col(LSC), qm(0), 2.0 ** -24, A.mult)
    ts(col(LBI), qm(0), 2.0 ** -16, A.mult, col(LAID), A.add)
    act(v("LV"), v("ior"), AF.Identity, scale=col(LSC), bias=col(LBI))
    ts(col(FSC), qm(0), 2.0 ** 24, A.mult)
    ts(col(FBI), qm(0), 2.0 ** 24 - 256.0, A.mult)
    ts(col(JBI), qm(0), 256.0, A.mult, 1024.0, A.add)
    act(v("JV"), v("ior"), AF.Identity, scale=qm(0), bias=col(JBI))
    act(v("DM"), v("ior"), AF.Identity, scale=0.0, bias=qm(0))
    ms(v("ZM"), 0.0)
    act(v("L255"), v("ior", 0, 96), AF.Identity, scale=0.0, bias=col(LAID))
    ts(v("ga"), v("io16"), v("qf"), A.add)
    ts(v("mq"), v("ga"), 15.5, A.is_lt, 16384.0, A.mult)
    ts(v("qr"), v("ga"), 15.0, A.is_equal)
    for b in range(NA):
        act(v("QR", 16 * b, 16 * b + 16), v("qr"))
    ts(v("RL", 0, NA), v("io16", 0, NA), -1.0, A.mult, NA - 1.0, A.add)
    for i in range(max(BC, NA)):
        o = 8 * i * (i + 1)
        act(v("MA", o, o + 16), v("mq"), AF.Identity, bias=v("tcq", i, i + 1))
        if i:
            act(v("MA", o + 16, o + 16 * i + 16), v("ior", 0, 16 * i), AF.Identity, scale=0.0, bias=v("tcq", i, i + 1))
    for k in range(16 // BC):
        act(v("MK", RUN * k, RUN * k + RUN), v("MA", 0, RUN))
    act(v("SC", RUN * NB // BC, RUN * (NB + 16) // BC), v("MK"))
    ts(v("ei"), v("pq", 1, 2), BC - 1, A.bitwise_and)
    tt(v("e4"), v("qf"), v("ei"), A.subtract)
    ts(v("e4"), v("e4"), float(RUN) / BC, A.mult, -1.0, A.add)
    ts(v("e1"), v("qf"), NA - 1.0, A.min)
    for k, (x, o) in enumerate((("ei", v("e4")), ("e1", -1.0))):
        ts(v("e2"), v(x), 8.0, A.mult, 8.0, A.add)
        ts(v("e3"), v(x), 2.0, A.add, v("e2"), A.mult)
        ts(v("EN", 2 * k, 2 * k + 1), v("e3"), o, A.add)
    ms(v("nlo", 32, 48), 0.0)
    ts(v("pd", 0, NA), v("tcq", 0, NA), 1.0 / 6.0, A.mult, -5.0 / 12.0, A.add)
    ts(v("pp", 0, NA), v("pd", 0, NA), -95.0, A.mult)
    ts(v("s2", 0, NA), v("tcq", 0, NA), 16.0, A.mult)
    tt(v("s3", 0, NA), v("s2", 0, NA), v("pp", 0, NA), A.add)
    cp(v("PL", 0, NA), v("s3", 0, NA))
    ms(v("U", E + S, E + W), 0.0)
    del setup[:]
    for k in range(16):
        x, y = v("U", E + 256 * k, E + 256 * k + 256), v("UO", E + 256 * k, E + 256 * k + 256)
        if k in UV:
            ts(x, y, col(CN256), A.add)
        else:
            act(x, y, AF.Identity, bias=col(CN256))

    def best(n, keys, d0, d1, hr, rr, outs):
        ts(v(rr, 0, 2 * n), v(keys, 15, 32 * n, 16), M256, A.add, M256, A.subtract)
        for j in (0, 1):
            tt(v(d1, 3 * j, HS * n, HS), v(keys, 16 * n * j + 15, 16 * n * (j + 1), 16), v(rr, n * j, n * j + n), A.subtract)
        scan(v(hr, 0, HS * n), v(d0, 0, HS * n), v(d1, 0, HS * n), 0.0, A.mult, A.add)
        for o in outs:
            tt(v(o, 0, n), v(hr, 6, HS * n, HS), v(hr, 9, HS * n, HS), A.subtract)

    def split(hi, lo, x):
        ts(v(hi), v(x), M128, A.add, M128, A.subtract)
        tt(v(lo), v(x), v(hi), A.subtract)

    def rows(hi, lo, sh, sl):
        for name, shift in ((hi, sh), (lo, sl)):
            for q in range(16):
                mm(v("p6", q, 512, 16), mat("Y", q, shift - 16), v(name), False, name == "Dl" and q == 15, q % 8 > 0)

    def flags(t, dense):
        up = v("UP", 96 * t, 96 * t + 96)
        if dense:
            ts(v("NG", 0, 256), ind(up, v("ngu", 0, 16)), -2048.0, A.is_lt)
            act(v("NG", 256, 512), ind(up, v("ngu", 16, 32)), AF.Relu, scale=-1.0 / 2048.0, bias=col(TMP + 21))
        else:
            act(v("NG"), ind(up, v("ngu")), AF.Relu, scale=-1.0 / 2048.0, bias=col(TMP + 21))
        n = 64 if dense else NB
        to_list(v("p7", 0, n), "F0", "NG", dense)
        if not dense:
            behind.append(v("vf"))
        tt(v("w4", 0, n), v("p7", 0, n), v("n4", 0, n), A.mult)
    setup.append(1)
    ms(col(TMP + 21), -1.0)
    ms(col(TMP + 22), -4096.0)
    ms(v("gm"), 0.0)
    ms(col(TMP + 24), 2304.0)
    ms(col(TMP + 25), 1280.0)
    ms(col(TMP + 27), 0.5)
    ts(v("kw"), v("KM"), v("hwf", 0, 1), A.mult)
    ts(v("kw"), v("kw"), 4095, A.bitwise_and)
    ts(v("kx"), v("kw"), 2048.0, A.is_ge, -4096.0, A.mult)
    tt(v("kx"), v("kx"), v("kw"), A.add)
    for k in range(8):
        ts(v("RK", 16 * k, 16 * k + 16), v("kx"), v("BF", 16 * k, 16 * k + 1), A.mult)
    cp(v("ci"), col(CU))
    ts(v("ci"), v("ci"), 4095, A.bitwise_and)
    ts(v("ci"), v("ci"), v("kmf"), A.mult)
    ts(v("ci"), v("ci"), 4095, A.bitwise_and)
    cp(col(CK), v("ci"))
    ts(col(EA), col(LO), 255.0 / 256.0, A.mult, 1.0 / 256.0, A.add)
    ts(col(EG), col(LO), 257.0, A.mult, 1023.0, A.add)
    ts(col(TMP + 26), col(CU), col(LO), A.mult)
    ts(col(EB), col(CV), col(HI), A.mult, col(TMP + 26), A.add)
    ts(col(TMP + 23), v("qf"), 1008.0, A.add)
    ms(v("c16f"), 16.0)
    ms(v("pw", 0, 1), 0.0)
    ts(v("pn", 0, 1), v("qf"), 0.0, A.mult)
    ms(v("TS", 0, 96), 1024.0)
    for a in (96, 224):
        ms(v("Tw", a, a + 32), 0.0)
    ms(v("U", 0, E), 0.0)
    del setup[:]

    for t in range(R):
        last = t == R - 1
        lender, asker = T.cores[(rank + 1 + t) % 8], T.cores[(rank - 1 - t) % 8]
        base, thr = float(S + 96 * t), col(THR + t % 2)
        stones, e0 = v("U", E, E + S), 0 if t == 1 else 128
        cp(v("CL", 0, 32), idx)
        mm(v("p7", 32, 64), v("SH1"), idx, True, False)
        mm(v("p7", 32, 64), v("SH2"), v("idx1", 1, 33), False, True, True)
        cp(v("CL", 32, 64), v("p7", 32, 64))
        tops = v("Tw", E, E + S + 96 * t)
        act(v("GA"), ind(tops, v("CL", 0, 32)), AF.Identity, scale=col(ZSC), bias=col(ZBI))
        cp(v("GB"), ind(tops, v("CL", 32, 64)))
        tt(v("Z"), v("GA"), v("GB"), A.min)
        act(v("Zf"), v("Z"), AF.Identity, bias=col(TMP + 25))
        act(v("NZ"), v("Z"), scale=-1.0)
        for k, (wt, z) in enumerate((("WA", "GA"), ("WB", "GB"))):
            for r in range(8):
                mm(v("p0", 0, 64), slid(wt, r), v(z, r, 512, 8), k + r == 0, k + r == 8, r > 0)
        for j in (0, 1):
            ts(v("uva", 64 * j, 64 * j + 64), v("p0", 0, 64), col(EB), A.add, 2048.0 * j, A.add)
        ts(v("uv"), v("uva"), 4095, A.bitwise_and)
        ts(v("u16"), v("uv"), -2048.0, A.add)
        mm(v("p1", 0, 64), v("IL", 8, 136), v("u16", 0, 128, 2), True, False)
        mm(v("p1", 0, 64), v("IL", 0, 128), v("u16", 1, 128, 2), False, True, True)
        mm(v("p1", 64, 96), v("IH", 16, 144), v("u16", 0, 64, 2), True, False, True)
        mm(v("p1", 64, 96), v("IH", 8, 136), v("u16", 1, 64, 2), False, True, True)
        uh = v("uh")
        cp(uh, v("p1", 32, 64))
        ts(v("uf"), v("p1", 0, 32), 2048.0, A.add)
        ts(v("vf"), v("p1", 64, 96), 2048.0, A.add)
        act(v("H0", 6, HS * NB, HS), v("p1", 32, 64))
        tt(v("PR"), v("uf"), v("vf"), A.mult)
        ts(v("qi"), v("PR"), 5, A.arith_shift_right, 4095, A.bitwise_and)
        ts(v("qh"), v("qi"), -2048.0, A.add)
        for lo, hi, bank in ((0, N1, "p2"), (N1, 16, "p3")):
            if lo:
                mm(v(bank, 32 * lo, 32 * hi), v("ZM"), v("DM", 32 * lo, 32 * hi), True, False)
            for i in range(lo, hi):
                mm(v(bank, 32 * i, 32 * i + 32), mat("KD", LISTS[i]), uh, lo == 0, lo == 0, i % 4 > 0)
            for i in range(lo, hi if lo else 0):
                mm(v(bank, 32 * i, 32 * i + 32), v("ID"), v("qh"), False, i == hi - 1, i % 4 > 0)
            if lo == 0:
                for i in range(lo, hi):
                    tt(v("X", 32 * i, 32 * i + 32), v(bank, 32 * i, 32 * i + 32), v("qi"), A.add)
            else:
                ts(v("X", 32 * lo, 32 * hi), v(bank, 32 * lo, 32 * hi), 2048.0, A.add)
            for a, b in ((lo, hi),) if lo else ((0, N0), (N0, hi)):
                ts(v("X2", 32 * a, 32 * b), v("X", 32 * a, 32 * b), 4095, A.bitwise_and)
                urge.append(0.0 if a else U4)
                cp(v("HL", 32 * a, 32 * b), v("X2", 32 * a, 32 * b))
        ts(v("H1", 6, HS * NB, HS), v("X2", 32 * LISTS.index(15), 32 * LISTS.index(15) + 32), -2047.5, A.add)
        if t:
            flags(t - 1, False)
            tt(v("Cf"), idx, v("w4", 0, NB), A.subtract)
            tt(v("Ci"), idx, v("w4", 0, NB), A.subtract)
        else:
            cp(v("Cf"), idx)
            cp(v("Ci"), idx)
        ts(v("f3"), v("Ci"), 3, A.bitwise_and)
        tt(v("wv"), v("f3"), v("W4"), A.add)
        mm(v("p7", 64, 96), v("BD"), v("wv"))
        mm(v("p7", 96, 128), v("GE"), v("wv"))
        scan(v("cw"), v("on"), v("p7", 64, 96), 0.0, A.mult, A.add)
        tt(v("ee"), v("cw"), v("p7", 96, 128), A.subtract)
        tt(v("ec"), v("ee"), v("wv"), A.add)
        ts(v("fi"), v("ee"), 0.2, A.mult, 512.0, A.min)
        ts(v("nx"), v("ec"), 0.2, A.mult, 512.0, A.min)
        tt(v("mu"), v("nx"), v("fi"), A.subtract)
        ts(v("rc"), v("mu"), 0.5, A.is_ge)
        ts(v("pj"), v("mu"), 0.5, A.is_lt)
        tt(v("pj2"), v("pj"), v("tc512"), A.mult)
        tt(v("fo"), v("fi"), v("pj2"), A.max)
        urge.append(U1)
        cp(v("fou"), v("fo"))
        if t:
            behind.append(v("SU"))
        act(v("JW", 0, 512), v("ior"), scale=0.0)
        act(ind(v("JW"), v("fou")), v("JV"), AF.Silu)
        urge.append(U2)
        scan(v("JS"), v("DM"), v("JW", 0, 512), 0.0, A.mult, A.max)
        n2 = 64 if last else NB
        to_list(v("p7", 160, 192), "F0", "JS")
        ts(v("JJ"), v("p7", 160, 192), -1024.0, A.add)
        if last:
            to_list(v("p7", 160, 224), "F0", "JS", True)
        ts(v("Js", 0, n2), v("p7", 160, 160 + n2), -1280.0, A.add)
        fs = v("p7", 224, 224 + n2)
        to_list(fs, "FJ", "JS", last)
        ts(v("Cb"), v("Cf"), -base, A.add)
        split("Ch", "Cl", "Cf")
        tt(v("nrt"), v("rc"), v("nt1024"), A.mult)
        n = 0
        for k in range(8):
            for j in (1, 0):
                o, cut = 32 * LISTS.index(k + 8 * j), SG.get(k, 0) if j else 0
                if cut:
                    w = 16 * cut
                    i = sorted(SG).index(k)
                    gs = v("GS%d" % i, 0, w)
                    if i:
                        behind.append(half(AFTER[i - 1] // 2, 1 - AFTER[i - 1] % 2))
                    act(gs, ind(stones, v("HL", o, o + cut)))
                    if k in SP:
                        mm(v("p5", 0, w), v("ID"), gs, True, False)
                        mm(v("p5", 0, w), v("NI"), v("Z", 0, w), False, True)
                        act(half(k % NAB, j, 0, cut), v("p5", 0, w), AF.Abs)
                    else:
                        nz = v("NZ", 0, w)
                        add("G", lambda gs=gs, nz=nz: g.dma_start(gs[0], nz[0], accum_op=A.add), [gs, nz], [gs], 1.0, "D", "da%d" % i, 3.5)
                        act(half(k % NAB, j, 0, cut), gs, AF.Abs)
                cuts = (cut, LAST, NB) if k == 7 and not j else (cut, NB) if cut < NB else ()
                for a, b in zip(cuts, cuts[1:]):
                    df = v("DF%d" % (n % 5), 16 * a, 16 * b)
                    if a == LAST:
                        behind.append(v("DF%d" % ((n - 1) % 5)))
                    n += 1
                    tt(df, ind(stones, v("HL", o + a, o + b)), v("Z", 16 * a, 16 * b), A.subtract)
                    act(half(k % NAB, j, a, b), df, AF.Abs)
        for k in SUMS:
            for q in range(16):
                mm(v("p4", k, 512, 8), slid("FD", q), both(k % NAB, q), q == 0, q == 15, q > 0)
        scan(v("KAB", 0, 512), v("DA"), v("p4"), 0.0, A.add, A.min)
        scan(v("KAB", 512, 1024), v("DB"), v("p4"), 0.0, A.add, A.min)
        behind.append(half(7 % NAB, 0))
        mm(v("p6"), v("ZM"), v("Z"), True, False)
        rows("Ch", "Cl", 2, 3)
        ts(v("nf"), v("KAB", 15, 512, 16), thr, A.is_ge)
        tt(v("pw", 1, 33), v("nf"), v("mu"), A.mult)
        tt(v("pn", 1, 33), v("nf"), v("nrt"), A.mult)
        for k, (a, b, o) in enumerate((("GE", "pw", 0), ("LT", "pw", 1), ("NI", "pn", 0), ("ID", "pn", 1))):
            mm(v("p1", 0, 32), v(a), v(b, o, o + 32), k == 0, k == 3, k > 0)
        scan(v("OF"), v("c16f"), v("p1", 0, 32), col(TMP + 23), A.add, A.add)
        cp(v("OFu"), v("OF"))
        act(v("ZS", 0, 96), v("ior", 0, 96), AF.Identity, scale=0.0, bias=col(TMP + 24))
        act(ind(v("ZS"), v("OFu")), v("Zf"), AF.Silu)
        zr = v("ZR%d" % t)
        ts(v("ZB"), ind(v("ZS", 0, 96), v("PL", 0, NA)), M1, A.add, M1 + 1280.0, A.subtract)
        send("az%d" % t, "lz", lender, zr, v("ZB"), FIRST if t == 0 else 0.0)
        tt(v("lf"), v("rc"), v("nf"), A.is_gt)
        ts(v("H1", 9, HS * NB, HS), v("lf"), -8192.0, A.mult, 8191.5, A.add)
        best(NB, "KAB", "H0", "H1", "hr", "rr", ("hh", "hx"))
        for q in range(16):
            mm(v("p2", 15 - q, 512 - q, -16), mat("E1", q), v("hh"), True, True, q > 0)
        ts(v("nh"), v("hx"), -8192.0, A.mult)
        ts(v("n0"), v("hx"), 2047.0 + E - e0, A.add)
        tt(v("nlo", 0, 32), v("n0"), v("tcd"), A.max)
        for hi, lo in zip(BATCH, BATCH[1:]):
            for k in range(hi - 1, lo - 1, -1):
                for i in range(BC):
                    b, o = BC * k + i, RUN * k + 8 * i * (i + 1)
                    a0, a1 = 496 - 16 * b, 512 - 16 * BC * k
                    act(v("NE", o, o + a1 - a0), v("p2", a0, a1), AF.Abs, scale=8192.0, bias=v("nh", b, b + 1))
            o, w, c0, c1 = RUN * lo, RUN * (hi - lo), BC * lo, BC * hi
            scan(v("SC", o, o + w), v("NE", o, o + w), v("MK", 0, w), 0.0, A.min, A.max)
            tt(v("la", 16 * lo, 16 * lo + 16), ind(v("SC", o, o + RUN * 16 // BC), v("EN", 0, 1)), v("nlo", c0, c0 + 16), A.min)
            cp(v("lou", c0, c1), v("la", 16 * lo, 16 * lo + c1 - c0))
            for k in range(hi - 1, lo - 1, -1):
                cp(ind(v("U", e0, E + S), v("lou", BC * k, BC * k + BC)), v("LV", 16 * BC * k, 16 * BC * k + 16 * BC))
        if not last:
            act(v("Tf"), v("GA"), AF.Identity, scale=col(EA), bias=col(EG))
            behind.append(v("NE"))
            act(ind(v("TS"), v("OFu")), v("Tf"), AF.Silu)
            ts(v("TB"), v("TS", 0, 96), M1, A.add, M1 + 1024.0, A.subtract)
            send("ae%d" % t, "lw", lender, v("Tw", e0, e0 + 96), v("TB"))
        ts(v("Ca"), v("Cf"), -2047.0, A.add)
        tt(v("a1"), v("hx"), v("Ca"), A.subtract)
        tt(v("a2"), v("a1"), v("lf"), A.mult)
        tt(v("a3"), v("OF"), v("Cb"), A.subtract)
        ts(v("a4"), v("OF"), 95.5, A.is_lt)
        tt(v("a5"), v("a3"), v("a4"), A.mult)
        tt(v("dd"), v("a2"), v("a5"), A.add)
        split("Dh", "Dl", "dd")
        rows("Dh", "Dl", 5, 7)
        if not last:
            behind.append(v("TS"))
        act(v("NW"), v("p6"))
        if t:
            dma("Y", "d3", T.yc[:, 512 * t - 512:512 * t], T.NW[3:128:16, :], [v("NW")], [])
        act(v("NR"), ind(v("NW"), v("JJ")))
        to_list(v("p7", 0, 32), "FC", "NR")
        cp(v("Hs"), v("p7", 0, 32))
        ts(v("ngu"), v("p7", 0, 32), -base, A.add)
        pc = v("p7", 0, 32)
        if last:
            pc = v("p6", 64, 128)
            to_list(pc, "FC", "NR", True)
        to_list(v("p6", 0, n2), "FO", "NR", last)
        Os, Js, d0, df, pl, n4, w1, w2, w3, a6 = (v(x, 0, n2) for x in "Os Js d0 df pl n4 w1 w2 w3 a6".split())
        cp(Os, v("p6", 0, n2))
        tt(d0, pc, Os, A.subtract)
        ts(pl, pc, base, A.is_ge)
        tt(df, d0, fs, A.mult)
        tt(n4, pl, df, A.mult)
        act(v("FG"), ind(v("U", E, E + W), v("Hs")), AF.Identity, scale=col(FSC), bias=col(FBI))
        to_list(v("p2", 0, n2), "F0", "FG", last)
        tt(w1, v("p2", 0, n2), Js, A.is_equal)
        tt(w2, df, n4, A.subtract)
        tt(a6, Os, n4, A.add)
        tt(w3, w1, w2, A.mult)
        tt(v("yi") if last else idx, w3, a6, A.add)
        mm(v("p3", 0, 96), v("RU"), zr)
        mm(v("p3", 96, 192), v("RV"), zr, True, True, True)
        mm(v("p3", 192, 288), v("RK"), zr, True, True, True)
        for j, c in enumerate((CU, CV, CK)):
            ts(v("ua", 96 * j, 96 * j + 96), v("p3", 96 * j, 96 * j + 96), col(c), A.add)
        ts(v("ub", 0, 192), v("ua", 0, 192), 4095, A.bitwise_and)
        ts(v("ub", 192, 288), v("ua", 192, 288), 4095, A.bitwise_and)
        tt(v("PRa"), v("ub", 0, 96), v("ub", 96, 192), A.mult)
        ts(v("kua"), v("ub", 192, 288), 32.0, A.mult, -131072.0, A.add)
        tt(v("Xa"), v("kua"), v("PRa"), A.add)
        ts(v("Xb"), v("Xa"), 5, A.arith_shift_right, 4095, A.bitwise_and)
        cp(v("HA"), v("Xb"))
        urge.append(U3)
        ts(v("R2", 0, 192, 2), v("ub", 0, 96), -2048.0, A.add)
        urge.append(U3)
        ts(v("R2", 1, 192, 2), v("Xb"), -2048.0, A.add)
        for q in range(16):
            mm(v("p0", 0, 12), slid("F15", q), v("R2", 12 * q, 12 * q + 12), q == 0, q == 15, q % 4 > 0)
        ts(v("gb", 0, NA), v("p0", 0, 12, 2), 0.0, A.is_lt, 4096.0, A.mult)
        ts(v("k7", 0, NA), v("p0", 0, 12, 2), -2048.0, A.add)
        tt(v("G0", 6, HS * NA, HS), v("gb", 0, NA), v("k7", 0, NA), A.add)
        act(v("G1", 6, HS * NA, HS), v("p0", 1, 12, 2), AF.Identity, bias=col(TMP + 27))
        for m in range(16):
            if not last:
                behind.append(v("TS"))
            act(v("z16", m, 1536, 16), zr)
        for k, (a, b) in enumerate(zip(QA, QA[1:])):
            w = 96 * (b - a)
            z = v("z16", 96 * a, 96 * b)
            df, ab = v("DF%d" % k, 0, w), v("AA", 96 * a, 96 * b)
            if k in SA:
                act(v("GS", 0, w), ind(stones, v("HA", 6 * a, 6 * b)))
                mm(v("p4", 0, w), v("NI"), z, True, False)
                mm(v("p4", 0, w), v("ID"), v("GS", 0, w), False, True)
                act(ab, v("p4", 0, w), AF.Abs)
            else:
                tt(df, ind(stones, v("HA", 6 * a, 6 * b)), z, A.subtract)
                act(ab, df, AF.Abs)
            for q in range(a, b):
                mm(v("p5", 0, 96), slid("FD", q), v("AA", 96 * q, 96 * q + 96), q == 0, q == 15, q > a)
        behind.append(v("AA"))
        act(v("U", e0, e0 + 96), v("ior", 0, 96), AF.Identity, scale=0.0, bias=col(TMP + 22))
        scan(v("KE", 0, 96), v("DA", 0, 96), v("p5", 0, 96), 0.0, A.add, A.min)
        scan(v("KE", 96, 192), v("DB", 0, 96), v("p5", 0, 96), 0.0, A.add, A.min)
        ts(v("k6", 0, NA), v("KE", 15, 96, 16), thr, A.is_ge, 8192.0, A.mult)
        ts(v("G1", 9, HS * NA, HS), v("k6", 0, NA), -0.5, A.add)
        best(NA, "KE", "G0", "G1", "gr", "ra", ("ga1",))
        tt(v("RX"), ind(v("ga1", 0, NA), v("RL", 0, NA)), v("QR"), A.mult)
        mm(v("p1", 0, 96), v("BD"), v("RX"))
        mm(v("p3", 0, 96), v("BD"), v("RX"))
        ts(v("ga3", 0, NA), v("ga1", 0, NA), -8192.0, A.mult)
        ts(v("ga2", 0, NA), v("ga1", 0, NA), 2047.0 + E - e0, A.add)
        tt(v("gm", 0, NA), v("ga2", 0, NA), v("tcq", 0, NA), A.max)
        for b in range(NA):
            o = 8 * b * (b + 1)
            if b in (0, 1, 5):
                ts(v("NE", o, o + 16 * b + 16), v("p1", 80 - 16 * b, 96), v("ga1", b, b + 1), A.not_equal, 8192.0, A.mult)
            else:
                act(v("NE", o, o + 16 * b + 16), v("p3", 80 - 16 * b, 96), AF.Abs, scale=8192.0, bias=v("ga3", b, b + 1))
        scan(v("SC", 0, 336), v("NE", 0, 336), v("MA", 0, 336), 0.0, A.min, A.max)
        tt(v("ga"), ind(v("SC", 0, 336), v("EN", 2, 3)), v("gm"), A.min)
        glu = v("glu", 0, NA)
        cp(glu, v("ga", 0, NA))
        if not last:
            cp(v("SB"), ind(v("Tw", e0, E + S), glu))
            send("at%d" % t, "ly", asker, v("Tw", E + S + 96 * t, E + S + 96 * t + 96), v("SB"))
        act(v("SU"), ind(v("U", e0, E + S), glu))
        send("au%d" % t, "lx", asker, v("UP", 96 * t, 96 * t + 96), v("SU"))
        if not last:
            cp(ind(v("U", e0, E + S), glu), v("L255"))
            behind.append(v("SB"))
            mm(v("p3", 0, 32), v("ON"), v("pw", 1, 33))
            op("V", lambda: g.vector.tensor_reduce(_(v("Pf")), _(v("p3", 0, 32)), AxisListType.X, A.add), v("Pf"), [v("p3", 0, 32)])
            cp(v("Pi"), v("Pf"))
            ts(v("Pj"), v("Pi"), 63, A.bitwise_and)
            tt(col(TMP), col(TH), v("Pj"), A.add)
            ts(col(THR + (t + 1) % 2), col(TMP), 4096.0, A.mult, -3968.0, A.add)
        else:
            for k in range(16):
                x, y = v("U", E + 256 * k, E + 256 * k + 256), v("UO", E + 256 * k, E + 256 * k + 256)
                if k % 4 == 3:
                    ts(y, x, col(C256), A.add)
                else:
                    act(y, x, AF.Identity, bias=col(C256))
            ms(v("L255"), 255.0)
            cp(ind(v("UO", e0, E + S), glu), v("L255"))
            y = v("UO", E, E + S)
            dma("Y", "d4", T.yu[:, 0:S], y[0], [y], [], 6.0)

    flags(R - 1, True)
    tt(v("yo"), v("yi"), v("w4"), A.subtract)
    dma("Y", "d6", T.yc[:, 512 * R - 512:512 * R], T.yo[0:128:2, :], [v("yo")], [])
    ts(v("UQ"), v("UP"), col(C256), A.add, 0.0, A.max)
    dma("S", "d5", T.yu[:, S:W], T.UQ[:, :], [v("UQ")], [])

    seen = {}
    for n, c in enumerate(calls):
        c["pre"] = {}
        for xs, isw in ((c["rs"], False), (c["ws"], True)):
            for r in xs:
                for (o, k, w) in seen.get(r[0], []):
                    d = calls[k]
                    if hit(r, o) and (w or isw or (is_bank(r[0]) and d["q"] != c["q"])):
                        wait = 0.0 if d["q"] == c["q"] == "P" else d["late"] * (1 if w else 3) + HOP
                        c["pre"][k] = max(c["pre"].get(k, 0.0), wait)
        for xs, isw in ((c["rs"], False), (c["ws"] + (c["far"] or []), True)):
            for r in xs:
                old = seen.setdefault(r[0], [])
                if isw:
                    old[:] = [o for o in old if not (o[0][1] >= r[1] and o[0][2] <= r[2] and r[3] == 1)]
                old.append((r, n, isw))
    for c in calls:
        c["tail"] = c["cost"] + c["late"]
    for n in range(len(calls) - 1, -1, -1):
        for k, wait in calls[n]["pre"].items():
            calls[k]["tail"] = max(calls[k]["tail"], calls[k]["cost"] + calls[k]["urge"] + wait + calls[n]["tail"])
    for c in calls:
        c["post"] = {}
    for n, c in enumerate(calls):
        for k, wait in c["pre"].items():
            calls[k]["post"][n] = wait

    def place(order, side):
        busy, at = {q: [] for q in Q}, {}
        for n in order:
            c = calls[n]
            t0 = max([at[k] + calls[k]["cost"] + wait for k, wait in c[side].items()] + [c["late"] if side == "post" else 0.0])
            t0 += c["urge"] if side == "post" else 0.0
            line = busy[c["q"]]
            i = len(line)
            while i and line[i - 1][1] > t0:
                i -= 1
            while i < len(line) and line[i][0] < t0 + c["cost"] - 1e-9:
                t0 = max(t0, line[i][1])
                i += 1
            line.insert(i, (t0, t0 + c["cost"]))
            at[n] = t0
        return at
    every = range(len(calls))
    key = {n: -calls[n]["tail"] for n in every}
    at = ORDER
    for k in range(0 if ORDER else PASSES + 1):
        at = place(sorted(every, key=lambda n: (calls[n]["kind"] != "F", n if calls[n]["kind"] == "F" else key[n], n)), "pre")
        if k < PASSES:
            back = place(sorted(every, key=lambda n: (-at[n] - calls[n]["cost"], -n)), "post")
            key = {n: -back[n] - calls[n]["cost"] for n in every}
    if not ORDER:
        ORDER.update(improve(calls, at))
    for n in every:
        calls[n]["at"] = ORDER[n]

    count, known, snaps, rec = {}, {q: {} for q in Q}, {}, {}

    def settle(q, reads, writes):
        need = {}
        for xs, isw in ((reads, False), (writes, True)):
            for r in xs:
                for (o, e, n, w) in rec.get(r[0], []):
                    if not hit(r, o) or (e == q and q == "P") or not (w or isw or (is_bank(r[0]) and e != q)):
                        continue
                    need[e] = max(need.get(e, 0), count[e] if e[0] in "DL" else n)
        for e, n in sorted(need.items(), key=lambda kv: -kv[1]):
            if known[q].get(e, 0) < n:
                Q[q].wait_ge(T.sem[SEM.get(e, e[1:])], n)
                known[q][e] = n
                for e2, n2 in snaps.get((e, n), {}).items():
                    known[q][e2] = max(known[q].get(e2, 0), n2)

    def note(e, n, reads, writes, snap):
        snaps[(e, n)] = dict(snap)
        for xs, isw in ((reads, False), (writes, True)):
            for r in xs:
                old = rec.setdefault(r[0], [])
                if isw:
                    old[:] = [o for o in old if not (o[0][1] >= r[1] and o[0][2] <= r[2] and r[3] == 1)]
                old[:] = [o for o in old if not (o[0] == r and o[1] == e and o[3] == isw)]
                old.append((r, e, n, isw))

    for t in range(R):
        asker, lender = T.cores[(rank - 1 - t) % 8], T.cores[(rank + 1 + t) % 8]
        for sem, src, ws in (("az%d" % t, asker, v("ZR%d" % t)), ("at%d" % t, lender, v("Tw", E + S + 96 * t, E + S + 96 * t + 96)), ("au%d" % t, lender, v("UP", 96 * t, 96 * t + 96)),
                             ("ae%d" % t, asker, v("Tw", 128 - 128 * t, 224 - 128 * t))):
            if sem in SEMAPHORES:
                count["A" + sem] = len(topo.engines(src, core)[:8])
                note("A" + sem, count["A" + sem], [], ws[1], {})
    for n in sorted(range(len(calls)), key=lambda n: (calls[n]["at"], n)):
        c = calls[n]
        q = c["q"]
        for f, rs, ws in c["parts"]:
            settle(q, rs, ws)
            if c["kind"] == "R":
                e, step = "L" + c["sem"][0], c["sem"][1]
                f()
            else:
                e, step = (q, 1) if c["kind"] == "C" else ("D" + c["sem"], 16)
                f().then_inc(T.sem[SEM.get(e, e[1:])], step)
            count[e] = count.get(e, 0) + step
            note(e, count[e], rs, ws, known[q])
    for e, n in sorted(count.items()):
        g.wait_ge(T.sem[SEM.get(e, e[1:])], n)
